import numpy as np, ml_dtypes
CORES = [23,119,17,113]
N = 4
BF = ml_dtypes.bfloat16
S, A, L, M, R, D = 512, 8, 16, 4, 32, 16
def steps(nx, sy):
    g = np.arange(8); s = np.zeros(8, np.int64); place = np.zeros((N * L, 8), np.int64); cnt = np.zeros((N * L, 8), np.int64)
    for i in range(N * L):
        place[i] = sy[i // L, :, i % L].astype(np.int64) * S + s
        v = nx[i // L, g, place[i]].astype(np.int64)
        s = v % S; cnt[i] = v // S
    return place, cnt
def counts(rng, uneven=False):
    k = np.argsort(rng.random((N, 8, S, A)), -1)
    w = rng.integers(0, 2, k.shape) * M if uneven else rng.integers(0, M + 1, k.shape)
    return np.ascontiguousarray(np.where(k <= M, k, w).transpose(0, 1, 3, 2))
def perms(rng):
    return np.argsort(rng.random((N, 8, A, S)), -1)
def bounds(rng):
    e = np.zeros((8, N + 1), np.int64)
    e[:, 1:N] = np.arange(1, N) * R + rng.integers(-D, D + 1, (8, N - 1)); e[:, N] = N * R - rng.integers(0, D + 1, 8)
    e[0, N] = N * R - D; e[7, N] = N * R
    return e
def draw(rng, to, ct, e, burst=False):
    n = (e[:, 1:] - e[:, :-1])[:, :, None]
    k = (np.arange(L * M) - M * rng.integers(0, L, (8, N, 1))) % (L * M) if burst else np.argsort(rng.random((8, N, L * M)), -1)
    c = np.sum((k < n).reshape(8, N, L, M), axis=-1)
    g = np.arange(8); s = np.zeros(8, np.int64); sy = np.zeros((N, 8, L), np.int32)
    for i in range(N * L):
        q = i // L; ok = ct[q][g, :, s] == c[:, q, i % L][:, None]
        a = np.argmax(np.where(ok, rng.random((8, A)), -1.0), axis=1)
        sy[q, :, i % L] = a; s = to[q][g, a, s]
    return {"nx": (ct * S + to).reshape(N, 8, A * S).astype(np.int32), "em": rng.integers(0, 64 ** M, (N, 8, A * S)).astype(np.int32), "sy": sy}
def setup_inputs(rng):
    to = np.where(rng.random((N, 8, A, 1)) < 0.125, rng.integers(0, S, (N, 8, A, S)), perms(rng))
    return draw(rng, to, counts(rng), bounds(rng))
def setup_inputs_edge(rng):
    e = bounds(rng); g = np.arange(8)[:, None]; r = np.arange(1, N)[None, :]
    e[:, 1:N] = r * R + D * np.where(g % 2 == 0, 1 - 2 * ((r + g // 2) % 2), 1 - 2 * (g // 2 % 2)); e[:, N] = N * R - D * (np.arange(8) // 4)
    return draw(rng, perms(rng), counts(rng), e)
def setup_inputs_even(rng):
    e = bounds(rng); e[:] = np.arange(N + 1) * R
    return draw(rng, perms(rng), counts(rng), e)
def setup_inputs_merge(rng):
    kind = (np.argsort(rng.random((N, 8, A)), -1) % 4)[:, :, :, None]; h = (N, 8, A, 1); s = np.arange(S)
    one = np.where(rng.random(h) < 0.5, rng.integers(0, 2, h) * (S - 1), rng.integers(0, S, h))
    to = np.where(kind == 0, one, np.where(kind == 1, s, np.where(kind == 2, (s + 1) % S, rng.integers(0, S, (N, 8, A, S)))))
    return draw(rng, to, counts(rng), bounds(rng))
def setup_inputs_spread(rng):
    to = np.minimum(np.floor(S * rng.random((N, 8, A, S)) ** 6), S - 1).astype(np.int64)
    d = draw(rng, to, counts(rng, True), bounds(rng), True)
    h = (N, 8, A * S); d["em"] = (d["em"] >> np.where(rng.random(h) < 0.5, rng.integers(0, 6 * M, h), 0)).astype(np.int32)
    return d
def check_inputs(d):
    bad = []
    for k, top in (("nx", (M + 1) * S), ("em", 64 ** M), ("sy", A)):
        if d[k].min() < 0 or d[k].max() >= top: bad.append("range of " + k)
    if bad: return bad
    place, cnt = steps(d["nx"], d["sy"])
    off = np.add.accumulate(cnt, 0)[L - 1::L] - R * np.arange(1, N + 1)[:, None]
    if (np.abs(off) > D).any(): bad.append("running totals")
    if (off[-1] > 0).any(): bad.append("whole total")
    return bad
def reference(nx, em, sy):
    place, cnt = steps(nx, sy); g = np.broadcast_to(np.arange(8), (N * L, 8)); r = (np.arange(N * L) // L)[:, None]
    e = em[r, g, place].astype(np.int64); beg = np.add.accumulate(cnt, 0) - cnt
    z = np.full((8, N * R), -1, np.int64)
    for m in range(M):
        on = cnt > m
        z[g[on], beg[on] + m] = ((e >> (6 * m)) & 63)[on]
    return {"y": np.ascontiguousarray(z.reshape(8, N, R).transpose(1, 0, 2)).astype(np.float32)}

@@ -1,0 +1,567 @@
+import numpy as np
+from concourse.bass import DstId, RemoteDMATransfer
+from concourse.mybir import dt, AluOpType, AxisListType, ActivationFunctionType
+
+F, H, I, U = "float32", "bfloat16", "int32", "uint16"
+SCRATCH = {
+    "nxi": ("sbuf", [128, 256], I), "emi": ("sbuf", [128, 256], I), "syr": ("sbuf", [1, 128], I),
+    "syb": ("sbuf", [1, 128], H), "one": ("sbuf", [1, 128], H), "syc": ("sbuf", [128, 1], I),
+    "evr": ("sbuf", [1, 128], F), "evh": ("sbuf", [1, 128], H), "evl": ("sbuf", [1, 128], H), "ramp": ("sbuf", [1, 512], H),
+    "pci": ("sbuf", [128, 2], I), "pf": ("sbuf", [128, 1], F), "igf": ("sbuf", [128, 128], F),
+    "rowf": ("sbuf", [128, 128], F), "io4": ("sbuf", [128, 128], F),
+    "ci5": ("sbuf", [128, 5], I), "cf5": ("sbuf", [128, 5], F), "cols": ("sbuf", [128, 12], F),
+    "bo": ("sbuf", [128, 128], H), "tri": ("sbuf", [128, 128], H), "idn": ("sbuf", [128, 128], H),
+    "mask": ("sbuf", [128, 16], F), "pm": ("sbuf", [128, 8], F), "gind": ("sbuf", [128, 8], H), "thr": ("sbuf", [128, 4], F),
+    "ti": ("sbuf", [128, 256], I), "sel": ("sbuf", [128, 256], H), "selo": ("sbuf", [128, 256], H), "tb": ("sbuf", [128, 256], H),
+    "hi": ("sbuf", [128, 256], I), "ci": ("sbuf", [128, 256], I), "za": ("sbuf", [128, 256], H), "emf": ("sbuf", [128, 256], F),
+    "self": ("sbuf", [128, 256], F), "selc": ("sbuf", [128, 256], H), "selfx": ("sbuf", [128, 256], F),
+    "selx": ("sbuf", [128, 256], H), "emx": ("sbuf", [128, 256], F), "zax": ("sbuf", [128, 256], H),
+    "tp": ("sbuf", [128, 256], I), "tpi": ("sbuf", [128, 256], I), "tq": ("sbuf", [128, 288], F), "tab": ("sbuf", [128, 544], F),
+    "d16": ("sbuf", [128, 16], H), "ot": ("sbuf", [128, 32], U), "lt": ("sbuf", [128, 512], U),
+    "w": ("sbuf", [128, 512], H), "w1": ("sbuf", [128, 512], H), "wx": ("sbuf", [128, 512], H),
+    "e": ("sbuf", [128, 512], F), "ex": ("sbuf", [128, 512], F),
+    "cp": ("sbuf", [128, 4096], H), "cpm": ("sbuf", [128, 512], H), "cpx": ("sbuf", [128, 512], H), "cp1": ("sbuf", [128, 512], H),
+    "s1": ("sbuf", [128, 2], U), "zero": ("sbuf", [128, 2], U), "tt": ("sbuf", [128, 1080], U),
+    "eea": ("sbuf", [128, 272], F), "eeb": ("sbuf", [128, 272], F), "pos": ("sbuf", [128, 4], F), "zed": ("sbuf", [8, 1], F),
+    "rc0": ("sbuf", [128, 1], F), "rc1": ("sbuf", [128, 1], F), "rc2": ("sbuf", [128, 1], F),
+    "oca": ("sbuf", [128, 1], F), "ocb": ("sbuf", [128, 1], F), "ysb": ("sbuf", [8, 32], F), "neg": ("sbuf", [8, 32], F),
+    "px": ("psum", [128, 512], F), "pwa": ("psum", [128, 512], F), "pwb": ("psum", [128, 512], F),
+    "pcm": ("psum", [128, 512], F), "pew": ("psum", [128, 512], F), "pb": ("psum", [128, 512], F),
+    "pc": ("psum", [128, 512], F), "py": ("psum", [128, 512], F),
+}
+for _q in range(4):
+    SCRATCH["qi%d" % _q] = ("sbuf", [128, 1], I)
+    SCRATCH["di%d" % _q] = ("sbuf", [128, 4], I)
+    SCRATCH["g4%d" % _q] = ("sbuf", [128, 4], H)
+    SCRATCH["ep%d" % _q] = ("sbuf", [128, 4], F)
+    SCRATCH["oh%d" % _q] = ("sbuf", [128, 128], H)
+SEMAPHORES = ["v", "s", "t", "p", "lnx", "lsy", "lsc", "ltp", "lem", "st", "loc",
+              "as1", "aw1", "acp1", "awx", "aselx", "aemx", "azax", "acpx", "arc0", "arc1", "arc2"]
+OP = AluOpType
+AF = ActivationFunctionType
+FIRST = {2: 1, 3: 0}
+FOURS = (8, 12)
+CODE = 262144.0
+
+
+def rank_program(g, core, T, topo):
+    r = T.rank_of(core)
+    if r is None:
+        return
+    Q = {"v": g.vector, "s": g.scalar, "t": g.tensor, "p": g, "y": g.sync}
+    cnt = {}
+    seen = {}
+    vec, act, mm = g.vector, g.scalar.activation, g.tensor.matmul
+    first = FIRST.get(r, 8)
+
+    def waits(qn, deps):
+        need = {}
+        for d in deps:
+            if d is not None:
+                need[d[0]] = max(need.get(d[0], 0), d[1])
+        for sn in need:
+            if seen.get((qn, sn), 0) < need[sn]:
+                Q[qn].wait_ge(T.sem[sn], need[sn])
+                seen[(qn, sn)] = need[sn]
+
+    def do(qn, deps, fn):
+        waits(qn, deps)
+        fn().then_inc(T.sem[qn], 1)
+        cnt[qn] = cnt.get(qn, 0) + 1
+        return (qn, cnt[qn])
+
+    def ts(deps, *a):
+        return do("v", deps, lambda: vec.tensor_scalar(*a))
+
+    def dma(qn, deps, sn, out, in_):
+        waits(qn, deps)
+        Q[qn].dma_start(out, in_).then_inc(T.sem[sn], 16)
+        cnt[sn] = cnt.get(sn, 0) + 16
+        return (sn, cnt[sn])
+
+    def fan(src):
+        m = -1
+        for c in T.cores:
+            if c != T.cores[src]:
+                m &= topo.mask(T.cores[src], c)
+        return m
+
+    def inside(src, dst):
+        if topo.chip(T.cores[src]) != topo.chip(T.cores[dst]):
+            return 0
+        return topo.mask(T.cores[src], T.cores[dst]) & ~fan(src)
+
+    def send(deps, dsts, name_out, src, sn, apart=False):
+        waits("p", deps)
+        lanes = {}
+        for d in dsts:
+            m = (inside(r, d) if apart else 0) or fan(r)
+            lanes[m] = lanes.get(m, []) + [d]
+        trs = []
+        for m in lanes:
+            ids = []
+            for d in lanes[m]:
+                rid, pid, _ = topo.addr(T.cores[d])
+                ids.append(DstId(rid=rid, pnc=pid))
+            trs.append(RemoteDMATransfer(dst_ids=ids, dma_engine_mask=m, remote_sem=T.sem[sn], srcs=[src],
+                                         dsts=[T[name_out][:] for _ in ids], alu_op=0))
+            cnt["loc"] = cnt.get("loc", 0) + bin(m).count("1")
+        g.remote_dma_fused(trs, local_sem=T.sem.loc)
+
+    def arrive(src, sn, apart=False):
+        cnt[sn] = bin((inside(src, r) if apart else 0) or fan(src)).count("1")
+        return (sn, cnt[sn])
+
+    def play(fs):
+        for f in fs:
+            f()
+
+    l_nx = dma("y", [], "lnx", T.nxi[:], T.nx[:])
+    l_sy = dma("s", [], "lsy", T.syr[:], T.sy[:])
+    if r > 0:
+        l_sc = dma("s", [], "lsc", T.syc[:], T.sy[:])
+        for a in range(8):
+            l_tp = dma("y" if a % 2 else "s", [], "ltp", T.tp[:, 32 * a:32 * a + 32], T.nx[:, 512 * a:512 * a + 512])
+    l_em = dma("y", [], "lem", T.emi[:], T.em[:])
+
+    lo = {"allow_small_or_imprecise_dtypes": True}
+    c_p = do("p", [], lambda: g.iota(T.pci[:], [[0, 2]], 0, 1))
+    c_ig = do("p", [], lambda: g.iota(T.igf[:], [[1, 8], [0, 16]], 0, 0, **lo))
+    if r > 1:
+        c_ev = do("p", [], lambda: g.iota(T.evr[:], [[0, 8], [1, 8], [-100, 2]], 0, 0, **lo))
+    c_row = do("p", [], lambda: g.iota(T.rowf[:], [[1, 128]], 0, 0, **lo))
+    c_pf = do("p", [], lambda: g.iota(T.pf[:], [[0, 1]], 0, 1, **lo))
+    if r > 1:
+        c_ramp = do("p", [], lambda: g.iota(T.ramp[:], [[1, 512]], -256, 0, **lo))
+    c_io = do("p", [], lambda: g.iota(T.io4[:], [[-1, 4], [1, 32]], 32 * r, 0, **lo))
+    c_one = do("v", [], lambda: vec.memset(T.one[:], 1.0))
+    c_zero = do("v", [], lambda: vec.memset(T.zero[:], 0)) if r == 0 else None
+    P1, CI, CF, CO = T.pci[:, 0:1], T.ci5, T.cf5, T.cols
+    ts([c_p], CI[:, 0:1], P1, 4, None, OP.arith_shift_right)
+    ts([], CI[:, 2:3], P1, 1, 7, OP.arith_shift_right, OP.bitwise_and)
+    ts([], CI[:, 3:4], P1, 1, None, OP.bitwise_and)
+    ts([], CI[:, 1:2], P1, 15, None, OP.bitwise_and)
+    x = ts([], CI[:, 4:5], P1, 4, 1, OP.arith_shift_right, OP.bitwise_and)
+    c_cf = do("v", [x], lambda: vec.tensor_copy(CF[:], CI[:]))
+    c_bo = ts([c_cf, c_ig], T.bo[:], T.igf[:], CF[:, 0:1], None, OP.is_equal)
+    m_sy = ts([l_sy], T.syb[:], T.syr[:], -16.0, None, OP.add)
+    if r > 1:
+        ts([c_ev], T.evh[:], T.evr[:], float(first), 64.0, OP.is_ge, OP.mult)
+        c_evl = ts([], T.evl[:], T.evr[:], float(first), None, OP.is_ge)
+        do("t", [c_bo], lambda: mm(T.pc[:, 0:128], T.bo[:], T.bo[:], True, False))
+        do("t", [c_evl], lambda: mm(T.pc[:, 0:128], T.one[:], T.evh[:], False, False))
+        m_o = do("t", [m_sy], lambda: mm(T.pc[:, 0:128], T.one[:], T.syb[:], False, True))
+    do("t", [c_bo], lambda: mm(T.px[:, 0:128], T.bo[:], T.bo[:], True, False))
+    m_x = do("t", [m_sy, c_one], lambda: mm(T.px[:, 0:128], T.one[:], T.syb[:], False, True))
+    m_ta = ts([l_nx], T.ti[:, 0:128], T.nxi[:, 0:128], 511, None, OP.bitwise_and)
+    m_ti = ts([], T.ti[:, 128:256], T.nxi[:, 128:256], 511, None, OP.bitwise_and)
+    x = ts([], CO[:, 2:3], CF[:, 3:4], 100.0, CF[:, 2:3], OP.mult, OP.add)
+    c_k0 = ts([], CO[:, 0:1], CF[:, 3:4], -100.0, CF[:, 2:3], OP.mult, OP.add)
+    if r > 0:
+        ne = do("v", [], lambda: vec.tensor_tensor(CO[:, 4:5], CF[:, 4:5], CF[:, 3:4], OP.not_equal))
+        gt = do("v", [], lambda: vec.tensor_tensor(CO[:, 5:6], CF[:, 3:4], CF[:, 4:5], OP.is_gt))
+        do("v", [], lambda: vec.memset(T.tq[:, 0:16], 0.0))
+        k = ts([ne], CO[:, 6:7], CO[:, 4:5], 256.0, CF[:, 2:3], OP.mult, OP.add)
+        do("v", [], lambda: vec.memset(T.tq[:, 272:288], 0.0))
+        k = ts([k], CO[:, 7:8], CF[:, 4:5], 16.0, CO[:, 6:7], OP.mult, OP.add)
+    so, po, mo = (T.selo, T.pc, m_o) if r > 1 else (T.sel, T.px, m_x)
+    ts([m_ta], T.tb[:, 0:128], T.ti[:, 0:128], -256.0, None, OP.add)
+    m_tb = ts([m_ti], T.tb[:, 128:256], T.ti[:, 128:256], -256.0, None, OP.add)
+    c_k1 = ts([x], CO[:, 1:2], CO[:, 2:3], -100.0, None, OP.add)
+    ts([mo, c_k0], so[:, 0:128], po[:, 0:128], CO[:, 0:1], None, OP.is_equal)
+    m_s1 = ts([c_k1], so[:, 128:256], po[:, 0:128], CO[:, 1:2], None, OP.is_equal)
+    if r > 0:
+        k = ts([k, gt], CO[:, 8:9], CO[:, 5:6], 32.0, CO[:, 7:8], OP.mult, OP.add)
+    if r > 1:
+        ts([m_x], T.selc[:, 0:128], T.px[:, 0:128], CO[:, 0:1], CODE, OP.is_equal, OP.mult)
+        m_sf = ts([], T.selc[:, 128:256], T.px[:, 0:128], CO[:, 1:2], CODE, OP.is_equal, OP.mult)
+    c_mask = ts([c_row], T.mask[:], T.rowf[:, 0:16], CF[:, 1:2], None, OP.is_equal)
+    if r > 0:
+        c_k9 = ts([k], CO[:, 9:10], CO[:, 8:9], 8.0, None, OP.add)
+    c_tri = do("p", [c_bo], lambda: g.affine_select(T.tri[:], T.bo[:], [[1, 128]], OP.is_gt, 0.0, 0, -1))
+
+    def late_constants():
+        th = ts([], T.thr[:], T.rowf[:, 0:4], -3.0, CODE, OP.add, OP.mult)
+        return ts([], T.gind[:], T.rowf[:, 0:8], CF[:, 0:1], None, OP.is_equal), th
+
+    def window_ab(sel, tb, w, deps):
+        a = do("t", deps, lambda: mm(T.pwa[:, 0:256], sel[:, 0:128], tb[:], True, True))
+        b = do("t", [], lambda: mm(T.pwb[:, 0:256], sel[:, 128:256], tb[:], True, True))
+        sa = do("s", [a], lambda: act(w[:, 0:256], T.pwa[:, 0:256], AF.Copy))
+        vb = do("v", [b], lambda: vec.tensor_copy(w[:, 256:512], T.pwb[:, 0:256]))
+        return [sa, vb]
+
+    def window_all(sel, tb, deps, pairs):
+        for h in range(2):
+            c = slice(256 * h, 256 * h + 256)
+            d = do("t", deps, lambda: mm(T.pwa[:, c], sel[:, 128 * h:128 * h + 128], tb[:], True, not pairs))
+            if pairs:
+                d = do("t", [c_ramp, c_evl], lambda: mm(T.pwa[:, c], T.evl[:], T.ramp[:, c], False, True))
+        return d
+
+    def window_out(w, d):
+        return [do("s", [d], lambda: act(w[:], T.pwa[:], AF.Copy))]
+
+    def em_float():
+        return ts([l_em], T.emf[:], T.emi[:], -4 * CODE, None, OP.add)
+
+    def code_parts(c0, c1):
+        c = slice(c0, c1)
+
+        def a0():
+            ts([l_em], T.hi[:, c], T.emi[:, c], 18, None, OP.arith_shift_right)
+
+        def a1():
+            ts([l_nx], T.pb[:, c], T.nxi[:, c], 2048.0, 64.0, OP.is_lt, OP.mult)
+
+        def a2():
+            ts([], T.ci[:, c], T.nxi[:, c], 9, None, OP.arith_shift_right)
+        return [a0, a1, a2]
+
+    def code_rest():
+        n = do("v", [("v", cnt["v"])], lambda: vec.tensor_tensor(T.pb[:, 256:512], T.hi[:], T.pb[:, 0:256], OP.min))
+        return do("v", [n], lambda: vec.tensor_tensor(T.za[:], T.ci[:], T.pb[:, 256:512], OP.subtract))
+
+    def code_mm(banks, sf, em, sc, za, dep_em, dep_za):
+        def numbers(h):
+            c = slice(128 * h, 128 * h + 128)
+            return lambda: do("t", dep_em, lambda: mm(banks[h][:, 0:256], sf[:, c], em[:], True, False))
+
+        def counts():
+            for h in range(2):
+                c = slice(128 * h, 128 * h + 128)
+                d = do("t", dep_za, lambda: mm(banks[h][:, 0:256], sc[:, c], za[:], False, True))
+            return d
+        return [numbers(0), numbers(1), counts]
+
+    def code_out(banks, w, d):
+        do("s", [d], lambda: act(w[:, 0:256], banks[0][:, 0:256], AF.Copy))
+        return do("s", [d], lambda: act(w[:, 256:512], banks[1][:, 0:256], AF.Copy))
+
+    def scaled(out, src, by, deps):
+        return do("s", deps, lambda: act(out[:], src[:], AF.Copy, scale=by))
+
+    em_box, id_box = [None], [None, None]
+    each = 1 if r == 1 else 2
+
+    def lists():
+        sf = do("v", [l_sc], lambda: vec.tensor_copy(CO[:, 3:4], T.syc[:]))
+        ti = ts([l_tp], T.tpi[:], T.tp[:], 511, None, OP.bitwise_and)
+        if r > 1:
+            em_box[0] = em_float()
+        d = ts([sf, c_mask], T.d16[:], T.mask[:], CO[:, 3:4], None, OP.mult)
+        am = do("t", [d], lambda: mm(T.py[:, 64:80], T.bo[:], T.d16[:], True, True))
+        tq = do("v", [ti], lambda: vec.tensor_copy(T.tq[:, 16:272], T.tpi[:]))
+        id_box[0] = ts([c_pf], T.idn[:], T.rowf[:], T.pf[:], None, OP.is_equal)
+        id_box[1] = ts([], T.pm[:], T.rowf[:, 0:8], CF[:, 2:3], None, OP.is_equal)
+        n = 32 // each
+        ts([am, c_k9], T.ot[:, 0:n:2], T.py[:, 64:80:each], 32.0, CO[:, 8:9], OP.mult, OP.add)
+        do("v", [tq], lambda: vec.transpose(T.tab[:, 0:256], T.tq[:, 16:272]))
+        o = ts([], T.ot[:, 1:n:2], T.py[:, 64:80:each], 32.0, CO[:, 9:10], OP.mult, OP.add)
+        tr = do("v", [tq], lambda: vec.transpose(T.tab[:, 256:544], T.tq[:, 0:288]))
+        n0, n1 = (2 * FOURS[0], 30) if r == 1 else (2 * first, 16)
+        return do("v", [tr, o], lambda: vec.tensor_copy(T.lt[:, 16 * n0:16 * n1], T.tab[:].indirect(T.ot[:, n0:n1])))
+
+    def joined(n):
+        return T.cp[:, 512 * n:512 * n + 512]
+
+    def join(n, win, j, deps, qn, m):
+        i = 32 * (j // each)
+        out, src = joined(n), win.indirect(T.lt[:, i:i + 32])
+        keep = 1.0 if m is None else T.pm[:, m:m + 1]
+        if qn == "v":
+            return ts(deps + id_box, out, src, keep, None, OP.mult)
+        return do("s", deps + id_box, lambda: act(out, src, AF.Copy, scale=keep))
+
+    def gather(win, at, deps, k, col):
+        b = col - k
+        tile, x0, d = at
+        return (T.tt, col, ts([d] + deps, T.tt[:, b:b + 16], win.indirect(tile[:, x0:x0 + 1]), 256.0, None, OP.add))
+
+    def code_at(qn, reads, j, ewin, edep, ee):
+        tile, x0, d = reads[j]
+        b = 0 if j == 0 else 16 * j + 16
+        out, src = ee[:, b:b + 16], ewin[:].indirect(tile[:, x0:x0 + 1])
+        if qn == "v":
+            return ts([d, edep, c_mask], out, src, T.mask[:, j:j + 1], None, OP.mult)
+        return do("s", [d, edep, c_mask], lambda: act(out, src, AF.Copy, scale=T.mask[:, j:j + 1]))
+
+    def follow(reads, ewin, edep, ee, steps):
+        for j in steps:
+            last = code_at("s", reads, j, ewin, edep, ee)
+        return last
+
+    def string(q, at, w, wdep, pw, pdep, reg, hooks, last_too):
+        reads = []
+        for j in range(16):
+            reads.append(at)
+            pair = j >= 2 * FIRST.get(q, 8)
+            if not (pair and j % 2):
+                k, col = (j - 1) % 16, reg + 16 + 18 * j
+                if pair:
+                    at = gather(pw(j // 2), at, pdep(j // 2), k, col)
+                elif j < 15 or last_too:
+                    at = gather(w[:], at, wdep, k, col)
+            play(hooks.get(j, []))
+        return reads, at
+
+    gd, ed_, ydep = {}, {}, [None, 0]
+
+    def total(ee, last, out):
+        return do("v", last, lambda: vec.tensor_reduce(out[:], ee[:, 15:271:17], AxisListType.X, OP.add))
+
+    def gates(q, code, dep):
+        gd[q] = ts([dep, c_thr], T["g4%d" % q][:], T.thr[:], code[:], None, OP.is_le)
+
+    def digits(q, code, dep):
+        qi, di, ep = T["qi%d" % q], T["di%d" % q], T["ep%d" % q]
+        box = {}
+
+        def d0():
+            box[0] = do("v", [dep], lambda: vec.tensor_copy(qi[:], code[:]))
+
+        def d1():
+            ts([box[0]], di[:, 0:1], qi[:], 63, None, OP.bitwise_and)
+            ts([], di[:, 1:2], qi[:], 6, 63, OP.arith_shift_right, OP.bitwise_and)
+
+        def d2():
+            ts([], di[:, 2:3], qi[:], 12, 63, OP.arith_shift_right, OP.bitwise_and)
+            box[1] = ts([], di[:, 3:4], qi[:], 18, 63, OP.arith_shift_right, OP.bitwise_and)
+
+        def d3():
+            ed_[q] = do("v", [box[1], gd[q]], lambda: vec.tensor_tensor(ep[:], di[:], T["g4%d" % q][:], OP.mult))
+        return [d0, d1, d2, d3]
+
+    def decode(q, code, dep):
+        return [lambda: gates(q, code, dep)] + digits(q, code, dep)
+
+    banks = {0: T.pb, 1: T.pc, 2: T.pcm, 3: T.pb}
+    free = {}
+    begun = {}
+    bdep = {}
+
+    def count(q, b, stop=False):
+        n = 1 if q == 3 else 4
+        for m in range(0, 4, n):
+            bdep[q] = do("t", [gd[b], c_tri, free.get(q)], lambda: mm(
+                banks[q][:, 0:n], (T.tri if b == q else T.bo)[:], T["g4%d" % b][:, m:m + n], q not in begun, stop and m + n == 4))
+            begun[q] = True
+
+    def position(q):
+        if q < 3:
+            bdep[q] = do("v", [bdep[q]], lambda: vec.tensor_reduce(T.pos[:, q:q + 1], banks[q][:, 0:4], AxisListType.X, OP.add))
+
+    def place(q, final):
+        oh, ep = T["oh%d" % q], T["ep%d" % q]
+
+        def one(m):
+            o = ts([bdep[q], ed_[q], c_io], oh[:, 32 * m:32 * m + 32], T.io4[:, 32 * m:32 * m + 32],
+                   T.pos[:, q:q + 1] if q < 3 else banks[q][:, 0:1], ep[:, m:m + 1], OP.is_equal, OP.mult)
+            ydep[0] = do("t", [o, c_gi], lambda: mm(
+                T.py[0:8, 0:32], T.gind[:], oh[:, 32 * m:32 * m + 32], ydep[1] == 0, final and m == 3))
+            ydep[1] += 1
+        return [lambda: position(q), lambda: one(0), lambda: one(1), lambda: one(2), lambda: one(3)]
+
+    if r == 0:
+        wdep = window_ab(T.sel, T.tb, T.w, [m_s1, m_tb])
+        sfd = scaled(T.self, T.sel, 1.0, [m_s1])
+        scd = scaled(T.selc, T.sel, CODE, [m_s1])
+        parts = []
+        for c in range(0, 256, 64):
+            parts += code_parts(c, c + 64)
+        hooks = {}
+        for n in range(len(parts)):
+            hooks[n + 2] = [parts[n]]
+        reads, at = string(0, (T.zero, 0, c_zero), T.w, wdep, None, None, 0, hooks, True)
+        s1 = T.tt[:, at[1]:at[1] + 2]
+        send([at[2]], [2, 3], "s1", s1, "as1")
+        send([], [1], "s1", s1, "as1")
+        emd = em_float()
+        zad = code_rest()
+        cb = (T.pew, T.pcm)
+        fs = code_mm(cb, T.self, T.emf, T.selc, T.za, [sfd, emd], [scd, zad])
+        play(fs[:2])
+        ed = code_out(cb, T.e, fs[2]())
+        c_gi, c_thr = late_constants()
+        last = follow(reads, T.e, ed, T.eea, range(0, 16, 2))
+        for j in range(1, 16, 2):
+            last_v = code_at("v", reads, j, T.e, ed, T.eea)
+        oc = total(T.eea, [last, last_v], T.oca)
+        send([oc], [2, 3, 1], "rc0", T.oca[:], "arc0")
+        play(decode(0, T.oca, oc))
+        count(0, 0, True)
+        play(place(0, False))
+        count(1, 0)
+        a1 = arrive(1, "arc1")
+        gates(1, T.rc1, a1)
+        count(1, 1, True)
+        play(digits(1, T.rc1, a1))
+        play(place(1, True))
+    elif r == 1:
+        wdep = window_out(T.w, window_all(T.sel, T.tb, [m_s1, m_tb], False))
+        send(wdep, [2, 3], "w1", T.w[:], "aw1", True)
+        ltd = lists()
+        va, sa = FOURS
+        dv = join(0, T.w[:], va + 2, wdep + [ltd], "v", None)
+        ds = join(3, T.w[:], sa + 2, wdep + [ltd], "s", None)
+        emd = em_float()
+        dv = join(1, joined(0), va + 1, [dv], "v", None)
+        ds = join(4, joined(3), sa + 1, [ds], "s", None)
+        parts = code_parts(0, 256)
+        parts[0]()
+        dv = join(2, joined(1), va, [dv], "v", (va + 3) // 2)
+        ds = join(5, joined(4), sa, [ds], "s", (sa + 3) // 2)
+        play(parts[1:])
+        md = []
+        for n, d in ((2, dv), (5, ds)):
+            for h in range(2):
+                x = 512 * n + 256 * h
+                md.append(do("t", [d] + id_box, lambda: mm((T.pcm, T.px)[h][:, 0:256], T.idn[:], T.cp[:, x:x + 256],
+                                                           n == 2, n == 5)))
+        cmd = [do("v", [md[2]], lambda: vec.tensor_copy(T.cpm[:, 0:256], T.pcm[:, 0:256])),
+               do("s", [md[3]], lambda: act(T.cpm[:, 256:512], T.px[:, 0:256], AF.Copy))]
+        free[2] = cmd[0]
+        send(cmd, [2, 3], "cp1", T.cpm[:], "acp1", True)
+        sfd = scaled(T.self, T.sel, 1.0, [m_s1])
+        scd = scaled(T.selc, T.sel, CODE, [m_s1])
+        zad = code_rest()
+        cb = (T.pew, T.pwb)
+        fs = code_mm(cb, T.self, T.emf, T.selc, T.za, [sfd, emd], [scd, zad])
+        play(fs[:2])
+        ed = code_out(cb, T.e, fs[2]())
+        reads = string(1, (T.s1, 0, arrive(0, "as1")), T.w, wdep, None, None, 0, {}, False)[0]
+        last = follow(reads, T.e, ed, T.eea, range(15))
+        c_gi, c_thr = late_constants()
+        last_v = code_at("v", reads, 15, T.e, ed, T.eea)
+        oc = total(T.eea, [last, last_v], T.oca)
+        send([oc], [2, 3, 0], "rc1", T.oca[:], "arc1", True)
+        play(decode(1, T.oca, oc))
+        count(1, 1)
+        a0 = arrive(0, "arc0")
+        gates(0, T.rc0, a0)
+        count(1, 0, True)
+        count(0, 0, True)
+        count(2, 0)
+        count(2, 1)
+        play(digits(0, T.rc0, a0))
+        play(place(0, False))
+        play(place(1, False))
+        a2 = arrive(3, "arc2")
+        gates(2, T.rc2, a2)
+        count(2, 2, True)
+        play(digits(2, T.rc2, a2))
+        play(place(2, True))
+    else:
+        o = 5 - r
+        wdep = window_out(T.w, window_all(T.selo, T.tb, [m_s1, m_tb], True))
+        sfd = scaled(T.self, T.selc, 1.0 / CODE, [m_sf])
+        send([m_sf], [o], "selx", T.selc[:], "aselx")
+        ltd = lists()
+        emd = em_box[0]
+        send([emd], [o], "emx", T.emf[:], "aemx")
+        if first:
+            send(wdep, [o], "wx", T.w[:], "awx")
+        on_s, made = list(range(first, 5)), {}
+        axs = arrive(o, "aselx")
+        between = 2 if r == 3 else len(on_s)
+        for m in on_s[:between]:
+            made[m] = join(m, T.w[:], 2 * m, wdep + [ltd], "s", m)
+        sfx = scaled(T.selfx, T.selx, 1.0 / CODE, [axs])
+        for m in on_s[between:]:
+            made[m] = join(m, T.w[:], 2 * m, wdep + [ltd], "s", m)
+        for m in (5, 6, 7):
+            made[m] = join(m, T.w[:], 2 * m, wdep + [ltd], "v", m)
+        play(code_parts(0, 256))
+        zad = code_rest()
+        send([zad], [o], "zax", T.za[:], "azax")
+        own_banks, other_banks = (T.pew, T.pwb), (T.px, T.pwa)
+        axe, axz = arrive(o, "aemx"), arrive(o, "azax")
+        own = code_mm(own_banks, T.self, T.emf, T.selc, T.za, [sfd, emd], [zad])
+        other = code_mm(other_banks, T.selfx, T.emx, T.selx, T.zax, [sfx, axe, m_sf, wdep[0]], [axz])
+        codes = {r: (own, own_banks, T.e), o: (other, other_banks, T.ex)}
+        code2, code3 = codes[2][0], codes[3][0]
+        e2, e3 = codes[2][2], codes[3][2]
+        order = [5, on_s[0], 6, on_s[1], 7] + on_s[2:]
+        for n in range(len(order)):
+            if r == 3 and n == 5:
+                code2.pop(0)()
+            m = order[n]
+            md = do("t", [made[m]] + id_box, lambda: mm(T.pcm[:], T.idn[:], joined(m), n == 0, n == len(order) - 1))
+        cmd = do("s", [md], lambda: act(T.cpm[:], T.pcm[:], AF.Copy))
+        free[2] = cmd
+        send([cmd], [o], "cpx", T.cpm[:], "acpx")
+        play(code2[:-1])
+        e2d = code_out(codes[2][1], e2, code2[-1]())
+        play(code3[:-1])
+        m3 = code3[-1]()
+        aw1, acp1 = [arrive(1, "aw1", True)], [arrive(1, "acp1", True)]
+        awx, acpx = [arrive(o, "awx")] if FIRST[o] else [], [arrive(o, "acpx")]
+        at = (T.s1, 0, arrive(0, "as1"))
+        for j in range(FOURS[0]):
+            at = gather(T.w1[:], at, aw1, (j - 1) % 16, 16 + 18 * j)
+            if j == 0:
+                c_gi, c_thr = late_constants()
+        for j in FOURS:
+            at = gather(T.cp1[:], at, acp1, j - 1, 16 + 18 * j)
+        runs = {r: (T.w, wdep, joined, lambda m: [made[m]]), o: (T.wx, awx, lambda m: T.cpx[:], lambda m: acpx)}
+        reads, at = string(2, at, *runs[2], 320, {}, True)
+        last = follow(reads, e2, e2d, T.eea, range(16))
+        e3d = code_out(codes[3][1], e3, m3)
+        a0, a1 = arrive(0, "arc0"), arrive(1, "arc1", True)
+        box = {}
+
+        def g0():
+            gates(0, T.rc0, a0)
+            for q in range(1 if r == 2 else 2, 4):
+                count(q, 0)
+
+        def t2():
+            box[2] = total(T.eea, [last], T.oca)
+            if r == 3:
+                send([box[2]], [1], "rc2", T.oca[:], "arc2")
+
+        def g2():
+            gates(2, T.oca, box[2])
+            count(2, 2)
+            count(3, 2)
+
+        def g1():
+            gates(1, T.rc1, a1)
+            if r == 2:
+                count(1, 1, True)
+            count(2, 1, True)
+            count(3, 1)
+        D2, p2 = digits(2, T.oca, None), place(2, False)
+        D1, p1 = (digits(1, T.rc1, a1), place(1, False)) if r == 2 else ([], [])
+        hooks = {0: [g0], 2: [t2], 4: [g2] + D2[:1], 6: D2[1:2], 8: D2[2:3], 10: D2[3:], 12: [g1] + D1[:1], 14: D1[1:3]}
+        reads3 = string(3, at, *runs[3], 640, hooks, False)[0]
+        last3 = follow(reads3, e3, e3d, T.eeb, range(15))
+        last_v = code_at("v", reads3, 15, e3, e3d, T.eeb)
+        play(D1[3:])
+        oc = total(T.eeb, [last3, last_v], T.ocb)
+        play(p2[:1] + p1[:1])
+        D3 = digits(3, T.ocb, oc)
+        D3[0]()
+        gates(3, T.ocb, oc)
+        count(3, 3, True)
+        play(p2[1:4])
+        play(D3[1:3])
+        play(p2[4:] + p1[1:3])
+        D3[3]()
+        play(p1[3:])
+        if r == 3:
+            for b in (0, 2, 1, 3):
+                zd = do("t", [gd[b], e3d], lambda: mm(T.pew[0:8, 0:4], T.gind[:], T["g4%d" % b][:], b == 0, b == 3))
+        play(place(3, True))
+        if r == 3:
+            zr = do("v", [zd], lambda: vec.tensor_reduce(T.zed[:], T.pew[0:8, 0:4], AxisListType.X, OP.add))
+            nd = ts([zr, c_io], T.neg[:], T.io4[0:8, 0:32], T.zed[:], -1.0, OP.is_ge, OP.mult)
+    if r == 3:
+        yd = do("v", [ydep[0], nd], lambda: vec.tensor_tensor(T.ysb[:], T.py[0:8, 0:32], T.neg[:], OP.add))
+    else:
+        yd = do("v", [ydep[0]], lambda: vec.tensor_copy(T.ysb[:], T.py[0:8, 0:32]))
+    dma("y", [yd], "st", T.y[:], T.ysb[:])
+    for sn in list(cnt):
+        if sn != "st":
+            waits("p", [(sn, cnt[sn])])
+    waits("p", [("st", 16)])

@@ -5,43 +5,55 @@ from concourse.mybir import dt, AluOpType, AxisListType, ActivationFunctionType
 F, H, I, U = "float32", "bfloat16", "int32", "uint16"
 SCRATCH = {
     "nxi": ("sbuf", [128, 256], I), "emi": ("sbuf", [128, 256], I), "syr": ("sbuf", [1, 128], I),
-    "syb": ("sbuf", [1, 128], H), "one": ("sbuf", [1, 128], H), "syc": ("sbuf", [128, 1], I),
-    "evr": ("sbuf", [1, 128], F), "evh": ("sbuf", [1, 128], H), "evl": ("sbuf", [1, 128], H), "ramp": ("sbuf", [1, 512], H),
+    "syb": ("sbuf", [1, 128], H), "one": ("sbuf", [1, 128], H), "six": ("sbuf", [1, 128], H), "syc": ("sbuf", [128, 1], I),
+    "evl": ("sbuf", [1, 128], H), "ramp": ("sbuf", [1, 512], H),
     "pci": ("sbuf", [128, 2], I), "pf": ("sbuf", [128, 1], F), "igf": ("sbuf", [128, 128], F),
-    "rowf": ("sbuf", [128, 128], F), "io4": ("sbuf", [128, 128], F),
-    "ci5": ("sbuf", [128, 5], I), "cf5": ("sbuf", [128, 5], F), "cols": ("sbuf", [128, 12], F),
-    "bo": ("sbuf", [128, 128], H), "tri": ("sbuf", [128, 128], H), "idn": ("sbuf", [128, 128], H),
-    "mask": ("sbuf", [128, 16], F), "pm": ("sbuf", [128, 8], F), "gind": ("sbuf", [128, 8], H), "thr": ("sbuf", [128, 4], F),
-    "ti": ("sbuf", [128, 256], I), "sel": ("sbuf", [128, 256], H), "selo": ("sbuf", [128, 256], H), "tb": ("sbuf", [128, 256], H),
+    "rowf": ("sbuf", [128, 128], F), "pl": ("sbuf", [128, 36], F), "plb": ("sbuf", [128, 36], F), "mg": ("sbuf", [128, 64], F),
+    "ci5": ("sbuf", [128, 6], I), "cf5": ("sbuf", [128, 6], F), "cols": ("sbuf", [128, 16], F),
+    "bo": ("sbuf", [128, 128], H), "tri": ("sbuf", [128, 128], H), "idn": ("sbuf", [128, 128], H), "dba": ("sbuf", [128, 128], H),
+    "mask": ("sbuf", [128, 16], F), "pm": ("sbuf", [128, 16], F), "gind": ("sbuf", [128, 8], H), "thr": ("sbuf", [128, 4], F),
+    "thg": ("sbuf", [128, 32], F), "tho": ("sbuf", [128, 32], F), "l32": ("sbuf", [128, 4], U),
+    "ti": ("sbuf", [128, 256], I), "sel": ("sbuf", [128, 256], H), "selo": ("sbuf", [128, 256], H),
     "hi": ("sbuf", [128, 256], I), "ci": ("sbuf", [128, 256], I), "za": ("sbuf", [128, 256], H), "emf": ("sbuf", [128, 256], F),
-    "self": ("sbuf", [128, 256], F), "selc": ("sbuf", [128, 256], H), "selfx": ("sbuf", [128, 256], F),
-    "selx": ("sbuf", [128, 256], H), "emx": ("sbuf", [128, 256], F), "zax": ("sbuf", [128, 256], H),
-    "tp": ("sbuf", [128, 256], I), "tpi": ("sbuf", [128, 256], I), "tq": ("sbuf", [128, 288], F), "tab": ("sbuf", [128, 544], F),
+    "self": ("sbuf", [128, 256], F), "tq": ("sbuf", [128, 288], H), "tab": ("sbuf", [128, 544], H),
     "d16": ("sbuf", [128, 16], H), "ot": ("sbuf", [128, 32], U), "lt": ("sbuf", [128, 512], U),
-    "w": ("sbuf", [128, 512], H), "w1": ("sbuf", [128, 512], H), "wx": ("sbuf", [128, 512], H),
-    "e": ("sbuf", [128, 512], F), "ex": ("sbuf", [128, 512], F),
-    "cp": ("sbuf", [128, 4096], H), "cpm": ("sbuf", [128, 512], H), "cpx": ("sbuf", [128, 512], H), "cp1": ("sbuf", [128, 512], H),
+    "w": ("sbuf", [128, 512], H), "w1": ("sbuf", [128, 512], H), "e": ("sbuf", [128, 512], F), "ex": ("sbuf", [128, 512], F),
+    "cp": ("sbuf", [128, 7168], H), "cpm": ("sbuf", [128, 512], H), "cpx": ("sbuf", [128, 512], H),
     "s1": ("sbuf", [128, 2], U), "zero": ("sbuf", [128, 2], U), "tt": ("sbuf", [128, 1080], U),
     "eea": ("sbuf", [128, 272], F), "eeb": ("sbuf", [128, 272], F), "pos": ("sbuf", [128, 4], F), "zed": ("sbuf", [8, 1], F),
-    "rc0": ("sbuf", [128, 1], F), "rc1": ("sbuf", [128, 1], F), "rc2": ("sbuf", [128, 1], F),
-    "oca": ("sbuf", [128, 1], F), "ocb": ("sbuf", [128, 1], F), "ysb": ("sbuf", [8, 32], F), "neg": ("sbuf", [8, 32], F),
+    "ysb": ("sbuf", [8, 32], F), "neg": ("sbuf", [8, 32], F),
     "px": ("psum", [128, 512], F), "pwa": ("psum", [128, 512], F), "pwb": ("psum", [128, 512], F),
     "pcm": ("psum", [128, 512], F), "pew": ("psum", [128, 512], F), "pb": ("psum", [128, 512], F),
     "pc": ("psum", [128, 512], F), "py": ("psum", [128, 512], F),
 }
 for _q in range(4):
-    SCRATCH["qi%d" % _q] = ("sbuf", [128, 1], I)
-    SCRATCH["di%d" % _q] = ("sbuf", [128, 4], I)
-    SCRATCH["g4%d" % _q] = ("sbuf", [128, 4], H)
-    SCRATCH["ep%d" % _q] = ("sbuf", [128, 4], F)
-    SCRATCH["oh%d" % _q] = ("sbuf", [128, 128], H)
-SEMAPHORES = ["v", "s", "t", "p", "lnx", "lsy", "lsc", "ltp", "lem", "st", "loc",
-              "as1", "aw1", "acp1", "awx", "aselx", "aemx", "azax", "acpx", "arc0", "arc1", "arc2"]
+    SCRATCH["oh%d" % _q] = ("sbuf", [128, 36], H)
+for _q in "ab":
+    SCRATCH["rc" + _q] = ("sbuf", [128, 8], F)
+    SCRATCH["qi" + _q] = ("sbuf", [128, 2], I)
+    SCRATCH["di" + _q] = ("sbuf", [128, 8], I)
+    SCRATCH["g4" + _q] = ("sbuf", [128, 8], H)
+    SCRATCH["gg" + _q] = ("sbuf", [128, 64], H)
+    SCRATCH["ep" + _q] = ("sbuf", [128, 64], H)
+for _q in "01":
+    SCRATCH["dec" + _q] = ("sbuf", [128, 34], H)
+SEMAPHORES = ["v", "s", "t", "p", "lnx", "lsy", "lsc", "lem", "st", "loc",
+              "as1", "aw1", "acpx", "aex", "arc0", "arc1", "arc2"]
 OP = AluOpType
 AF = ActivationFunctionType
-FIRST = {2: 1, 3: 0}
-FOURS = (8, 12)
+SEGS = {0: [(1, "")] * 16,
+        1: [(1, "")] * 9 + [(3, "s"), (4, "v")],
+        2: [(1, "")] * 4 + [(3, "s"), (3, "v"), (3, "s"), (3, "v")],
+        3: [(3, "s"), (3, "v"), (3, "s"), (3, "v"), (3, "s")]}
 CODE = 262144.0
+
+
+def segments(q):
+    out, j = [], 0
+    for n, qn in SEGS[q]:
+        out.append((j, n, qn))
+        j += n
+    return out
 
 
 def rank_program(g, core, T, topo):
@@ -52,7 +64,8 @@ def rank_program(g, core, T, topo):
     cnt = {}
     seen = {}
     vec, act, mm = g.vector, g.scalar.activation, g.tensor.matmul
-    first = FIRST.get(r, 8)
+    long = [s for s in segments(r) if s[1] > 1]
+    tb = T.tq[:, 16:272]
 
     def waits(qn, deps):
         need = {}
@@ -73,6 +86,9 @@ def rank_program(g, core, T, topo):
     def ts(deps, *a):
         return do("v", deps, lambda: vec.tensor_scalar(*a))
 
+    def tten(deps, *a):
+        return do("v", deps, lambda: vec.tensor_tensor(*a))
+
     def dma(qn, deps, sn, out, in_):
         waits(qn, deps)
         Q[qn].dma_start(out, in_).then_inc(T.sem[sn], 16)
@@ -86,30 +102,18 @@ def rank_program(g, core, T, topo):
                 m &= topo.mask(T.cores[src], c)
         return m
 
-    def inside(src, dst):
-        if topo.chip(T.cores[src]) != topo.chip(T.cores[dst]):
-            return 0
-        return topo.mask(T.cores[src], T.cores[dst]) & ~fan(src)
-
-    def send(deps, dsts, name_out, src, sn, apart=False):
+    def send(deps, dsts, out, src, sn):
         waits("p", deps)
-        lanes = {}
+        ids = []
         for d in dsts:
-            m = (inside(r, d) if apart else 0) or fan(r)
-            lanes[m] = lanes.get(m, []) + [d]
-        trs = []
-        for m in lanes:
-            ids = []
-            for d in lanes[m]:
-                rid, pid, _ = topo.addr(T.cores[d])
-                ids.append(DstId(rid=rid, pnc=pid))
-            trs.append(RemoteDMATransfer(dst_ids=ids, dma_engine_mask=m, remote_sem=T.sem[sn], srcs=[src],
-                                         dsts=[T[name_out][:] for _ in ids], alu_op=0))
-            cnt["loc"] = cnt.get("loc", 0) + bin(m).count("1")
-        g.remote_dma_fused(trs, local_sem=T.sem.loc)
+            rid, pid, _ = topo.addr(T.cores[d])
+            ids.append(DstId(rid=rid, pnc=pid))
+        g.remote_dma_fused([RemoteDMATransfer(dst_ids=ids, dma_engine_mask=fan(r), remote_sem=T.sem[sn], srcs=[src],
+                                              dsts=[out for _ in ids], alu_op=0)], local_sem=T.sem.loc)
+        cnt["loc"] = cnt.get("loc", 0) + bin(fan(r)).count("1")
 
-    def arrive(src, sn, apart=False):
-        cnt[sn] = bin((inside(src, r) if apart else 0) or fan(src)).count("1")
+    def arrive(src, sn):
+        cnt[sn] = bin(fan(src)).count("1")
         return (sn, cnt[sn])
 
     def play(fs):
@@ -120,163 +124,233 @@ def rank_program(g, core, T, topo):
     l_sy = dma("s", [], "lsy", T.syr[:], T.sy[:])
     if r > 0:
         l_sc = dma("s", [], "lsc", T.syc[:], T.sy[:])
-        for a in range(8):
-            l_tp = dma("y" if a % 2 else "s", [], "ltp", T.tp[:, 32 * a:32 * a + 32], T.nx[:, 512 * a:512 * a + 512])
     l_em = dma("y", [], "lem", T.emi[:], T.em[:])
 
     lo = {"allow_small_or_imprecise_dtypes": True}
-    c_p = do("p", [], lambda: g.iota(T.pci[:], [[0, 2]], 0, 1))
+    c_p = do("p", [], lambda: g.iota(T.pci[:, 0:1], [[0, 1]], 0, 1))
     c_ig = do("p", [], lambda: g.iota(T.igf[:], [[1, 8], [0, 16]], 0, 0, **lo))
-    if r > 1:
-        c_ev = do("p", [], lambda: g.iota(T.evr[:], [[0, 8], [1, 8], [-100, 2]], 0, 0, **lo))
+    if r > 0:
+        c_17 = do("p", [], lambda: g.iota(T.pci[:, 1:2], [[0, 1]], 0, 17))
     c_row = do("p", [], lambda: g.iota(T.rowf[:], [[1, 128]], 0, 0, **lo))
-    c_pf = do("p", [], lambda: g.iota(T.pf[:], [[0, 1]], 0, 1, **lo))
-    if r > 1:
+    if r > 0:
         c_ramp = do("p", [], lambda: g.iota(T.ramp[:], [[1, 512]], -256, 0, **lo))
-    c_io = do("p", [], lambda: g.iota(T.io4[:], [[-1, 4], [1, 32]], 32 * r, 0, **lo))
-    c_one = do("v", [], lambda: vec.memset(T.one[:], 1.0))
-    c_zero = do("v", [], lambda: vec.memset(T.zero[:], 0)) if r == 0 else None
+        x = do("v", [], lambda: vec.memset(T.evl[:], 0.0))
+    c_six = do("v", [], lambda: vec.memset(T.six[:], 64.0))
     P1, CI, CF, CO = T.pci[:, 0:1], T.ci5, T.cf5, T.cols
     ts([c_p], CI[:, 0:1], P1, 4, None, OP.arith_shift_right)
-    ts([], CI[:, 2:3], P1, 1, 7, OP.arith_shift_right, OP.bitwise_and)
-    ts([], CI[:, 3:4], P1, 1, None, OP.bitwise_and)
-    ts([], CI[:, 1:2], P1, 15, None, OP.bitwise_and)
-    x = ts([], CI[:, 4:5], P1, 4, 1, OP.arith_shift_right, OP.bitwise_and)
-    c_cf = do("v", [x], lambda: vec.tensor_copy(CF[:], CI[:]))
-    c_bo = ts([c_cf, c_ig], T.bo[:], T.igf[:], CF[:, 0:1], None, OP.is_equal)
-    m_sy = ts([l_sy], T.syb[:], T.syr[:], -16.0, None, OP.add)
-    if r > 1:
-        ts([c_ev], T.evh[:], T.evr[:], float(first), 64.0, OP.is_ge, OP.mult)
-        c_evl = ts([], T.evl[:], T.evr[:], float(first), None, OP.is_ge)
-        do("t", [c_bo], lambda: mm(T.pc[:, 0:128], T.bo[:], T.bo[:], True, False))
-        do("t", [c_evl], lambda: mm(T.pc[:, 0:128], T.one[:], T.evh[:], False, False))
-        m_o = do("t", [m_sy], lambda: mm(T.pc[:, 0:128], T.one[:], T.syb[:], False, True))
-    do("t", [c_bo], lambda: mm(T.px[:, 0:128], T.bo[:], T.bo[:], True, False))
-    m_x = do("t", [m_sy, c_one], lambda: mm(T.px[:, 0:128], T.one[:], T.syb[:], False, True))
-    m_ta = ts([l_nx], T.ti[:, 0:128], T.nxi[:, 0:128], 511, None, OP.bitwise_and)
-    m_ti = ts([], T.ti[:, 128:256], T.nxi[:, 128:256], 511, None, OP.bitwise_and)
-    x = ts([], CO[:, 2:3], CF[:, 3:4], 100.0, CF[:, 2:3], OP.mult, OP.add)
-    c_k0 = ts([], CO[:, 0:1], CF[:, 3:4], -100.0, CF[:, 2:3], OP.mult, OP.add)
+    y = ts([], CI[:, 1:2], P1, 15, None, OP.bitwise_and)
+    if r == 0:
+        c_zero = do("v", [], lambda: vec.memset(T.zero[:], 0))
+    else:
+        for j, n, _ in long:
+            c_evl = do("v", [x], lambda: vec.memset(T.evl[:, j + n - 2:128:16], 1.0))
+    c_cf = do("v", [y], lambda: vec.tensor_copy(CF[:, 0:2], CI[:, 0:2]))
     if r > 0:
-        ne = do("v", [], lambda: vec.tensor_tensor(CO[:, 4:5], CF[:, 4:5], CF[:, 3:4], OP.not_equal))
-        gt = do("v", [], lambda: vec.tensor_tensor(CO[:, 5:6], CF[:, 3:4], CF[:, 4:5], OP.is_gt))
+        ne = ts([c_17], CI[:, 2:3], T.pci[:, 1:2], 4, 1, OP.arith_shift_right, OP.bitwise_and)
         do("v", [], lambda: vec.memset(T.tq[:, 0:16], 0.0))
-        k = ts([ne], CO[:, 6:7], CO[:, 4:5], 256.0, CF[:, 2:3], OP.mult, OP.add)
-        do("v", [], lambda: vec.memset(T.tq[:, 272:288], 0.0))
-        k = ts([k], CO[:, 7:8], CF[:, 4:5], 16.0, CO[:, 6:7], OP.mult, OP.add)
-    so, po, mo = (T.selo, T.pc, m_o) if r > 1 else (T.sel, T.px, m_x)
-    ts([m_ta], T.tb[:, 0:128], T.ti[:, 0:128], -256.0, None, OP.add)
-    m_tb = ts([m_ti], T.tb[:, 128:256], T.ti[:, 128:256], -256.0, None, OP.add)
-    c_k1 = ts([x], CO[:, 1:2], CO[:, 2:3], -100.0, None, OP.add)
-    ts([mo, c_k0], so[:, 0:128], po[:, 0:128], CO[:, 0:1], None, OP.is_equal)
-    m_s1 = ts([c_k1], so[:, 128:256], po[:, 0:128], CO[:, 1:2], None, OP.is_equal)
+    c_bo = ts([c_cf, c_ig], T.bo[:], T.igf[:], CF[:, 0:1], None, OP.is_equal)
     if r > 0:
-        k = ts([k, gt], CO[:, 8:9], CO[:, 5:6], 32.0, CO[:, 7:8], OP.mult, OP.add)
-    if r > 1:
-        ts([m_x], T.selc[:, 0:128], T.px[:, 0:128], CO[:, 0:1], CODE, OP.is_equal, OP.mult)
-        m_sf = ts([], T.selc[:, 128:256], T.px[:, 0:128], CO[:, 1:2], CODE, OP.is_equal, OP.mult)
+        c_k8 = ts([ne], CO[:, 8:9], CI[:, 2:3], 17.0, CF[:, 1:2], OP.mult, OP.add)
+        do("v", [], lambda: vec.memset(T.tq[:, 272:288], 0.0))
+    m_sy = ts([l_sy], T.syb[:], T.syr[:], 1.0 / 32, -0.25, OP.mult, OP.add)
     c_mask = ts([c_row], T.mask[:], T.rowf[:, 0:16], CF[:, 1:2], None, OP.is_equal)
     if r > 0:
-        c_k9 = ts([k], CO[:, 9:10], CO[:, 8:9], 8.0, None, OP.add)
+        do("t", [c_bo], lambda: mm(T.pc[:, 0:128], T.bo[:], T.bo[:], True, False))
+        do("t", [c_evl, c_six], lambda: mm(T.pc[:, 0:128], T.six[:], T.evl[:], False, False))
+        m_o = do("t", [m_sy], lambda: mm(T.pc[:, 0:128], T.six[:], T.syb[:], False, True))
+        sf = do("v", [l_sc], lambda: vec.tensor_copy(CO[:, 3:4], T.syc[:]))
+        c_k9 = ts([c_k8], CO[:, 9:10], CO[:, 8:9], 1.0 / 16, None, OP.add)
+        c_pm = tten([c_mask], T.pm[:, 1:16], T.mask[:, 1:16], T.mask[:, 0:15], OP.add)
+    do("t", [c_bo], lambda: mm(T.px[:, 0:128], T.bo[:], T.bo[:], True, False))
+    m_x = do("t", [m_sy, c_six], lambda: mm(T.px[:, 0:128], T.six[:], T.syb[:], False, True))
+    m_ta = ts([l_nx], T.ti[:, 0:128], T.nxi[:, 0:128], 511, None, OP.bitwise_and)
+    if r > 0:
+        d16 = ts([sf, c_mask], T.d16[:], T.mask[:], CO[:, 3:4], 0.125, OP.mult, OP.mult)
+        am = do("t", [d16], lambda: mm(T.py[:, 64:80], T.bo[:], T.d16[:], True, True))
+    m_ti = ts([], T.ti[:, 128:256], T.nxi[:, 128:256], 511, None, OP.bitwise_and)
+
+    def select(out, X, h, deps):
+        return ts(deps, out[:, 128 * h:128 * h + 128], X[:, 0:128], float(h), CF[:, 1:2], OP.add, OP.is_equal)
+    so, po, mo = (T.selo, T.pc, m_o) if r > 0 else (T.sel, T.px, m_x)
+    m_s0 = select(so, po, 0, [mo])
+    m_t0 = ts([m_ta], T.tq[:, 16:144], T.ti[:, 0:128], -256.0, None, OP.add)
+    if r == 0:
+        m_0 = do("t", [m_s0, m_t0], lambda: mm(T.pc[:, 0:2], T.sel[:, 0:128], T.tq[:, 16:18], True, True))
+    m_tb = ts([m_ti], T.tq[:, 144:272], T.ti[:, 128:256], -256.0, None, OP.add)
+    m_s1 = select(so, po, 1, [])
+    if r > 0:
+        c_idn = do("p", [c_bo], lambda: g.affine_select(T.idn[:], T.bo[:], [[1, 128]], OP.is_equal, 0.0, 0, -1))
     c_tri = do("p", [c_bo], lambda: g.affine_select(T.tri[:], T.bo[:], [[1, 128]], OP.is_gt, 0.0, 0, -1))
+    c_pl = do("p", [], lambda: g.iota(T.pl[:], [[1, 36]], 32 * r - 3, 0, **lo))
+    do("p", [], lambda: g.iota(T.mg[:, 0:32], [[0, 4], [1, 8]], 0, 0, **lo))
+    c_mg = do("p", [], lambda: g.iota(T.mg[:, 32:64], [[1, 4], [0, 8]], -3, 0, **lo))
+    K = {"pm": c_pm} if r > 0 else {}
 
     def late_constants():
-        th = ts([], T.thr[:], T.rowf[:, 0:4], -3.0, CODE, OP.add, OP.mult)
-        return ts([], T.gind[:], T.rowf[:, 0:8], CF[:, 0:1], None, OP.is_equal), th
+        def a():
+            K["o"] = ts([c_mg], T.tho[:], T.mg[:, 0:32], CF[:, 0:1], 256.0, OP.not_equal, OP.mult)
+            K["up"] = ts([], CO[:, 5:6], CF[:, 1:2], 8.0, None, OP.is_ge)
 
-    def window_ab(sel, tb, w, deps):
-        a = do("t", deps, lambda: mm(T.pwa[:, 0:256], sel[:, 0:128], tb[:], True, True))
-        b = do("t", [], lambda: mm(T.pwb[:, 0:256], sel[:, 128:256], tb[:], True, True))
-        sa = do("s", [a], lambda: act(w[:, 0:256], T.pwa[:, 0:256], AF.Copy))
-        vb = do("v", [b], lambda: vec.tensor_copy(w[:, 256:512], T.pwb[:, 0:256]))
-        return [sa, vb]
+        def b():
+            ts([], T.thr[:], T.rowf[:, 0:4], -3.0, None, OP.add)
+            ts([K["up"]], T.l32[:], T.rowf[:, 0:8:2], CO[:, 5:6], None, OP.add)
 
-    def window_all(sel, tb, deps, pairs):
+        def c():
+            K["late"] = tten([K["o"]], T.thg[:], T.tho[:], T.mg[:, 32:64], OP.add)
+        return [a, b, c]
+
+    def code_parts():
+        def part(kind, h):
+            c = slice(128 * h, 128 * h + 128)
+            u = slice(256 + 128 * h, 384 + 128 * h)
+
+            def f():
+                if kind == "sel":
+                    d = select(T.sel, T.px, h, [m_x])
+                elif kind == "em":
+                    d = ts([l_em], T.emf[:, c], T.emi[:, c], 1.0 / CODE, -4.0, OP.mult, OP.add)
+                elif kind == "hi":
+                    d = ts([l_em], T.hi[:, c], T.emi[:, c], 18, None, OP.arith_shift_right)
+                elif kind == "top":
+                    d = ts([], T.pb[:, c], T.nxi[:, c], 2048.0, 64.0, OP.is_lt, OP.mult)
+                elif kind == "ci":
+                    d = ts([], T.ci[:, c], T.nxi[:, c], 9, None, OP.arith_shift_right)
+                elif kind == "min":
+                    d = tten([K["hi", h], K["top", h]], T.pb[:, u], T.hi[:, c], T.pb[:, c], OP.min)
+                else:
+                    d = tten([K["min", h], K["ci", h]], T.za[:, c], T.ci[:, c], T.pb[:, u], OP.subtract)
+                K[kind, h] = d
+            return f
+        kinds = (["sel"] if r > 0 else []) + ["em", "hi", "top", "ci", "min", "za"]
+        return [part(kind, h) for kind in kinds for h in range(2)]
+
+    EB = (T.pew, T.pwb)
+
+    def code_sel():
+        K["self"] = do("s", [K.get(("sel", 1), m_s1)], lambda: act(T.self[:], T.sel[:], AF.Copy))
+
+    def code_numbers(deps):
         for h in range(2):
-            c = slice(256 * h, 256 * h + 256)
-            d = do("t", deps, lambda: mm(T.pwa[:, c], sel[:, 128 * h:128 * h + 128], tb[:], True, not pairs))
-            if pairs:
-                d = do("t", [c_ramp, c_evl], lambda: mm(T.pwa[:, c], T.evl[:], T.ramp[:, c], False, True))
+            do("t", [K["self"], K["em", 1]] + deps, lambda: mm(EB[h][:, 0:256], T.self[:, 128 * h:128 * h + 128], T.emf[:], True, False))
+
+    def code_counts():
+        for h in range(2):
+            K["eb", h] = do("t", [K["za", 1]], lambda: mm(EB[h][:, 0:256], T.sel[:, 128 * h:128 * h + 128], T.za[:], False, True))
+
+    def code_out():
+        for h in range(2):
+            d = do("s", [K["eb", h]], lambda: act(T.e[:, 256 * h:256 * h + 256], EB[h][:, 0:256], AF.Copy))
         return d
 
-    def window_out(w, d):
-        return [do("s", [d], lambda: act(w[:], T.pwa[:], AF.Copy))]
+    def window():
+        wb = (T.pwa, T.pwb)
+        for h in range(2):
+            do("t", [c_ramp], lambda: mm(wb[h][:, 0:256], T.evl[:], T.ramp[:, 256 * h:256 * h + 256], True, False))
+        for h in range(2):
+            d = do("t", [m_s1 if h else m_s0, m_tb], lambda: mm(wb[h][:, 0:256], T.selo[:, 128 * h:128 * h + 128], tb, False, True))
+            d = do("s", [d], lambda: act(T.w[:, 256 * h:256 * h + 256], wb[h][:, 0:256], AF.Copy))
+        return d
 
-    def em_float():
-        return ts([l_em], T.emf[:], T.emi[:], -4 * CODE, None, OP.add)
+    def turned():
+        do("v", [m_tb], lambda: vec.transpose(T.tab[:, 0:256], T.tq[:, 16:272]))
+        do("v", [], lambda: vec.transpose(T.tab[:, 256:544], T.tq[:, 0:288]))
+        ts([am, c_k9], T.ot[:, 0:32:2], T.py[:, 64:80], CO[:, 8:9], 16.0, OP.add, OP.mult)
+        K["tab"] = ts([], T.ot[:, 1:32:2], T.py[:, 64:80], CO[:, 9:10], 16.0, OP.add, OP.mult)
 
-    def code_parts(c0, c1):
-        c = slice(c0, c1)
+    def lists(seg):
+        j, n, _ = seg
+        K["lt", j] = ts([K["tab"]], T.lt[:, 32 * j:32 * (j + n - 1)], T.tab[:].indirect(T.ot[:, 2 * j:2 * (j + n - 1)]),
+                        256.0, None, OP.add)
 
-        def a0():
-            ts([l_em], T.hi[:, c], T.emi[:, c], 18, None, OP.arith_shift_right)
+    slot = [0]
 
-        def a1():
-            ts([l_nx], T.pb[:, c], T.nxi[:, c], 2048.0, 64.0, OP.is_lt, OP.mult)
+    def joins(seg, plus=None):
+        j, n, qn = seg
+        box = [T.w[:], K["w"]]
 
-        def a2():
-            ts([], T.ci[:, c], T.nxi[:, c], 9, None, OP.arith_shift_right)
-        return [a0, a1, a2]
+        def one(i):
+            def f():
+                x = slot[0]
+                out = T.cp[:, 512 * x:512 * x + 512]
+                slot[0] += 1
+                src = box[0].indirect(T.lt[:, 32 * i:32 * i + 32])
+                keep = T.pm[:, j + n - 1:j + n] if i == (j + n - 2 if plus else j) else 1.0
+                deps = [box[1], K["lt", j], K["pm"]]
+                if plus and i == j:
+                    y, e = K["join", plus[0]]
+                    d = tten(deps + [e], T.cpm[:] if r == 1 else out, src, T.cp[:, 512 * y:512 * y + 512], OP.add)
+                elif qn == "v":
+                    d = ts(deps, out, src, keep, None, OP.mult)
+                else:
+                    d = do("s", deps, lambda: act(out, src, AF.Copy, scale=keep))
+                box[0], box[1] = out, d
+                if i == j:
+                    K["join", j] = (x, d)
+            return f
+        return [one(i) for i in range(j + n - 2, j - 1, -1)]
 
-    def code_rest():
-        n = do("v", [("v", cnt["v"])], lambda: vec.tensor_tensor(T.pb[:, 256:512], T.hi[:], T.pb[:, 0:256], OP.min))
-        return do("v", [n], lambda: vec.tensor_tensor(T.za[:], T.ci[:], T.pb[:, 256:512], OP.subtract))
+    def merge_constants():
+        ends = [T.pm[:, j + n - 1:j + n] for j, n, _ in long]
+        d = K["pm"]
+        while len(ends) > 2:
+            d = ts([d], CO[:, 10 + len(ends):11 + len(ends)], ends[0], ends[1], ends[2], OP.add, OP.add)
+            ends = [CO[:, 10 + len(ends):11 + len(ends)]] + ends[3:]
+        d = ts([d], CO[:, 10:11], ends[0], ends[-1], 0.0, OP.add, OP.is_equal)
+        K["dba"] = do("s", [d, c_idn], lambda: act(T.dba[:], T.idn[:], AF.Copy, scale=CO[:, 10:11]))
 
-    def code_mm(banks, sf, em, sc, za, dep_em, dep_za):
-        def numbers(h):
-            c = slice(128 * h, 128 * h + 128)
-            return lambda: do("t", dep_em, lambda: mm(banks[h][:, 0:256], sf[:, c], em[:], True, False))
+    MB = (T.pcm, T.pc)
 
-        def counts():
-            for h in range(2):
-                c = slice(128 * h, 128 * h + 128)
-                d = do("t", dep_za, lambda: mm(banks[h][:, 0:256], sc[:, c], za[:], False, True))
-            return d
-        return [numbers(0), numbers(1), counts]
+    def merge_add(lhs, src, x, deps, first=False, last=False):
+        return [do("t", deps, lambda: mm(MB[h][:, 0:256], lhs[:], src[:, x + 256 * h:x + 256 * h + 256], first, last))
+                for h in range(2)]
 
-    def code_out(banks, w, d):
-        do("s", [d], lambda: act(w[:, 0:256], banks[0][:, 0:256], AF.Copy))
-        return do("s", [d], lambda: act(w[:, 256:512], banks[1][:, 0:256], AF.Copy))
+    def merge(order):
+        merge_add(T.dba, T.w, 0, [K["dba"], K["w"]], True)
+        for seg in order:
+            n, d = K["join", seg[0]]
+            md = merge_add(T.idn, T.cp, 512 * n, [d], False, seg == order[-1])
+        return md
 
-    def scaled(out, src, by, deps):
-        return do("s", deps, lambda: act(out[:], src[:], AF.Copy, scale=by))
+    def merge_out(md):
+        return [do("v", [md[0]], lambda: vec.tensor_copy(T.cpm[:, 0:256], MB[0][:, 0:256])),
+                do("s", [md[1]], lambda: act(T.cpm[:, 256:512], MB[1][:, 0:256], AF.Copy))]
 
-    em_box, id_box = [None], [None, None]
-    each = 1 if r == 1 else 2
+    def weave(*rows):
+        rows = [list(x) for x in rows]
+        out = []
+        while any(rows):
+            for x in rows:
+                if x:
+                    out.append(x.pop(0))
+        return out
 
-    def lists():
-        sf = do("v", [l_sc], lambda: vec.tensor_copy(CO[:, 3:4], T.syc[:]))
-        ti = ts([l_tp], T.tpi[:], T.tp[:], 511, None, OP.bitwise_and)
-        if r > 1:
-            em_box[0] = em_float()
-        d = ts([sf, c_mask], T.d16[:], T.mask[:], CO[:, 3:4], None, OP.mult)
-        am = do("t", [d], lambda: mm(T.py[:, 64:80], T.bo[:], T.d16[:], True, True))
-        tq = do("v", [ti], lambda: vec.tensor_copy(T.tq[:, 16:272], T.tpi[:]))
-        id_box[0] = ts([c_pf], T.idn[:], T.rowf[:], T.pf[:], None, OP.is_equal)
-        id_box[1] = ts([], T.pm[:], T.rowf[:, 0:8], CF[:, 2:3], None, OP.is_equal)
-        n = 32 // each
-        ts([am, c_k9], T.ot[:, 0:n:2], T.py[:, 64:80:each], 32.0, CO[:, 8:9], OP.mult, OP.add)
-        do("v", [tq], lambda: vec.transpose(T.tab[:, 0:256], T.tq[:, 16:272]))
-        o = ts([], T.ot[:, 1:n:2], T.py[:, 64:80:each], 32.0, CO[:, 9:10], OP.mult, OP.add)
-        tr = do("v", [tq], lambda: vec.transpose(T.tab[:, 256:544], T.tq[:, 0:288]))
-        n0, n1 = (2 * FOURS[0], 30) if r == 1 else (2 * first, 16)
-        return do("v", [tr, o], lambda: vec.tensor_copy(T.lt[:, 16 * n0:16 * n1], T.tab[:].indirect(T.ot[:, n0:n1])))
+    free_col = [16]
 
-    def joined(n):
-        return T.cp[:, 512 * n:512 * n + 512]
-
-    def join(n, win, j, deps, qn, m):
-        i = 32 * (j // each)
-        out, src = joined(n), win.indirect(T.lt[:, i:i + 32])
-        keep = 1.0 if m is None else T.pm[:, m:m + 1]
-        if qn == "v":
-            return ts(deps + id_box, out, src, keep, None, OP.mult)
-        return do("s", deps + id_box, lambda: act(out, src, AF.Copy, scale=keep))
-
-    def gather(win, at, deps, k, col):
+    def gather(win, at, deps, k):
+        col = free_col[0]
+        free_col[0] += 32
         b = col - k
         tile, x0, d = at
         return (T.tt, col, ts([d] + deps, T.tt[:, b:b + 16], win.indirect(tile[:, x0:x0 + 1]), 256.0, None, OP.add))
+
+    def string(q, at, plain, joined, inner, hooks, start=0):
+        reads, late = {0: at}, []
+        segs = segments(q)
+        for m in range(start, len(segs)):
+            j, n, _ = segs[m]
+            win, deps = plain if n == 1 else joined
+            at = gather(win, at, deps, (j - 1) % 16)
+            play(late)
+            late = []
+            for i in range(j, j + n):
+                reads[i + 1] = at
+            if inner:
+                for i in range(j + (q > 1), j + n - 2):
+                    def f(i=i, win=win if q > 1 else plain[0]):
+                        reads[i + 1] = gather(win, reads[i], [], i - 1)
+                    late.append(f)
+            play(hooks.get(m, []))
+        return reads, at, late
 
     def code_at(qn, reads, j, ewin, edep, ee):
         tile, x0, d = reads[j]
@@ -286,280 +360,228 @@ def rank_program(g, core, T, topo):
             return ts([d, edep, c_mask], out, src, T.mask[:, j:j + 1], None, OP.mult)
         return do("s", [d, edep, c_mask], lambda: act(out, src, AF.Copy, scale=T.mask[:, j:j + 1]))
 
-    def follow(reads, ewin, edep, ee, steps):
+    def follow(qn, reads, ewin, edep, ee, steps):
         for j in steps:
-            last = code_at("s", reads, j, ewin, edep, ee)
+            last = code_at(qn, reads, j, ewin, edep, ee)
         return last
 
-    def string(q, at, w, wdep, pw, pdep, reg, hooks, last_too):
-        reads = []
-        for j in range(16):
-            reads.append(at)
-            pair = j >= 2 * FIRST.get(q, 8)
-            if not (pair and j % 2):
-                k, col = (j - 1) % 16, reg + 16 + 18 * j
-                if pair:
-                    at = gather(pw(j // 2), at, pdep(j // 2), k, col)
-                elif j < 15 or last_too:
-                    at = gather(w[:], at, wdep, k, col)
-            play(hooks.get(j, []))
-        return reads, at
+    cd, gd = {}, {}
+    ydep = [None, 0]
 
-    gd, ed_, ydep = {}, {}, [None, 0]
+    def buf(name, q, n):
+        x = n * (q == 3)
+        return T[name + "ab"[q // 2]][:, x:x + n]
 
-    def total(ee, last, out):
-        return do("v", last, lambda: vec.tensor_reduce(out[:], ee[:, 15:271:17], AxisListType.X, OP.add))
+    def code(q):
+        return T["rc" + "ab"[q // 2]][:, 4 * (q == 3):4 * (q == 3) + 1]
 
-    def gates(q, code, dep):
-        gd[q] = ts([dep, c_thr], T["g4%d" % q][:], T.thr[:], code[:], None, OP.is_le)
+    def total(q, ee, last):
+        cd[q] = do("v", last, lambda: vec.tensor_reduce(code(q), ee[:, 15:271:17], AxisListType.X, OP.add))
 
-    def digits(q, code, dep):
-        qi, di, ep = T["qi%d" % q], T["di%d" % q], T["ep%d" % q]
-        box = {}
+    def gates(q):
+        gd[q] = ts([cd[q], K["late"]], buf("g4", q, 4), T.thr[:], code(q), None, OP.is_le)
 
-        def d0():
-            box[0] = do("v", [dep], lambda: vec.tensor_copy(qi[:], code[:]))
+    def spread(q):
+        K["gg", q] = ts([cd[q], K["late"]], buf("gg", q, 32), T.thg[:], code(q), None, OP.is_le)
 
-        def d1():
-            ts([box[0]], di[:, 0:1], qi[:], 63, None, OP.bitwise_and)
-            ts([], di[:, 1:2], qi[:], 6, 63, OP.arith_shift_right, OP.bitwise_and)
+    def digits(qs, ep):
+        n, x = len(qs), "ab"[qs[0] // 2]
+        qi, di = T["qi" + x][:, 0:n], T["di" + x]
 
-        def d2():
-            ts([], di[:, 2:3], qi[:], 12, 63, OP.arith_shift_right, OP.bitwise_and)
-            box[1] = ts([], di[:, 3:4], qi[:], 18, 63, OP.arith_shift_right, OP.bitwise_and)
+        def whole():
+            K["qi"] = ts([cd[q] for q in qs], qi, T["rc" + x][:, 0:4 * n:4], CODE, None, OP.mult)
 
-        def d3():
-            ed_[q] = do("v", [box[1], gd[q]], lambda: vec.tensor_tensor(ep[:], di[:], T["g4%d" % q][:], OP.mult))
-        return [d0, d1, d2, d3]
+        def low():
+            ts([K["qi"]], di[:, 0:4 * n:4], qi, 63, None, OP.bitwise_and)
+            ts([], di[:, 1:4 * n:4], qi, 6, 63, OP.arith_shift_right, OP.bitwise_and)
 
-    def decode(q, code, dep):
-        return [lambda: gates(q, code, dep)] + digits(q, code, dep)
+        def high():
+            ts([], di[:, 2:4 * n:4], qi, 12, 63, OP.arith_shift_right, OP.bitwise_and)
+            K["di"] = ts([], di[:, 3:4 * n:4], qi, 18, 63, OP.arith_shift_right, OP.bitwise_and)
 
-    banks = {0: T.pb, 1: T.pc, 2: T.pcm, 3: T.pb}
-    free = {}
-    begun = {}
-    bdep = {}
+        def used():
+            K["ep"] = tten([K["di"]] + [K["gg", q] for q in qs], ep, di[:, 0:4 * n].indirect(T.l32[:, 0:2 * n]),
+                           T["gg" + x][:, 0:32 * n], OP.mult)
+        return [whole, low, high, used]
 
-    def count(q, b, stop=False):
-        n = 1 if q == 3 else 4
-        for m in range(0, 4, n):
-            bdep[q] = do("t", [gd[b], c_tri, free.get(q)], lambda: mm(
-                banks[q][:, 0:n], (T.tri if b == q else T.bo)[:], T["g4%d" % b][:, m:m + n], q not in begun, stop and m + n == 4))
-            begun[q] = True
+    def count(out, lhs, q, start=True, stop=True):
+        g4 = T["g4" + "ab"[q // 2]]
+        for m in range(4):
+            x = 4 * (q == 3) + m
+            d = do("t", [gd[q], c_tri], lambda: mm(out, lhs[:], g4[:, x:x + 1], start and m == 0, stop and m == 3))
+        return d
 
-    def position(q):
-        if q < 3:
-            bdep[q] = do("v", [bdep[q]], lambda: vec.tensor_reduce(T.pos[:, q:q + 1], banks[q][:, 0:4], AxisListType.X, OP.add))
+    def hot(q, deps, first):
+        K["oh", q] = ts(deps + [c_pl], T["oh%d" % q][:], (T.pl if q < 2 else T.plb)[:], first, None, OP.is_equal)
 
-    def place(q, final):
-        oh, ep = T["oh%d" % q], T["ep%d" % q]
+    def from_two(deps):
+        return ts(deps + [c_pl], T.plb[:], T.pl[:], T.dec1[:, 33:34], None, OP.subtract)
 
-        def one(m):
-            o = ts([bdep[q], ed_[q], c_io], oh[:, 32 * m:32 * m + 32], T.io4[:, 32 * m:32 * m + 32],
-                   T.pos[:, q:q + 1] if q < 3 else banks[q][:, 0:1], ep[:, m:m + 1], OP.is_equal, OP.mult)
-            ydep[0] = do("t", [o, c_gi], lambda: mm(
-                T.py[0:8, 0:32], T.gind[:], oh[:, 32 * m:32 * m + 32], ydep[1] == 0, final and m == 3))
+    def add(q, src, x, deps, final=False):
+        for m in range(4):
+            ydep[0] = do("t", [K["oh", q]] + deps, lambda: mm(
+                T.py[0:8, 0:32], src[:, x + 8 * m:x + 8 * m + 8], T["oh%d" % q][:, 3 - m:35 - m], ydep[1] == 0, final and m == 3))
             ydep[1] += 1
-        return [lambda: position(q), lambda: one(0), lambda: one(1), lambda: one(2), lambda: one(3)]
+
+    def finish(q, base, bdep):
+        dec = T["dec%d" % q]
+        D = digits([q], dec[:, 0:32])
+
+        def a():
+            D[0]()
+            gates(q)
+            count(T.pb[:, 0:1], T.tri, q)
+            K["sum"] = count(T.pb[:, 1:2], T.bo, q)
+            spread(q)
+
+        def b():
+            K["pos"] = ts([K["sum"], bdep], dec[:, 32:34], T.pb[:, 0:2], base, None, OP.add)
+        return [a] + D[1:] + [b]
 
     if r == 0:
-        wdep = window_ab(T.sel, T.tb, T.w, [m_s1, m_tb])
-        sfd = scaled(T.self, T.sel, 1.0, [m_s1])
-        scd = scaled(T.selc, T.sel, CODE, [m_s1])
-        parts = []
-        for c in range(0, 256, 64):
-            parts += code_parts(c, c + 64)
-        hooks = {}
-        for n in range(len(parts)):
-            hooks[n + 2] = [parts[n]]
-        reads, at = string(0, (T.zero, 0, c_zero), T.w, wdep, None, None, 0, hooks, True)
-        s1 = T.tt[:, at[1]:at[1] + 2]
-        send([at[2]], [2, 3], "s1", s1, "as1")
-        send([], [1], "s1", s1, "as1")
-        emd = em_float()
-        zad = code_rest()
-        cb = (T.pew, T.pcm)
-        fs = code_mm(cb, T.self, T.emf, T.selc, T.za, [sfd, emd], [scd, zad])
-        play(fs[:2])
-        ed = code_out(cb, T.e, fs[2]())
-        c_gi, c_thr = late_constants()
-        last = follow(reads, T.e, ed, T.eea, range(0, 16, 2))
-        for j in range(1, 16, 2):
-            last_v = code_at("v", reads, j, T.e, ed, T.eea)
-        oc = total(T.eea, [last, last_v], T.oca)
-        send([oc], [2, 3, 1], "rc0", T.oca[:], "arc0")
-        play(decode(0, T.oca, oc))
-        count(0, 0, True)
-        play(place(0, False))
-        count(1, 0)
-        a1 = arrive(1, "arc1")
-        gates(1, T.rc1, a1)
-        count(1, 1, True)
-        play(digits(1, T.rc1, a1))
-        play(place(1, True))
-    elif r == 1:
-        wdep = window_out(T.w, window_all(T.sel, T.tb, [m_s1, m_tb], False))
-        send(wdep, [2, 3], "w1", T.w[:], "aw1", True)
-        ltd = lists()
-        va, sa = FOURS
-        dv = join(0, T.w[:], va + 2, wdep + [ltd], "v", None)
-        ds = join(3, T.w[:], sa + 2, wdep + [ltd], "s", None)
-        emd = em_float()
-        dv = join(1, joined(0), va + 1, [dv], "v", None)
-        ds = join(4, joined(3), sa + 1, [ds], "s", None)
-        parts = code_parts(0, 256)
-        parts[0]()
-        dv = join(2, joined(1), va, [dv], "v", (va + 3) // 2)
-        ds = join(5, joined(4), sa, [ds], "s", (sa + 3) // 2)
-        play(parts[1:])
-        md = []
-        for n, d in ((2, dv), (5, ds)):
-            for h in range(2):
-                x = 512 * n + 256 * h
-                md.append(do("t", [d] + id_box, lambda: mm((T.pcm, T.px)[h][:, 0:256], T.idn[:], T.cp[:, x:x + 256],
-                                                           n == 2, n == 5)))
-        cmd = [do("v", [md[2]], lambda: vec.tensor_copy(T.cpm[:, 0:256], T.pcm[:, 0:256])),
-               do("s", [md[3]], lambda: act(T.cpm[:, 256:512], T.px[:, 0:256], AF.Copy))]
-        free[2] = cmd[0]
-        send(cmd, [2, 3], "cp1", T.cpm[:], "acp1", True)
-        sfd = scaled(T.self, T.sel, 1.0, [m_s1])
-        scd = scaled(T.selc, T.sel, CODE, [m_s1])
-        zad = code_rest()
-        cb = (T.pew, T.pwb)
-        fs = code_mm(cb, T.self, T.emf, T.selc, T.za, [sfd, emd], [scd, zad])
-        play(fs[:2])
-        ed = code_out(cb, T.e, fs[2]())
-        reads = string(1, (T.s1, 0, arrive(0, "as1")), T.w, wdep, None, None, 0, {}, False)[0]
-        last = follow(reads, T.e, ed, T.eea, range(15))
-        c_gi, c_thr = late_constants()
-        last_v = code_at("v", reads, 15, T.e, ed, T.eea)
-        oc = total(T.eea, [last, last_v], T.oca)
-        send([oc], [2, 3, 0], "rc1", T.oca[:], "arc1", True)
-        play(decode(1, T.oca, oc))
-        count(1, 1)
-        a0 = arrive(0, "arc0")
-        gates(0, T.rc0, a0)
-        count(1, 0, True)
-        count(0, 0, True)
-        count(2, 0)
-        count(2, 1)
-        play(digits(0, T.rc0, a0))
-        play(place(0, False))
-        play(place(1, False))
-        a2 = arrive(3, "arc2")
-        gates(2, T.rc2, a2)
-        count(2, 2, True)
-        play(digits(2, T.rc2, a2))
-        play(place(2, True))
+        a = do("t", [m_tb], lambda: mm(T.pwa[:, 0:256], T.sel[:, 0:128], tb, True, True))
+        b = do("t", [m_s1], lambda: mm(T.pwb[:, 0:256], T.sel[:, 128:256], tb, True, True))
+        at = (T.s1, 0, ts([m_0], T.s1[:], T.pc[:, 0:2], 256.0, None, OP.add))
+        wdep = [do("s", [a], lambda: act(T.w[:, 0:256], T.pwa[:, 0:256], AF.Copy)),
+                do("v", [b], lambda: vec.tensor_copy(T.w[:, 256:512], T.pwb[:, 0:256]))]
+        code_sel()
+        parts = code_parts()
+        hooks = {n + 2: [parts[n]] for n in range(len(parts))}
+        hooks[3].append(lambda: code_numbers(wdep))
+        hooks[13].append(code_counts)
+        reads, at1, _ = string(0, at, (T.w[:], wdep), None, False, hooks, 1)
+        reads[0], reads[1] = (T.zero, 0, c_zero), at
+        send([at1[2]], [1], T.s1[:], T.tt[:, at1[1]:at1[1] + 2], "as1")
+        last = follow("s", reads, T.e, code_out(), T.eea, range(16))
+        lc = late_constants()
+        hooks = {n: [lc[n]] for n in range(3)}
+        at = string(1, at1, (T.w1[:], [arrive(1, "aw1")]), (T.cpx[:], [arrive(1, "acpx")]), False, hooks)[1]
+        send([at[2]], [3, 2], T.s1[:], T.tt[:, at[1]:at[1] + 2], "as1")
+        total(0, T.eea, [last])
+        play(finish(0, 0.0, None))
+        send([K["pos"]], [1], T.dec0[:], T.dec0[:], "arc0")
+        hot(0, [K["pos"]], T.dec0[:, 32:33])
+        add(0, T.dec0, 0, [])
+        hot(1, [arrive(1, "arc1")], T.dec1[:, 32:33])
+        add(1, T.dec1, 0, [], True)
     else:
-        o = 5 - r
-        wdep = window_out(T.w, window_all(T.selo, T.tb, [m_s1, m_tb], True))
-        sfd = scaled(T.self, T.selc, 1.0 / CODE, [m_sf])
-        send([m_sf], [o], "selx", T.selc[:], "aselx")
-        ltd = lists()
-        emd = em_box[0]
-        send([emd], [o], "emx", T.emf[:], "aemx")
-        if first:
-            send(wdep, [o], "wx", T.w[:], "awx")
-        on_s, made = list(range(first, 5)), {}
-        axs = arrive(o, "aselx")
-        between = 2 if r == 3 else len(on_s)
-        for m in on_s[:between]:
-            made[m] = join(m, T.w[:], 2 * m, wdep + [ltd], "s", m)
-        sfx = scaled(T.selfx, T.selx, 1.0 / CODE, [axs])
-        for m in on_s[between:]:
-            made[m] = join(m, T.w[:], 2 * m, wdep + [ltd], "s", m)
-        for m in (5, 6, 7):
-            made[m] = join(m, T.w[:], 2 * m, wdep + [ltd], "v", m)
-        play(code_parts(0, 256))
-        zad = code_rest()
-        send([zad], [o], "zax", T.za[:], "azax")
-        own_banks, other_banks = (T.pew, T.pwb), (T.px, T.pwa)
-        axe, axz = arrive(o, "aemx"), arrive(o, "azax")
-        own = code_mm(own_banks, T.self, T.emf, T.selc, T.za, [sfd, emd], [zad])
-        other = code_mm(other_banks, T.selfx, T.emx, T.selx, T.zax, [sfx, axe, m_sf, wdep[0]], [axz])
-        codes = {r: (own, own_banks, T.e), o: (other, other_banks, T.ex)}
-        code2, code3 = codes[2][0], codes[3][0]
-        e2, e3 = codes[2][2], codes[3][2]
-        order = [5, on_s[0], 6, on_s[1], 7] + on_s[2:]
-        for n in range(len(order)):
-            if r == 3 and n == 5:
-                code2.pop(0)()
-            m = order[n]
-            md = do("t", [made[m]] + id_box, lambda: mm(T.pcm[:], T.idn[:], joined(m), n == 0, n == len(order) - 1))
-        cmd = do("s", [md], lambda: act(T.cpm[:], T.pcm[:], AF.Copy))
-        free[2] = cmd
-        send([cmd], [o], "cpx", T.cpm[:], "acpx")
-        play(code2[:-1])
-        e2d = code_out(codes[2][1], e2, code2[-1]())
-        play(code3[:-1])
-        m3 = code3[-1]()
-        aw1, acp1 = [arrive(1, "aw1", True)], [arrive(1, "acp1", True)]
-        awx, acpx = [arrive(o, "awx")] if FIRST[o] else [], [arrive(o, "acpx")]
-        at = (T.s1, 0, arrive(0, "as1"))
-        for j in range(FOURS[0]):
-            at = gather(T.w1[:], at, aw1, (j - 1) % 16, 16 + 18 * j)
-            if j == 0:
-                c_gi, c_thr = late_constants()
-        for j in FOURS:
-            at = gather(T.cp1[:], at, acp1, j - 1, 16 + 18 * j)
-        runs = {r: (T.w, wdep, joined, lambda m: [made[m]]), o: (T.wx, awx, lambda m: T.cpx[:], lambda m: acpx)}
-        reads, at = string(2, at, *runs[2], 320, {}, True)
-        last = follow(reads, e2, e2d, T.eea, range(16))
-        e3d = code_out(codes[3][1], e3, m3)
-        a0, a1 = arrive(0, "arc0"), arrive(1, "arc1", True)
-        box = {}
+        K["w"] = window()
+        parts = code_parts()
+        to = {1: 0, 2: 3, 3: 2}[r]
+        if SEGS[r][0][0] == 1:
+            send([K["w"]], [to], T.w1[:], T.w[:], "aw1")
+        on = {qn: [s for s in long if s[2] == qn] for qn in "sv"}
+        numbers = [code_sel, lambda: code_numbers([K["w"]])]
+        if r == 3:
+            play(parts[:2] + numbers[:1])
+        turned()
+        for s in on["s"]:
+            lists(s)
+        if r == 3:
+            play(parts[2:4] + numbers[1:])
+        for s in on["v"]:
+            lists(s)
+        js = weave(*[joins(s) for s in on["s"]])
+        jv = weave(*[joins(s, p) for s, p in zip(on["v"], on["s"])])
+        order = on["v"][:1] + on["s"][len(on["v"]):] + on["v"][1:]
+        lc = late_constants()
+        if r == 1:
+            play(js + weave(jv[:-1], parts[0:4:2], parts[1:4:2]) + numbers + jv[-1:])
+            cmd = [K["join", on["v"][0][0]][1]]
+            send(cmd, [to], T.cpx[:], T.cpm[:], "acpx")
+            play(parts[4:] + [code_counts] + lc)
+            ed = code_out()
+        if r == 2:
+            play(js[:1] + [merge_constants] + js[1:] + jv[:2] + parts[:4] + numbers[:1] + jv[2:])
+            md = merge(order)
+            play(parts[4:7])
+            cmd = merge_out(md)
+            send(cmd, [to], T.cpx[:], T.cpm[:], "acpx")
+            play(numbers[1:] + parts[7:] + [code_counts] + lc)
+            ed = code_out()
+        if r == 3:
+            play(js[:1] + [merge_constants] + js[1:4] + parts[4:] + [code_counts])
+            ed = code_out()
+            send([ed], [to], T.ex[:], T.e[:], "aex")
+            play(js[4:] + jv)
+            md = merge(order)
+            play(lc)
+            cmd = merge_out(md)
+            send(cmd, [to], T.cpx[:], T.cpm[:], "acpx")
+    if r == 1:
+        reads, _, late = string(1, (T.s1, 0, arrive(0, "as1")), (T.w[:], []), (T.cpm[:], cmd), True, {})
+        play(late)
+        last = follow("s", reads, T.e, ed, T.eea, range(13))
+        last_v = follow("v", reads, T.e, ed, T.eea, (15, 13, 14))
+        total(1, T.eea, [last, last_v])
+        a0 = arrive(0, "arc0")
+        play(finish(1, T.dec0[:, 33:34], a0))
+        send([K["pos"]], [2, 3, 0], T.dec1[:], T.dec1[:], "arc1")
+        for q in range(2):
+            hot(q, [K["pos"]], T["dec%d" % q][:, 32:33])
+            add(q, T["dec%d" % q], 0, [])
+        base = from_two([])
+        cd[2] = arrive(2, "arc2")
+        D = digits([2], T.epb[:, 0:32])
+        D[0]()
+        gates(2)
+        c2 = count(T.pwa[:, 0:1], T.tri, 2)
+        spread(2)
+        play(D[1:])
+        hot(2, [c2, base], T.pwa[:, 0:1])
+        add(2, T.epb, 0, [], True)
+    if r > 1:
+        own, other = (T.cpm[:], cmd), (T.cpx[:], [arrive(5 - r, "acpx")])
+        plain = (T.w[:], []) if r == 2 else (T.w1[:], [arrive(2, "aw1")])
+        reads2, at, late = string(2, (T.s1, 0, arrive(0, "as1")), plain, own if r == 2 else other, r == 2, {})
+        a1 = arrive(1, "arc1")
 
-        def g0():
-            gates(0, T.rc0, a0)
-            for q in range(1 if r == 2 else 2, 4):
-                count(q, 0)
+        def counts2(start):
+            gates(2)
+            K["c2"] = count(T.pwa[:, 0:1], T.tri, 2)
+            K["c3"] = count(T.pb[:, 0:1], T.bo, 2, start, not start)
+            spread(2)
 
         def t2():
-            box[2] = total(T.eea, [last], T.oca)
-            if r == 3:
-                send([box[2]], [1], "rc2", T.oca[:], "arc2")
+            total(2, T.eea, [K["l2"], K["v2"]])
+            send([cd[2]], [3, 1], code(2), code(2), "arc2")
 
-        def g2():
-            gates(2, T.oca, box[2])
-            count(2, 2)
-            count(3, 2)
-
-        def g1():
-            gates(1, T.rc1, a1)
-            if r == 2:
-                count(1, 1, True)
-            count(2, 1, True)
-            count(3, 1)
-        D2, p2 = digits(2, T.oca, None), place(2, False)
-        D1, p1 = (digits(1, T.rc1, a1), place(1, False)) if r == 2 else ([], [])
-        hooks = {0: [g0], 2: [t2], 4: [g2] + D2[:1], 6: D2[1:2], 8: D2[2:3], 10: D2[3:], 12: [g1] + D1[:1], 14: D1[1:3]}
-        reads3 = string(3, at, *runs[3], 640, hooks, False)[0]
-        last3 = follow(reads3, e3, e3d, T.eeb, range(15))
-        last_v = code_at("v", reads3, 15, e3, e3d, T.eeb)
-        play(D1[3:])
-        oc = total(T.eeb, [last3, last_v], T.ocb)
-        play(p2[:1] + p1[:1])
-        D3 = digits(3, T.ocb, oc)
-        D3[0]()
-        gates(3, T.ocb, oc)
-        count(3, 3, True)
-        play(p2[1:4])
-        play(D3[1:3])
-        play(p2[4:] + p1[1:3])
-        D3[3]()
-        play(p1[3:])
+        def v2():
+            K["l2"] = follow("s", reads2, T.e, ed, T.eea, range(14))
+            K["v2"] = follow("v", reads2, T.e, ed, T.eea, (14, 15))
+        if r == 2:
+            e3, e3d = T.ex, arrive(3, "aex")
+            hooks = {0: late + [v2], 1: [t2], 2: [lambda: counts2(True)]}
+        else:
+            e3, e3d = T.e, ed
+            hooks = {}
+        reads3, _, late = string(3, at, None, other if r == 2 else own, True, hooks)
+        on_s = 11 if r == 2 else 13
+        last = follow("s", reads3, e3, e3d, T.eeb, range(on_s))
+        last_v = follow("v", reads3, e3, e3d, T.eeb, range(on_s, 16))
+        total(3, T.eeb, [last, last_v])
+        D = digits([2, 3], T.epb[:])
+        gates(3)
+        K["c3"] = count(T.pb[:, 0:1], T.tri, 3, r == 3, r == 2)
         if r == 3:
-            for b in (0, 2, 1, 3):
-                zd = do("t", [gd[b], e3d], lambda: mm(T.pew[0:8, 0:4], T.gind[:], T["g4%d" % b][:], b == 0, b == 3))
-        play(place(3, True))
+            cd[2] = arrive(2, "arc2")
+            counts2(False)
+        D[0]()
+        spread(3)
+        base = from_two([a1])
+        if r == 2:
+            hot(1, [], T.dec1[:, 32:33])
+            add(1, T.dec1, 0, [])
+        play(D[1:3])
+        hot(2, [K["c2"], base], T.pwa[:, 0:1])
+        hot(3, [K["c3"]], T.pb[:, 0:1])
         if r == 3:
-            zr = do("v", [zd], lambda: vec.tensor_reduce(T.zed[:], T.pew[0:8, 0:4], AxisListType.X, OP.add))
-            nd = ts([zr, c_io], T.neg[:], T.io4[0:8, 0:32], T.zed[:], -1.0, OP.is_ge, OP.mult)
-    if r == 3:
-        yd = do("v", [ydep[0], nd], lambda: vec.tensor_tensor(T.ysb[:], T.py[0:8, 0:32], T.neg[:], OP.add))
-    else:
-        yd = do("v", [ydep[0]], lambda: vec.tensor_copy(T.ysb[:], T.py[0:8, 0:32]))
+            add(2, T.ggb, 0, [])
+            add(3, T.ggb, 32, [])
+        D[3]()
+        add(2, T.epb, 0, [K["ep"]])
+        add(3, T.epb, 32, [], True)
+    yd = ts([ydep[0]], T.ysb[:], T.py[0:8, 0:32], -1.0 if r == 3 else 0.0, None, OP.add)
     dma("y", [yd], "st", T.y[:], T.ysb[:])
     for sn in list(cnt):
         if sn != "st":

@@ -8,16 +8,19 @@ SCRATCH = {
     "syb": ("sbuf", [1, 128], H), "one": ("sbuf", [1, 128], H), "six": ("sbuf", [1, 128], H), "syc": ("sbuf", [128, 1], I),
     "evl": ("sbuf", [1, 128], H), "ramp": ("sbuf", [1, 512], H),
     "pci": ("sbuf", [128, 2], I), "pf": ("sbuf", [128, 1], F), "igf": ("sbuf", [128, 128], F),
-    "rowf": ("sbuf", [128, 128], F), "pl": ("sbuf", [128, 36], F), "plb": ("sbuf", [128, 36], F), "mg": ("sbuf", [128, 64], F),
+    "rowf": ("sbuf", [128, 128], F), "pl": ("sbuf", [128, 36], F), "plb": ("sbuf", [128, 36], F), "mg": ("sbuf", [128, 32], F),
     "ci5": ("sbuf", [128, 6], I), "cf5": ("sbuf", [128, 6], F), "cols": ("sbuf", [128, 16], F),
     "bo": ("sbuf", [128, 128], H), "tri": ("sbuf", [128, 128], H), "idn": ("sbuf", [128, 128], H), "dba": ("sbuf", [128, 128], H),
     "mask": ("sbuf", [128, 16], F), "pm": ("sbuf", [128, 16], F), "gind": ("sbuf", [128, 8], H), "thr": ("sbuf", [128, 4], F),
     "thg": ("sbuf", [128, 32], F), "tho": ("sbuf", [128, 32], F), "l32": ("sbuf", [128, 4], U),
     "ti": ("sbuf", [128, 256], I), "sel": ("sbuf", [128, 256], H), "selo": ("sbuf", [128, 256], H),
     "hi": ("sbuf", [128, 256], I), "ci": ("sbuf", [128, 256], I), "za": ("sbuf", [128, 256], H), "emf": ("sbuf", [128, 256], F),
-    "self": ("sbuf", [128, 256], F), "tq": ("sbuf", [128, 288], H), "tab": ("sbuf", [128, 544], H),
+    "nxix": ("sbuf", [128, 256], I), "emix": ("sbuf", [128, 256], I), "selx": ("sbuf", [128, 256], H),
+    "emfx": ("sbuf", [128, 256], F), "zax": ("sbuf", [128, 256], H), "selfx": ("sbuf", [128, 256], F),
+    "off": ("sbuf", [128, 1], H), "self": ("sbuf", [128, 256], F), "tq": ("sbuf", [128, 288], H), "tab": ("sbuf", [128, 544], H),
     "d16": ("sbuf", [128, 16], H), "ot": ("sbuf", [128, 32], U), "lt": ("sbuf", [128, 512], U),
-    "w": ("sbuf", [128, 512], H), "w1": ("sbuf", [128, 512], H), "e": ("sbuf", [128, 512], F), "ex": ("sbuf", [128, 512], F),
+    "w": ("sbuf", [128, 512], H), "w1": ("sbuf", [128, 512], H), "cpy": ("sbuf", [128, 512], H), "cp1": ("sbuf", [128, 512], H),
+    "e": ("sbuf", [128, 512], F), "ex": ("sbuf", [128, 512], F),
     "cp": ("sbuf", [128, 7168], H), "cpm": ("sbuf", [128, 512], H), "cpx": ("sbuf", [128, 512], H),
     "s1": ("sbuf", [128, 2], U), "zero": ("sbuf", [128, 2], U), "tt": ("sbuf", [128, 1080], U),
     "eea": ("sbuf", [128, 272], F), "eeb": ("sbuf", [128, 272], F), "pos": ("sbuf", [128, 4], F), "zed": ("sbuf", [8, 1], F),
@@ -32,19 +35,21 @@ for _q in "ab":
     SCRATCH["rc" + _q] = ("sbuf", [128, 8], F)
     SCRATCH["qi" + _q] = ("sbuf", [128, 2], I)
     SCRATCH["di" + _q] = ("sbuf", [128, 8], I)
-    SCRATCH["g4" + _q] = ("sbuf", [128, 8], H)
+    SCRATCH["cn" + _q] = ("sbuf", [128, 2], H)
     SCRATCH["gg" + _q] = ("sbuf", [128, 64], H)
     SCRATCH["ep" + _q] = ("sbuf", [128, 64], H)
 for _q in "01":
     SCRATCH["dec" + _q] = ("sbuf", [128, 34], H)
 SEMAPHORES = ["v", "s", "t", "p", "lnx", "lsy", "lsc", "lem", "st", "loc",
-              "as1", "aw1", "acpx", "aex", "arc0", "arc1", "arc2"]
+              "as1", "aw1", "acpx", "aex", "arc0", "arc1", "arc2", "anx", "aem", "asel", "acpy", "acp1"]
 OP = AluOpType
 AF = ActivationFunctionType
 SEGS = {0: [(1, "")] * 16,
-        1: [(1, "")] * 9 + [(3, "s"), (4, "v")],
-        2: [(1, "")] * 4 + [(3, "s"), (3, "v"), (3, "s"), (3, "v")],
+        1: [(1, "")] * 7 + [(5, "v"), (4, "s")],
+        2: [(1, "")] * 3 + [(3, "s"), (3, "v"), (4, "s"), (3, "v")],
         3: [(3, "s"), (3, "v"), (3, "s"), (3, "v"), (3, "s")]}
+FILL = {1: 2, 2: 14}
+OWN = [(4, 3, "s")]
 CODE = 262144.0
 
 
@@ -65,6 +70,7 @@ def rank_program(g, core, T, topo):
     seen = {}
     vec, act, mm = g.vector, g.scalar.activation, g.tensor.matmul
     long = [s for s in segments(r) if s[1] > 1]
+    single = len([s for s in SEGS[1] if s[0] == 1])
     tb = T.tq[:, 16:272]
 
     def waits(qn, deps):
@@ -102,18 +108,22 @@ def rank_program(g, core, T, topo):
                 m &= topo.mask(T.cores[src], c)
         return m
 
-    def send(deps, dsts, out, src, sn):
+    def lane(src, dst, how):
+        m = topo.mask(T.cores[src], T.cores[dst])
+        return m if how == "wide" else (m & ~fan(src) if how == "apart" else 0) or fan(src)
+
+    def send(deps, dsts, out, src, sn, how=None):
         waits("p", deps)
-        ids = []
+        lanes = {}
         for d in dsts:
             rid, pid, _ = topo.addr(T.cores[d])
-            ids.append(DstId(rid=rid, pnc=pid))
-        g.remote_dma_fused([RemoteDMATransfer(dst_ids=ids, dma_engine_mask=fan(r), remote_sem=T.sem[sn], srcs=[src],
-                                              dsts=[out for _ in ids], alu_op=0)], local_sem=T.sem.loc)
-        cnt["loc"] = cnt.get("loc", 0) + bin(fan(r)).count("1")
+            lanes[lane(r, d, how)] = lanes.get(lane(r, d, how), []) + [DstId(rid=rid, pnc=pid)]
+        g.remote_dma_fused([RemoteDMATransfer(dst_ids=lanes[m], dma_engine_mask=m, remote_sem=T.sem[sn], srcs=[src],
+                                              dsts=[out for _ in lanes[m]], alu_op=0) for m in lanes], local_sem=T.sem.loc)
+        cnt["loc"] = cnt.get("loc", 0) + sum(bin(m).count("1") for m in lanes)
 
-    def arrive(src, sn):
-        cnt[sn] = bin(fan(src)).count("1")
+    def arrive(src, sn, how=None, calls=1):
+        cnt[sn] = calls * bin(lane(src, r, how)).count("1")
         return (sn, cnt[sn])
 
     def play(fs):
@@ -176,79 +186,91 @@ def rank_program(g, core, T, topo):
     m_t0 = ts([m_ta], T.tq[:, 16:144], T.ti[:, 0:128], -256.0, None, OP.add)
     if r == 0:
         m_0 = do("t", [m_s0, m_t0], lambda: mm(T.pc[:, 0:2], T.sel[:, 0:128], T.tq[:, 16:18], True, True))
+        m_s1 = select(so, po, 1, [])
     m_tb = ts([m_ti], T.tq[:, 144:272], T.ti[:, 128:256], -256.0, None, OP.add)
-    m_s1 = select(so, po, 1, [])
+    if r > 0:
+        m_s1 = select(so, po, 1, [])
     if r > 0:
         c_idn = do("p", [c_bo], lambda: g.affine_select(T.idn[:], T.bo[:], [[1, 128]], OP.is_equal, 0.0, 0, -1))
-    c_tri = do("p", [c_bo], lambda: g.affine_select(T.tri[:], T.bo[:], [[1, 128]], OP.is_gt, 0.0, 0, -1))
-    c_pl = do("p", [], lambda: g.iota(T.pl[:], [[1, 36]], 32 * r - 3, 0, **lo))
-    do("p", [], lambda: g.iota(T.mg[:, 0:32], [[0, 4], [1, 8]], 0, 0, **lo))
-    c_mg = do("p", [], lambda: g.iota(T.mg[:, 32:64], [[1, 4], [0, 8]], -3, 0, **lo))
     K = {"pm": c_pm} if r > 0 else {}
 
     def late_constants():
+        x = do("p", [], lambda: g.iota(T.mg[:], [[2, 4], [0, 8]], -6, 0, **lo))
+        K["tri"] = do("p", [c_bo], lambda: g.affine_select(T.tri[:], T.bo[:], [[1, 128]], OP.is_gt, 0.0, 0, -1))
+        x = do("p", [x], lambda: g.affine_select(T.tho[:], T.mg[:], [[0, 4], [-16, 8]], OP.is_ge, 256.0, 0, 1))
+        do("p", [], lambda: g.iota(T.pl[:], [[2, 36]], 64 * r - 6, 0, **lo))
+        do("p", [], lambda: g.iota(T.off[:], [[0, 1]], -256, 0, **lo))
+        K["late"] = do("p", [x], lambda: g.affine_select(T.thg[:], T.tho[:], [[0, 4], [16, 8]], OP.is_ge, 256.0, 15, -1))
+
+    def digit_list():
         def a():
-            K["o"] = ts([c_mg], T.tho[:], T.mg[:, 0:32], CF[:, 0:1], 256.0, OP.not_equal, OP.mult)
             K["up"] = ts([], CO[:, 5:6], CF[:, 1:2], 8.0, None, OP.is_ge)
 
         def b():
-            ts([], T.thr[:], T.rowf[:, 0:4], -3.0, None, OP.add)
             ts([K["up"]], T.l32[:], T.rowf[:, 0:8:2], CO[:, 5:6], None, OP.add)
+        return [a, b]
 
-        def c():
-            K["late"] = tten([K["o"]], T.thg[:], T.tho[:], T.mg[:, 32:64], OP.add)
-        return [a, b, c]
 
-    def code_parts():
+    def code_window(x, EB, d_nx, d_em, d_sel):
+        nxi, emi, sel, emf, za, self_, e = [T[n + x] for n in ("nxi", "emi", "sel", "emf", "za", "self", "e")]
+        C = {("sel", 1): d_sel}
+
         def part(kind, h):
             c = slice(128 * h, 128 * h + 128)
             u = slice(256 + 128 * h, 384 + 128 * h)
 
             def f():
                 if kind == "sel":
-                    d = select(T.sel, T.px, h, [m_x])
+                    d = select(sel, T.px, h, [m_x])
                 elif kind == "em":
-                    d = ts([l_em], T.emf[:, c], T.emi[:, c], 1.0 / CODE, -4.0, OP.mult, OP.add)
+                    d = ts([d_em], emf[:, c], emi[:, c], 1.0 / CODE, -8.0, OP.mult, OP.add)
                 elif kind == "hi":
-                    d = ts([l_em], T.hi[:, c], T.emi[:, c], 18, None, OP.arith_shift_right)
+                    d = ts([d_em], T.hi[:, c], emi[:, c], 18, None, OP.arith_shift_right)
                 elif kind == "top":
-                    d = ts([], T.pb[:, c], T.nxi[:, c], 2048.0, 64.0, OP.is_lt, OP.mult)
+                    d = ts([d_nx], T.pb[:, c], nxi[:, c], 2048.0, 64.0, OP.is_lt, OP.mult)
                 elif kind == "ci":
-                    d = ts([], T.ci[:, c], T.nxi[:, c], 9, None, OP.arith_shift_right)
+                    d = ts([], T.ci[:, c], nxi[:, c], 8, 14, OP.arith_shift_right, OP.bitwise_and)
                 elif kind == "min":
-                    d = tten([K["hi", h], K["top", h]], T.pb[:, u], T.hi[:, c], T.pb[:, c], OP.min)
+                    d = tten([C["hi", h], C["top", h]], T.pb[:, u], T.hi[:, c], T.pb[:, c], OP.min)
                 else:
-                    d = tten([K["min", h], K["ci", h]], T.za[:, c], T.ci[:, c], T.pb[:, u], OP.subtract)
-                K[kind, h] = d
+                    d = tten([C["min", h], C["ci", h]], za[:, c], T.ci[:, c], T.pb[:, u], OP.subtract)
+                C[kind, h] = d
             return f
-        kinds = (["sel"] if r > 0 else []) + ["em", "hi", "top", "ci", "min", "za"]
-        return [part(kind, h) for kind in kinds for h in range(2)]
 
-    EB = (T.pew, T.pwb)
+        def wide():
+            C["self"] = do("s", [C["sel", 1]], lambda: act(self_[:], sel[:], AF.Copy))
 
-    def code_sel():
-        K["self"] = do("s", [K.get(("sel", 1), m_s1)], lambda: act(T.self[:], T.sel[:], AF.Copy))
+        def numbers():
+            for h in range(2):
+                do("t", [C["self"], C["em", 1]], lambda: mm(EB[h][:, 0:256], self_[:, 128 * h:128 * h + 128], emf[:], True, False))
 
-    def code_numbers(deps):
-        for h in range(2):
-            do("t", [K["self"], K["em", 1]] + deps, lambda: mm(EB[h][:, 0:256], T.self[:, 128 * h:128 * h + 128], T.emf[:], True, False))
+        def counts():
+            for h in range(2):
+                C["eb", h] = do("t", [C["za", 1]], lambda: mm(EB[h][:, 0:256], sel[:, 128 * h:128 * h + 128], za[:], False, True))
 
-    def code_counts():
-        for h in range(2):
-            K["eb", h] = do("t", [K["za", 1]], lambda: mm(EB[h][:, 0:256], T.sel[:, 128 * h:128 * h + 128], T.za[:], False, True))
+        def out(then=None):
+            for h in range(2):
+                c = slice(256 * h, 256 * h + 256)
+                d = do("s", [C["eb", h]], lambda: act(e[:, c], EB[h][:, 0:256], AF.Copy))
+                if then:
+                    then(c, d)
+            return d
+        kinds = ([] if d_sel else ["sel"]) + ["em", "hi", "top", "ci", "min", "za"]
+        return [part(kind, h) for kind in kinds for h in range(2)], wide, numbers, counts, out, C
 
-    def code_out():
-        for h in range(2):
-            d = do("s", [K["eb", h]], lambda: act(T.e[:, 256 * h:256 * h + 256], EB[h][:, 0:256], AF.Copy))
-        return d
+    parts, code_sel, code_numbers, code_counts, code_out, CW = code_window("", (T.pew, T.px), l_nx, l_em, None if r else m_s1)
 
-    def window():
-        wb = (T.pwa, T.pwb)
-        for h in range(2):
-            do("t", [c_ramp], lambda: mm(wb[h][:, 0:256], T.evl[:], T.ramp[:, 256 * h:256 * h + 256], True, False))
-        for h in range(2):
-            d = do("t", [m_s1 if h else m_s0, m_tb], lambda: mm(wb[h][:, 0:256], T.selo[:, 128 * h:128 * h + 128], tb, False, True))
-            d = do("s", [d], lambda: act(T.w[:, 256 * h:256 * h + 256], wb[h][:, 0:256], AF.Copy))
+    def window(to):
+        wb = (T.pwa, T.pcm, T.pwb, T.pew)
+        for x in range(4):
+            do("t", [c_ramp], lambda: mm(wb[x][:, 0:128], T.evl[:], T.ramp[:, 128 * x:128 * x + 128], True, False))
+        for x in range(4):
+            h, u = x // 2, x % 2
+            d = do("t", [m_s1 if h else m_s0, m_tb if u else m_t0], lambda: mm(
+                wb[x][:, 0:128], T.selo[:, 128 * h:128 * h + 128], T.tq[:, 16 + 128 * u:144 + 128 * u], False, True))
+            d = do("s", [d], lambda: act(T.w[:, 128 * x:128 * x + 128], wb[x][:, 0:128], AF.Copy))
+        if to is not None:
+            send([d], [to], T.w1[:], T.w[:], "aw1")
         return d
 
     def turned():
@@ -257,14 +279,17 @@ def rank_program(g, core, T, topo):
         ts([am, c_k9], T.ot[:, 0:32:2], T.py[:, 64:80], CO[:, 8:9], 16.0, OP.add, OP.mult)
         K["tab"] = ts([], T.ot[:, 1:32:2], T.py[:, 64:80], CO[:, 9:10], 16.0, OP.add, OP.mult)
 
-    def lists(seg):
-        j, n, _ = seg
-        K["lt", j] = ts([K["tab"]], T.lt[:, 32 * j:32 * (j + n - 1)], T.tab[:].indirect(T.ot[:, 2 * j:2 * (j + n - 1)]),
-                        256.0, None, OP.add)
+    def lists(segs):
+        def one(j, n):
+            def f():
+                K["lt", j] = ts([K["tab"]], T.lt[:, 32 * j:32 * (j + n - 1)],
+                                T.tab[:].indirect(T.ot[:, 2 * j:2 * (j + n - 1)]), 256.0, None, OP.add)
+            return f
+        return [one(j, n) for j, n, _ in segs]
 
     slot = [0]
 
-    def joins(seg, plus=None):
+    def joins(seg, plus=None, masked=True):
         j, n, qn = seg
         box = [T.w[:], K["w"]]
 
@@ -274,7 +299,7 @@ def rank_program(g, core, T, topo):
                 out = T.cp[:, 512 * x:512 * x + 512]
                 slot[0] += 1
                 src = box[0].indirect(T.lt[:, 32 * i:32 * i + 32])
-                keep = T.pm[:, j + n - 1:j + n] if i == (j + n - 2 if plus else j) else 1.0
+                keep = T.pm[:, j + n - 1:j + n] if masked and i == (j + n - 2 if plus else j) else 1.0
                 deps = [box[1], K["lt", j], K["pm"]]
                 if plus and i == j:
                     y, e = K["join", plus[0]]
@@ -291,29 +316,44 @@ def rank_program(g, core, T, topo):
 
     def merge_constants():
         ends = [T.pm[:, j + n - 1:j + n] for j, n, _ in long]
-        d = K["pm"]
-        while len(ends) > 2:
-            d = ts([d], CO[:, 10 + len(ends):11 + len(ends)], ends[0], ends[1], ends[2], OP.add, OP.add)
-            ends = [CO[:, 10 + len(ends):11 + len(ends)]] + ends[3:]
-        d = ts([d], CO[:, 10:11], ends[0], ends[-1], 0.0, OP.add, OP.is_equal)
-        K["dba"] = do("s", [d, c_idn], lambda: act(T.dba[:], T.idn[:], AF.Copy, scale=CO[:, 10:11]))
+
+        def three():
+            out = CO[:, 10 + len(ends):11 + len(ends)]
+            K["kb"] = ts([K.get("kb")], out, ends[0], ends[1], ends[2], OP.add, OP.add)
+            ends[0:3] = [out]
+
+        def last():
+            if len(ends) > 1:
+                d = ts([K.get("kb")], CO[:, 10:11], ends[0], ends[1], 0.0, OP.add, OP.is_equal)
+            else:
+                d = ts([K.get("kb")], CO[:, 10:11], ends[0], 0.0, None, OP.is_equal)
+            K["keep"] = d
+
+        def diagonal():
+            K["dba"] = do("s", [K["keep"], c_idn], lambda: act(T.dba[:], T.idn[:], AF.Copy, scale=CO[:, 10:11]))
+        return [three] * ((len(ends) - 1) // 2) + [last], diagonal
 
     MB = (T.pcm, T.pc)
+
+    def table(seg):
+        x = K["join", seg[0]][0]
+        return T.cp[:, 512 * x:512 * x + 512]
 
     def merge_add(lhs, src, x, deps, first=False, last=False):
         return [do("t", deps, lambda: mm(MB[h][:, 0:256], lhs[:], src[:, x + 256 * h:x + 256 * h + 256], first, last))
                 for h in range(2)]
 
     def merge(order):
-        merge_add(T.dba, T.w, 0, [K["dba"], K["w"]], True)
         for seg in order:
-            n, d = K["join", seg[0]]
-            md = merge_add(T.idn, T.cp, 512 * n, [d], False, seg == order[-1])
+            if seg is None:
+                merge_add(T.dba, T.w, 0, [K["dba"], K["w"]], seg == order[0])
+            else:
+                n, d = K["join", seg[0]]
+                md = merge_add(T.idn, T.cp, 512 * n, [d, c_idn], seg == order[0], seg == order[-1])
         return md
 
     def merge_out(md):
-        return [do("v", [md[0]], lambda: vec.tensor_copy(T.cpm[:, 0:256], MB[0][:, 0:256])),
-                do("s", [md[1]], lambda: act(T.cpm[:, 256:512], MB[1][:, 0:256], AF.Copy))]
+        return [[do("s", [md[h]], lambda: act(T.cpm[:, 256 * h:256 * h + 256], MB[h][:, 0:256], AF.Copy)) for h in range(2)][1]]
 
     def weave(*rows):
         rows = [list(x) for x in rows]
@@ -333,22 +373,29 @@ def rank_program(g, core, T, topo):
         tile, x0, d = at
         return (T.tt, col, ts([d] + deps, T.tt[:, b:b + 16], win.indirect(tile[:, x0:x0 + 1]), 256.0, None, OP.add))
 
-    def string(q, at, plain, joined, inner, hooks, start=0):
+    def plan(q, plain, joined):
+        out, segs = [], segments(q)
+        for m in range(len(segs)):
+            x = min(len(joined) - 1, len([s for s in segs[:m] if s[1] > 1]) // 2)
+            out.append(segs[m][:2] + (plain if segs[m][1] == 1 else joined[x]))
+        return out
+
+    def string(segs, at, inner, hooks, start=0):
         reads, late = {0: at}, []
-        segs = segments(q)
         for m in range(start, len(segs)):
-            j, n, _ = segs[m]
-            win, deps = plain if n == 1 else joined
+            j, n, win, deps = segs[m]
             at = gather(win, at, deps, (j - 1) % 16)
-            play(late)
-            late = []
             for i in range(j, j + n):
                 reads[i + 1] = at
-            if inner:
-                for i in range(j + (q > 1), j + n - 2):
-                    def f(i=i, win=win if q > 1 else plain[0]):
-                        reads[i + 1] = gather(win, reads[i], [], i - 1)
-                    late.append(f)
+            play(late)
+            late = []
+            steps, single = inner(j, n) if inner else ([], None)
+            for i in steps:
+                def f(i=i, single=single):
+                    reads[i + 1] = gather(single, reads[i], [], (i - 1) % 16)
+                late.append(f)
+            if j in steps:
+                late.pop(0)()
             play(hooks.get(m, []))
         return reads, at, late
 
@@ -360,10 +407,10 @@ def rank_program(g, core, T, topo):
             return ts([d, edep, c_mask], out, src, T.mask[:, j:j + 1], None, OP.mult)
         return do("s", [d, edep, c_mask], lambda: act(out, src, AF.Copy, scale=T.mask[:, j:j + 1]))
 
-    def follow(qn, reads, ewin, edep, ee, steps):
-        for j in steps:
-            last = code_at(qn, reads, j, ewin, edep, ee)
-        return last
+    def follow(reads, ewin, edep, ee, on_v):
+        steps = sorted(range(16), key=lambda j: reads[j][2][1] if j else 0)
+        return [[code_at(qn, reads, j, ewin, edep, ee) for j in part][-1]
+                for qn, part in (("s", steps[:16 - on_v]), ("v", steps[16 - on_v:])) if part]
 
     cd, gd = {}, {}
     ydep = [None, 0]
@@ -379,7 +426,7 @@ def rank_program(g, core, T, topo):
         cd[q] = do("v", last, lambda: vec.tensor_reduce(code(q), ee[:, 15:271:17], AxisListType.X, OP.add))
 
     def gates(q):
-        gd[q] = ts([cd[q], K["late"]], buf("g4", q, 4), T.thr[:], code(q), None, OP.is_le)
+        gd[q] = ts([cd[q]], buf("cn", q, 1), code(q), 0.0, 263.5, OP.min, OP.add)
 
     def spread(q):
         K["gg", q] = ts([cd[q], K["late"]], buf("gg", q, 32), T.thg[:], code(q), None, OP.is_le)
@@ -399,23 +446,29 @@ def rank_program(g, core, T, topo):
             ts([], di[:, 2:4 * n:4], qi, 12, 63, OP.arith_shift_right, OP.bitwise_and)
             K["di"] = ts([], di[:, 3:4 * n:4], qi, 18, 63, OP.arith_shift_right, OP.bitwise_and)
 
-        def used():
-            K["ep"] = tten([K["di"]] + [K["gg", q] for q in qs], ep, di[:, 0:4 * n].indirect(T.l32[:, 0:2 * n]),
-                           T["gg" + x][:, 0:32 * n], OP.mult)
-        return [whole, low, high, used]
+        def used(i):
+            def f():
+                K["ep", qs[i]] = tten([K["di"], K["gg", qs[i]]], ep[:, 32 * i:32 * i + 32],
+                                      di[:, 0:4 * n].indirect(T.l32[:, 2 * i:2 * i + 2]), T["gg" + x][:, 32 * i:32 * i + 32], OP.mult)
+            return f
+        return [whole, low, high] + [used(i) for i in range(n)]
 
-    def count(out, lhs, q, start=True, stop=True):
-        g4 = T["g4" + "ab"[q // 2]]
-        for m in range(4):
-            x = 4 * (q == 3) + m
-            d = do("t", [gd[q], c_tri], lambda: mm(out, lhs[:], g4[:, x:x + 1], start and m == 0, stop and m == 3))
-        return d
+    def begin(out, lhss, deps):
+        for lhs in lhss:
+            do("t", [K["late"]] + deps, lambda: mm(out, lhs[:], T.off[:], lhs is lhss[0], False))
+
+    def count(out, lhs, q, stop=True):
+        return do("t", [gd[q]], lambda: mm(out, lhs[:], buf("cn", q, 1), False, stop))
 
     def hot(q, deps, first):
-        K["oh", q] = ts(deps + [c_pl], T["oh%d" % q][:], (T.pl if q < 2 else T.plb)[:], first, None, OP.is_equal)
+        oh = T["oh%d" % q][:]
+        if q == 1:
+            K["oh", q] = ts(deps, oh, T.pl[:], T.dec0[:, 33:34], first, OP.subtract, OP.is_equal)
+        else:
+            K["oh", q] = ts(deps + [K["late"]], oh, (T.pl if q < 2 else T.plb)[:], first, None, OP.is_equal)
 
     def from_two(deps):
-        return ts(deps + [c_pl], T.plb[:], T.pl[:], T.dec1[:, 33:34], None, OP.subtract)
+        return ts(deps + [K["late"]], T.plb[:], T.pl[:], T.dec0[:, 33:34], T.dec1[:, 33:34], OP.subtract, OP.subtract)
 
     def add(q, src, x, deps, final=False):
         for m in range(4):
@@ -423,106 +476,126 @@ def rank_program(g, core, T, topo):
                 T.py[0:8, 0:32], src[:, x + 8 * m:x + 8 * m + 8], T["oh%d" % q][:, 3 - m:35 - m], ydep[1] == 0, final and m == 3))
             ydep[1] += 1
 
-    def finish(q, base, bdep):
+    def finish(q):
         dec = T["dec%d" % q]
-        D = digits([q], dec[:, 0:32])
+        D = digits([q], dec)
 
         def a():
             D[0]()
             gates(q)
-            count(T.pb[:, 0:1], T.tri, q)
-            K["sum"] = count(T.pb[:, 1:2], T.bo, q)
+            for x in range(2):
+                begin(T.pb[:, x:x + 1], [(T.tri, T.bo)[x]], [cd[q]])
+                K["sum"] = count(T.pb[:, x:x + 1], (T.tri, T.bo)[x], q)
             spread(q)
 
         def b():
-            K["pos"] = ts([K["sum"], bdep], dec[:, 32:34], T.pb[:, 0:2], base, None, OP.add)
-        return [a] + D[1:] + [b]
+            K["pos"] = do("v", [K["sum"]], lambda: vec.tensor_copy(dec[:, 32:34], T.pb[:, 0:2]))
+        return [a] + D[1:3] + [b] + D[3:]
 
     if r == 0:
-        a = do("t", [m_tb], lambda: mm(T.pwa[:, 0:256], T.sel[:, 0:128], tb, True, True))
-        b = do("t", [m_s1], lambda: mm(T.pwb[:, 0:256], T.sel[:, 128:256], tb, True, True))
         at = (T.s1, 0, ts([m_0], T.s1[:], T.pc[:, 0:2], 256.0, None, OP.add))
-        wdep = [do("s", [a], lambda: act(T.w[:, 0:256], T.pwa[:, 0:256], AF.Copy)),
-                do("v", [b], lambda: vec.tensor_copy(T.w[:, 256:512], T.pwb[:, 0:256]))]
+        wdep = [None, None]
+        for u in range(2):
+            for h in range(2):
+                bank, out = (T.pwa, T.pwb, T.pcm, T.py)[2 * u + h][:, 128:256], T.w[:, 256 * h + 128 * u:256 * h + 128 * u + 128]
+                d = do("t", [m_s1 if h else None, m_tb if u else None], lambda: mm(
+                    bank, T.sel[:, 128 * h:128 * h + 128], T.tq[:, 16 + 128 * u:144 + 128 * u], True, True))
+                wdep[h] = do("v", [d], lambda: vec.tensor_copy(out, bank)) if h else do("s", [d], lambda: act(out, bank, AF.Copy))
+        late_constants()
         code_sel()
-        parts = code_parts()
-        hooks = {n + 2: [parts[n]] for n in range(len(parts))}
-        hooks[3].append(lambda: code_numbers(wdep))
-        hooks[13].append(code_counts)
-        reads, at1, _ = string(0, at, (T.w[:], wdep), None, False, hooks, 1)
+        parts3, sel3, numbers3, counts3, out3, _ = code_window(
+            "x", (T.pwa, T.pwb), arrive(3, "anx"), arrive(3, "aem"), arrive(3, "asel"))
+        dl = digit_list()
+        fill = dl[:1] + parts + dl[1:] + parts3
+        hooks = {n + 1: [fill[n]] for n in range(15)}
+        hooks[3].append(code_numbers)
+        hooks[13] += [code_counts, sel3]
+        reads, at1, _ = string(plan(0, (T.w[:], wdep), [None]), at, None, hooks, 1)
         reads[0], reads[1] = (T.zero, 0, c_zero), at
         send([at1[2]], [1], T.s1[:], T.tt[:, at1[1]:at1[1] + 2], "as1")
-        last = follow("s", reads, T.e, code_out(), T.eea, range(16))
-        lc = late_constants()
-        hooks = {n: [lc[n]] for n in range(3)}
-        at = string(1, at1, (T.w1[:], [arrive(1, "aw1")]), (T.cpx[:], [arrive(1, "acpx")]), False, hooks)[1]
-        send([at[2]], [3, 2], T.s1[:], T.tt[:, at[1]:at[1] + 2], "as1")
-        total(0, T.eea, [last])
-        play(finish(0, 0.0, None))
-        send([K["pos"]], [1], T.dec0[:], T.dec0[:], "arc0")
+        last = follow(reads, T.e, code_out(), T.eea, 0)
+        hooks = {n: [fill[15 + n]] for n in range(single)}
+        hooks[0].append(numbers3)
+        at = string(plan(1, (T.w1[:], [arrive(1, "aw1")]), [(None, None)])[:single], at1, None, hooks)[1]
+        send([at[2]], [2, 3], T.s1[:], T.tt[:, at[1]:at[1] + 2], "as1")
+        play(fill[15 + single:] + [counts3])
+        out3(lambda c, d: send([d], [2], T.ex[:, c], T.ex[:, c], "aex", "wide"))
+        total(0, T.eea, last)
+        play(finish(0))
+        send([K["ep", 0]], [2, 3, 1], T.dec0[:], T.dec0[:], "arc0", "apart")
         hot(0, [K["pos"]], T.dec0[:, 32:33])
         add(0, T.dec0, 0, [])
         hot(1, [arrive(1, "arc1")], T.dec1[:, 32:33])
         add(1, T.dec1, 0, [], True)
     else:
-        K["w"] = window()
-        parts = code_parts()
+        mc, diagonal = merge_constants()
+        if r == 3:
+            send([l_em], [0], T.emix[:], T.emi[:], "aem")
+            send([l_nx], [0], T.nxix[:], T.nxi[:], "anx")
         to = {1: 0, 2: 3, 3: 2}[r]
-        if SEGS[r][0][0] == 1:
-            send([K["w"]], [to], T.w1[:], T.w[:], "aw1")
-        on = {qn: [s for s in long if s[2] == qn] for qn in "sv"}
-        numbers = [code_sel, lambda: code_numbers([K["w"]])]
-        if r == 3:
-            play(parts[:2] + numbers[:1])
-        turned()
-        for s in on["s"]:
-            lists(s)
-        if r == 3:
-            play(parts[2:4] + numbers[1:])
-        for s in on["v"]:
-            lists(s)
-        js = weave(*[joins(s) for s in on["s"]])
-        jv = weave(*[joins(s, p) for s, p in zip(on["v"], on["s"])])
-        order = on["v"][:1] + on["s"][len(on["v"]):] + on["v"][1:]
-        lc = late_constants()
-        if r == 1:
-            play(js + weave(jv[:-1], parts[0:4:2], parts[1:4:2]) + numbers + jv[-1:])
-            cmd = [K["join", on["v"][0][0]][1]]
-            send(cmd, [to], T.cpx[:], T.cpm[:], "acpx")
-            play(parts[4:] + [code_counts] + lc)
-            ed = code_out()
+        K["w"] = window(to if r < 3 else None)
         if r == 2:
-            play(js[:1] + [merge_constants] + js[1:] + jv[:2] + parts[:4] + numbers[:1] + jv[2:])
-            md = merge(order)
-            play(parts[4:7])
-            cmd = merge_out(md)
-            send(cmd, [to], T.cpx[:], T.cpm[:], "acpx")
-            play(numbers[1:] + parts[7:] + [code_counts] + lc)
+            late_constants()
+        on = {qn: [s for s in long if s[2] == qn] for qn in "sv"}
+        S, V = on["s"], on["v"]
+        turned()
+        js = weave(*[joins(s) for s in S])
+        if r == 1:
+            jv = joins(V[0], S[0])
+            n = 4
+            play(parts[:1] + lists(S + V) + js + weave(jv[:-1], parts[1:n]) + [code_sel, code_numbers] + jv[-1:])
+            cmd = [K["join", V[0][0]][1]]
+            send(cmd, [2, 3], T.cp1[:], T.cpm[:], "acp1", "apart")
+            js = weave(*[joins(s, None, False) for s in OWN])
+            play(lists(OWN) + js[:FILL[1]] + parts[n:] + [code_counts])
             ed = code_out()
+            play(js[FILL[1]:])
+        if r == 2:
+            ja, jb = joins(V[0], S[0]), joins(V[1], S[1])
+            play(parts[:1] + lists(S) + js[:1] + parts[1:2] + [code_sel] + weave(parts[2:4] + lists(V), mc) + [code_numbers] + js[1:]
+                 + [diagonal] + weave(ja[:-1], jb[:-1]) + parts[4:FILL[r]])
+            for i in range(2):
+                (ja, jb)[i][-1]()
+                send([K["join", V[i][0]][1]], [to], (T.cpx, T.cpy)[i][:], table(V[i]), ("acpx", "acpy")[i])
+            md = merge(V[:1] + [None] + V[1:])
+            play(parts[FILL[r]:] + [code_counts])
         if r == 3:
-            play(js[:1] + [merge_constants] + js[1:4] + parts[4:] + [code_counts])
-            ed = code_out()
-            send([ed], [to], T.ex[:], T.e[:], "aex")
-            play(js[4:] + jv)
-            md = merge(order)
-            play(lc)
+            jv = weave(joins(V[0], S[0]), joins(V[1], S[1]))
+            js, je = weave(joins(S[0]), joins(S[1])), joins(S[2])
+            play(parts[:1] + lists(S[:2]) + js[:1] + parts[1:2])
+            send([CW["sel", 1]], [0], T.selx[:], T.sel[:], "asel")
+            play([code_sel] + weave(parts[2:4] + lists(V), mc) + [code_numbers] + js[1:] + jv[:1]
+                 + lists(S[2:]) + je[:1] + [diagonal] + je[1:] + jv[1:])
+            md = merge(V[:1] + [None] + V[1:] + S[2:])
+            play(parts[4:] + [code_counts])
+        if r != 2:
+            late_constants()
+        dl = digit_list()
+        play(dl[:1])
+        if r > 1:
             cmd = merge_out(md)
+        if r == 3:
             send(cmd, [to], T.cpx[:], T.cpm[:], "acpx")
+        if r > 1:
+            ed = code_out()
+        play(dl[1:])
+        begin(T.pwa[:, 0:1], [T.tri], [])
     if r == 1:
-        reads, _, late = string(1, (T.s1, 0, arrive(0, "as1")), (T.w[:], []), (T.cpm[:], cmd), True, {})
+        segs = plan(1, (T.w[:], []), [(T.cpm[:], cmd)])
+        if OWN:
+            segs[OWN[0][0]:single] = [(s[0], s[1], table(s), [K["join", s[0]][1]]) for s in OWN]
+        reads, _, late = string(segs, (T.s1, 0, arrive(0, "as1")),
+                                lambda j, n: (range(j, j + n - (1 if j < single else 2)), T.w[:]), {})
         play(late)
-        last = follow("s", reads, T.e, ed, T.eea, range(13))
-        last_v = follow("v", reads, T.e, ed, T.eea, (15, 13, 14))
-        total(1, T.eea, [last, last_v])
-        a0 = arrive(0, "arc0")
-        play(finish(1, T.dec0[:, 33:34], a0))
-        send([K["pos"]], [2, 3, 0], T.dec1[:], T.dec1[:], "arc1")
+        total(1, T.eea, follow(reads, T.e, ed, T.eea, 4))
+        play(finish(1))
+        send([K["ep", 1]], [2, 3, 0], T.dec1[:], T.dec1[:], "arc1", "apart")
         for q in range(2):
-            hot(q, [K["pos"]], T["dec%d" % q][:, 32:33])
+            hot(q, [K["pos"], arrive(0, "arc0")], T["dec%d" % q][:, 32:33])
             add(q, T["dec%d" % q], 0, [])
         base = from_two([])
         cd[2] = arrive(2, "arc2")
-        D = digits([2], T.epb[:, 0:32])
+        D = digits([2], T.epb)
         D[0]()
         gates(2)
         c2 = count(T.pwa[:, 0:1], T.tri, 2)
@@ -531,57 +604,68 @@ def rank_program(g, core, T, topo):
         hot(2, [c2, base], T.pwa[:, 0:1])
         add(2, T.epb, 0, [], True)
     if r > 1:
-        own, other = (T.cpm[:], cmd), (T.cpx[:], [arrive(5 - r, "acpx")])
+        begin(T.pb[:, 0:1], [T.tri, T.bo], [])
+        own, other = [(T.cpm[:], cmd)], [(T.cpx[:], [arrive(5 - r, "acpx")])]
+        if r == 3:
+            other.append((T.cpy[:], [arrive(2, "acpy")]))
         plain = (T.w[:], []) if r == 2 else (T.w1[:], [arrive(2, "aw1")])
-        reads2, at, late = string(2, (T.s1, 0, arrive(0, "as1")), plain, own if r == 2 else other, r == 2, {})
-        a1 = arrive(1, "arc1")
+        rest = plan(1, (None, None), [(T.cp1[:], [arrive(1, "acp1", "apart")])])[single:]
+        at = string(rest, (T.s1, 0, arrive(0, "as1")), None, {})[1]
+        reads2, at, late = string(plan(2, plain, own if r == 2 else other), at,
+                                  (lambda j, n: (range(j + 1, j + n - 2), T.cpm[:])) if r == 2 else None, {})
+        a0, a1 = arrive(0, "arc0", "apart"), arrive(1, "arc1", "apart")
 
-        def counts2(start):
+        def counts2():
             gates(2)
             K["c2"] = count(T.pwa[:, 0:1], T.tri, 2)
-            K["c3"] = count(T.pb[:, 0:1], T.bo, 2, start, not start)
+            count(T.pb[:, 0:1], T.bo, 2, False)
             spread(2)
 
         def t2():
-            total(2, T.eea, [K["l2"], K["v2"]])
+            total(2, T.eea, K["l2"])
             send([cd[2]], [3, 1], code(2), code(2), "arc2")
-
-        def v2():
-            K["l2"] = follow("s", reads2, T.e, ed, T.eea, range(14))
-            K["v2"] = follow("v", reads2, T.e, ed, T.eea, (14, 15))
         if r == 2:
-            e3, e3d = T.ex, arrive(3, "aex")
-            hooks = {0: late + [v2], 1: [t2], 2: [lambda: counts2(True)]}
+            K["l2"] = follow(reads2, T.e, ed, T.eea, 2)
+            e3, e3d = T.ex, arrive(0, "aex", "wide", 2)
+            hooks = {0: [t2], 1: [counts2]}
         else:
             e3, e3d = T.e, ed
             hooks = {}
-        reads3, _, late = string(3, at, None, other if r == 2 else own, True, hooks)
-        on_s = 11 if r == 2 else 13
-        last = follow("s", reads3, e3, e3d, T.eeb, range(on_s))
-        last_v = follow("v", reads3, e3, e3d, T.eeb, range(on_s, 16))
-        total(3, T.eeb, [last, last_v])
-        D = digits([2, 3], T.epb[:])
-        gates(3)
-        K["c3"] = count(T.pb[:, 0:1], T.tri, 3, r == 3, r == 2)
+        reads3, _, late = string(plan(3, (other if r == 2 else own)[0], other if r == 2 else own), at,
+                                 lambda j, n: (range(j + 1, j + n - 2), (T.cpx if r == 2 else T.cpm)[:]), hooks)
+        last = follow(reads3, e3, e3d, T.eeb, 3)
         if r == 3:
             cd[2] = arrive(2, "arc2")
-            counts2(False)
+            counts2()
+        total(3, T.eeb, last)
+        D = digits([2, 3], T.epb)
         D[0]()
+        gates(3)
+        K["c3"] = count(T.pb[:, 0:1], T.tri, 3)
+        if r == 3:
+            Z, groups = T.pew[0:8, 0:1], T.bo[:, 0:128:16]
+            for q in (2, 3):
+                do("t", [], lambda: mm(Z, groups, T.off[:], q == 2, False))
+                do("t", [], lambda: mm(Z, groups, buf("cn", q, 1), False, False))
+            do("t", [a0], lambda: mm(Z, T.idn[:, 0:128:16], T.dec0[:, 33:34], False, False))
+            zd = do("t", [a1], lambda: mm(Z, T.idn[:, 0:128:16], T.dec1[:, 33:34], False, True))
         spread(3)
-        base = from_two([a1])
+        play(D[1:3])
+        base = from_two([a0, a1])
         if r == 2:
             hot(1, [], T.dec1[:, 32:33])
             add(1, T.dec1, 0, [])
-        play(D[1:3])
-        hot(2, [K["c2"], base], T.pwa[:, 0:1])
-        hot(3, [K["c3"]], T.pb[:, 0:1])
-        if r == 3:
-            add(2, T.ggb, 0, [])
-            add(3, T.ggb, 32, [])
         D[3]()
-        add(2, T.epb, 0, [K["ep"]])
+        hot(2, [K["c2"], base], T.pwa[:, 0:1])
+        add(2, T.epb, 0, [])
+        D[4]()
+        hot(3, [K["c3"]], T.pb[:, 0:1])
         add(3, T.epb, 32, [], True)
-    yd = ts([ydep[0]], T.ysb[:], T.py[0:8, 0:32], -1.0 if r == 3 else 0.0, None, OP.add)
+    if r == 3:
+        nd = ts([zd], T.neg[:], T.pl[0:8, 3:35], Z, -1.0, OP.is_ge, OP.mult)
+        yd = tten([ydep[0], nd], T.ysb[:], T.py[0:8, 0:32], T.neg[:], OP.add)
+    else:
+        yd = do("v", [ydep[0]], lambda: vec.tensor_copy(T.ysb[:], T.py[0:8, 0:32]))
     dma("y", [yd], "st", T.y[:], T.ysb[:])
     for sn in list(cnt):
         if sn != "st":

@@ -11,12 +11,13 @@ SCRATCH = {
     "rowf": ("sbuf", [128, 128], F), "pl": ("sbuf", [128, 36], F), "plb": ("sbuf", [128, 36], F), "mg": ("sbuf", [128, 32], F),
     "ci5": ("sbuf", [128, 6], I), "cf5": ("sbuf", [128, 6], F), "cols": ("sbuf", [128, 16], F),
     "bo": ("sbuf", [128, 128], H), "tri": ("sbuf", [128, 128], H), "idn": ("sbuf", [128, 128], H), "dba": ("sbuf", [128, 128], H),
-    "mask": ("sbuf", [128, 16], F), "pm": ("sbuf", [128, 16], F), "gind": ("sbuf", [128, 8], H), "thr": ("sbuf", [128, 4], F),
-    "thg": ("sbuf", [128, 32], F), "tho": ("sbuf", [128, 32], F), "l32": ("sbuf", [128, 4], U),
+    "mask": ("sbuf", [128, 16], F), "pm": ("sbuf", [128, 16], F), "far": ("sbuf", [128, 16], F),
+    "far3": ("sbuf", [128, 64], F), "ee2": ("sbuf", [128, 33], F), "ee3": ("sbuf", [128, 33], F),
+    "thg": ("sbuf", [128, 32], F), "tho": ("sbuf", [128, 32], F), "l32": ("sbuf", [128, 6], U),
     "ti": ("sbuf", [128, 256], I), "sel": ("sbuf", [128, 256], H), "selo": ("sbuf", [128, 256], H),
     "hi": ("sbuf", [128, 256], I), "ci": ("sbuf", [128, 256], I), "za": ("sbuf", [128, 256], H), "emf": ("sbuf", [128, 256], F),
     "nxix": ("sbuf", [128, 256], I), "emix": ("sbuf", [128, 256], I), "selx": ("sbuf", [128, 256], H),
-    "emfx": ("sbuf", [128, 256], F), "zax": ("sbuf", [128, 256], H), "selfx": ("sbuf", [128, 256], F),
+    "hix": ("sbuf", [128, 256], I), "cix": ("sbuf", [128, 256], I), "emfx": ("sbuf", [128, 256], F), "zax": ("sbuf", [128, 256], H), "selfx": ("sbuf", [128, 256], F),
     "off": ("sbuf", [128, 1], H), "self": ("sbuf", [128, 256], F), "tq": ("sbuf", [128, 288], H), "tab": ("sbuf", [128, 544], H),
     "d16": ("sbuf", [128, 16], H), "ot": ("sbuf", [128, 32], U), "lt": ("sbuf", [128, 512], U),
     "w": ("sbuf", [128, 512], H), "w1": ("sbuf", [128, 512], H), "cpy": ("sbuf", [128, 512], H), "cp1": ("sbuf", [128, 512], H),
@@ -32,24 +33,25 @@ SCRATCH = {
 for _q in range(4):
     SCRATCH["oh%d" % _q] = ("sbuf", [128, 36], H)
 for _q in "ab":
-    SCRATCH["rc" + _q] = ("sbuf", [128, 8], F)
-    SCRATCH["qi" + _q] = ("sbuf", [128, 2], I)
-    SCRATCH["di" + _q] = ("sbuf", [128, 8], I)
-    SCRATCH["cn" + _q] = ("sbuf", [128, 2], H)
-    SCRATCH["gg" + _q] = ("sbuf", [128, 64], H)
-    SCRATCH["ep" + _q] = ("sbuf", [128, 64], H)
-for _q in "01":
-    SCRATCH["dec" + _q] = ("sbuf", [128, 34], H)
+    SCRATCH["rc" + _q] = ("sbuf", [128, 12], F)
+    SCRATCH["qi" + _q] = ("sbuf", [128, 3], I)
+    SCRATCH["di" + _q] = ("sbuf", [128, 12], I)
+    SCRATCH["cn" + _q] = ("sbuf", [128, 3], H)
+    SCRATCH["gg" + _q] = ("sbuf", [128, 96], H)
+    SCRATCH["ep" + _q] = ("sbuf", [128, 96], H)
+SCRATCH["ep1"] = ("sbuf", [128, 32], H)
+SCRATCH["q2"] = ("sbuf", [128, 1], I)
 SEMAPHORES = ["v", "s", "t", "p", "lnx", "lsy", "lsc", "lem", "st", "loc",
-              "as1", "aw1", "acpx", "aex", "arc0", "arc1", "arc2", "anx", "aem", "asel", "acpy", "acp1"]
+              "as1", "aw1", "acpx", "aex", "arc0", "arc1", "arc2", "anx", "aem", "asel", "acpy", "acp1", "aep1"]
 OP = AluOpType
 AF = ActivationFunctionType
 SEGS = {0: [(1, "")] * 16,
         1: [(1, "")] * 7 + [(5, "v"), (4, "s")],
-        2: [(1, "")] * 3 + [(3, "s"), (3, "v"), (4, "s"), (3, "v")],
+        2: [(1, "")] * 2 + [(4, "s"), (4, "v"), (3, "s"), (3, "v")],
         3: [(3, "s"), (3, "v"), (3, "s"), (3, "v"), (3, "s")]}
-FILL = {1: 2, 2: 14}
+FILL = {1: 2, 2: 8, 4: 14, ("v", 2): 1, ("v", 3): 0}
 OWN = [(4, 3, "s")]
+LAST = (13, 3, "s")
 CODE = 262144.0
 
 
@@ -132,19 +134,21 @@ def rank_program(g, core, T, topo):
 
     l_nx = dma("y", [], "lnx", T.nxi[:], T.nx[:])
     l_sy = dma("s", [], "lsy", T.syr[:], T.sy[:])
-    if r > 0:
-        l_sc = dma("s", [], "lsc", T.syc[:], T.sy[:])
+    l_sc = dma("s", [], "lsc", T.syc[:], T.sy[:])
     l_em = dma("y", [], "lem", T.emi[:], T.em[:])
 
     lo = {"allow_small_or_imprecise_dtypes": True}
     c_p = do("p", [], lambda: g.iota(T.pci[:, 0:1], [[0, 1]], 0, 1))
     c_ig = do("p", [], lambda: g.iota(T.igf[:], [[1, 8], [0, 16]], 0, 0, **lo))
-    if r > 0:
-        c_17 = do("p", [], lambda: g.iota(T.pci[:, 1:2], [[0, 1]], 0, 17))
+    c_17 = do("p", [], lambda: g.iota(T.pci[:, 1:2], [[0, 1]], 0, 17))
     c_row = do("p", [], lambda: g.iota(T.rowf[:], [[1, 128]], 0, 0, **lo))
     if r > 0:
-        c_ramp = do("p", [], lambda: g.iota(T.ramp[:], [[1, 512]], -256, 0, **lo))
+        c_ramp = [do("s", [c_row], lambda: act(T.ramp[:, 128 * x:128 * x + 128], T.rowf[0:1, :], AF.Identity, bias=128.0 * x - 256))
+                  for x in range(4)]
         x = do("v", [], lambda: vec.memset(T.evl[:], 0.0))
+    do("v", [], lambda: vec.memset(T.off[:], -256 * CODE))
+    if r > 1:
+        c_far3 = do("v", [], lambda: vec.memset(T.far3[:], -256 * CODE))
     c_six = do("v", [], lambda: vec.memset(T.six[:], 64.0))
     P1, CI, CF, CO = T.pci[:, 0:1], T.ci5, T.cf5, T.cols
     ts([c_p], CI[:, 0:1], P1, 4, None, OP.arith_shift_right)
@@ -155,64 +159,88 @@ def rank_program(g, core, T, topo):
         for j, n, _ in long:
             c_evl = do("v", [x], lambda: vec.memset(T.evl[:, j + n - 2:128:16], 1.0))
     c_cf = do("v", [y], lambda: vec.tensor_copy(CF[:, 0:2], CI[:, 0:2]))
-    if r > 0:
-        ne = ts([c_17], CI[:, 2:3], T.pci[:, 1:2], 4, 1, OP.arith_shift_right, OP.bitwise_and)
-        do("v", [], lambda: vec.memset(T.tq[:, 0:16], 0.0))
+    ne = ts([c_17], CI[:, 2:3], T.pci[:, 1:2], 4, 1, OP.arith_shift_right, OP.bitwise_and)
+    do("v", [], lambda: vec.memset(T.tq[:, 0:16], 0.0))
     c_bo = ts([c_cf, c_ig], T.bo[:], T.igf[:], CF[:, 0:1], None, OP.is_equal)
-    if r > 0:
-        c_k8 = ts([ne], CO[:, 8:9], CI[:, 2:3], 17.0, CF[:, 1:2], OP.mult, OP.add)
-        do("v", [], lambda: vec.memset(T.tq[:, 272:288], 0.0))
     m_sy = ts([l_sy], T.syb[:], T.syr[:], 1.0 / 32, -0.25, OP.mult, OP.add)
+    c_k8 = ts([ne], CO[:, 8:9], CI[:, 2:3], 17.0, CF[:, 1:2], OP.mult, OP.add)
+    do("v", [], lambda: vec.memset(T.tq[:, 272:288], 0.0))
     c_mask = ts([c_row], T.mask[:], T.rowf[:, 0:16], CF[:, 1:2], None, OP.is_equal)
     if r > 0:
         do("t", [c_bo], lambda: mm(T.pc[:, 0:128], T.bo[:], T.bo[:], True, False))
         do("t", [c_evl, c_six], lambda: mm(T.pc[:, 0:128], T.six[:], T.evl[:], False, False))
         m_o = do("t", [m_sy], lambda: mm(T.pc[:, 0:128], T.six[:], T.syb[:], False, True))
-        sf = do("v", [l_sc], lambda: vec.tensor_copy(CO[:, 3:4], T.syc[:]))
-        c_k9 = ts([c_k8], CO[:, 9:10], CO[:, 8:9], 1.0 / 16, None, OP.add)
-        c_pm = tten([c_mask], T.pm[:, 1:16], T.mask[:, 1:16], T.mask[:, 0:15], OP.add)
-    do("t", [c_bo], lambda: mm(T.px[:, 0:128], T.bo[:], T.bo[:], True, False))
-    m_x = do("t", [m_sy, c_six], lambda: mm(T.px[:, 0:128], T.six[:], T.syb[:], False, True))
+        WB = (T.pwa, T.pwb, T.pcm, T.pew)
+        for x in range(4):
+            do("t", [c_ramp[x]], lambda: mm(WB[x][:, 0:128], T.evl[:], T.ramp[:, 128 * x:128 * x + 128], True, False))
+    K = {"pm": None}
+
+    def symbols():
+        do("t", [c_bo], lambda: mm(T.px[:, 0:128], T.bo[:], T.bo[:], True, False))
+        K["x"] = do("t", [m_sy, c_six], lambda: mm(T.px[:, 0:128], T.six[:], T.syb[:], False, True))
+
+    def columns():
+        K["sf"] = do("v", [l_sc], lambda: vec.tensor_copy(CO[:, 3:4], T.syc[:]))
+        K["k9"] = ts([c_k8], CO[:, 9:10], CO[:, 8:9], 1.0 / 16, None, OP.add)
+    if r == 0:
+        symbols()
     m_ta = ts([l_nx], T.ti[:, 0:128], T.nxi[:, 0:128], 511, None, OP.bitwise_and)
-    if r > 0:
-        d16 = ts([sf, c_mask], T.d16[:], T.mask[:], CO[:, 3:4], 0.125, OP.mult, OP.mult)
-        am = do("t", [d16], lambda: mm(T.py[:, 64:80], T.bo[:], T.d16[:], True, True))
     m_ti = ts([], T.ti[:, 128:256], T.nxi[:, 128:256], 511, None, OP.bitwise_and)
+    if r > 0:
+        columns()
+    am = T.py[:, 64:80] if r else T.pew[:, 304:320]
 
     def select(out, X, h, deps):
         return ts(deps, out[:, 128 * h:128 * h + 128], X[:, 0:128], float(h), CF[:, 1:2], OP.add, OP.is_equal)
-    so, po, mo = (T.selo, T.pc, m_o) if r > 0 else (T.sel, T.px, m_x)
+
+    def own_symbol():
+        K["d16"] = ts([K["sf"], c_mask], T.d16[:], T.mask[:], CO[:, 3:4], 0.125, OP.mult, OP.mult)
+
+    def group_symbols():
+        K["am"] = do("t", [K["d16"]], lambda: mm(am, T.bo[:], T.d16[:], True, True))
+    so, po, mo = (T.selo, T.pc, m_o) if r > 0 else (T.sel, T.px, K["x"])
     m_s0 = select(so, po, 0, [mo])
+    if r > 0:
+        own_symbol()
+        group_symbols()
     m_t0 = ts([m_ta], T.tq[:, 16:144], T.ti[:, 0:128], -256.0, None, OP.add)
-    if r == 0:
-        m_0 = do("t", [m_s0, m_t0], lambda: mm(T.pc[:, 0:2], T.sel[:, 0:128], T.tq[:, 16:18], True, True))
-        m_s1 = select(so, po, 1, [])
     m_tb = ts([m_ti], T.tq[:, 144:272], T.ti[:, 128:256], -256.0, None, OP.add)
+    m_s1 = select(so, po, 1, [])
+    turn = [lambda: do("v", [m_tb], lambda: vec.transpose(T.tab[:, 0:256], T.tq[:, 16:272])),
+            lambda: do("v", [], lambda: vec.transpose(T.tab[:, 256:544], T.tq[:, 0:288])),
+            lambda: ts([K["am"], K["k9"]], T.ot[:, 0:32:2], am, CO[:, 8:9], 16.0, OP.add, OP.mult),
+            lambda: K.update(tab=ts([], T.ot[:, 1:32:2], am, CO[:, 9:10], 16.0, OP.add, OP.mult))]
     if r > 0:
-        m_s1 = select(so, po, 1, [])
-    if r > 0:
-        c_idn = do("p", [c_bo], lambda: g.affine_select(T.idn[:], T.bo[:], [[1, 128]], OP.is_equal, 0.0, 0, -1))
-    K = {"pm": c_pm} if r > 0 else {}
+        turn.append(lambda: K.update(pm=tten([c_mask], T.pm[:, 1:16], T.mask[:, 1:16], T.mask[:, 0:15], OP.add)))
+    else:
+        columns()
+        turn[0]()
+        own_symbol()
+
+    def identity():
+        K["idn"] = do("p", [c_bo], lambda: g.affine_select(T.idn[:], T.bo[:], [[1, 128]], OP.is_equal, 0.0, 0, -1))
 
     def late_constants():
-        x = do("p", [], lambda: g.iota(T.mg[:], [[2, 4], [0, 8]], -6, 0, **lo))
+        x = do("p", [], lambda: g.iota(T.mg[:], [[4, 4], [0, 8]], -13, 0, **lo))
         K["tri"] = do("p", [c_bo], lambda: g.affine_select(T.tri[:], T.bo[:], [[1, 128]], OP.is_gt, 0.0, 0, -1))
         x = do("p", [x], lambda: g.affine_select(T.tho[:], T.mg[:], [[0, 4], [-16, 8]], OP.is_ge, 256.0, 0, 1))
-        do("p", [], lambda: g.iota(T.pl[:], [[2, 36]], 64 * r - 6, 0, **lo))
-        do("p", [], lambda: g.iota(T.off[:], [[0, 1]], -256, 0, **lo))
+        K["pl"] = do("p", [], lambda: g.iota(T.plb[:], [[2, 36]], 64 * r - 6, 0, **lo))
         K["late"] = do("p", [x], lambda: g.affine_select(T.thg[:], T.tho[:], [[0, 4], [16, 8]], OP.is_ge, 256.0, 15, -1))
 
     def digit_list():
         def a():
             K["up"] = ts([], CO[:, 5:6], CF[:, 1:2], 8.0, None, OP.is_ge)
+            K["far"] = ts([c_mask], T.far[:], T.mask[:], -1.0, 256 * CODE, OP.add, OP.mult)
 
         def b():
-            ts([K["up"]], T.l32[:], T.rowf[:, 0:8:2], CO[:, 5:6], None, OP.add)
+            ts([K["up"]], T.l32[:], T.rowf[:, 0:12:2], CO[:, 5:6], None, OP.add)
+            ts([K["pl"]], T.pl[:], T.plb[:], CODE, None, OP.mult)
         return [a, b]
 
 
     def code_window(x, EB, d_nx, d_em, d_sel):
-        nxi, emi, sel, emf, za, self_, e = [T[n + x] for n in ("nxi", "emi", "sel", "emf", "za", "self", "e")]
+        nxi, emi, sel, emf, za, self_, e, hi, ci = [T[n + x] for n in ("nxi", "emi", "sel", "emf", "za", "self", "e", "hi", "ci")]
+        pb = T.pc if x else T.pb
         C = {("sel", 1): d_sel}
 
         def part(kind, h):
@@ -221,37 +249,40 @@ def rank_program(g, core, T, topo):
 
             def f():
                 if kind == "sel":
-                    d = select(sel, T.px, h, [m_x])
+                    d = select(sel, T.px, h, [K["x"]])
                 elif kind == "em":
                     d = ts([d_em], emf[:, c], emi[:, c], 1.0 / CODE, -8.0, OP.mult, OP.add)
                 elif kind == "hi":
-                    d = ts([d_em], T.hi[:, c], emi[:, c], 18, None, OP.arith_shift_right)
+                    d = ts([d_em], hi[:, c], emi[:, c], 18, None, OP.arith_shift_right)
                 elif kind == "top":
-                    d = ts([d_nx], T.pb[:, c], nxi[:, c], 2048.0, 64.0, OP.is_lt, OP.mult)
+                    d = ts([d_nx], pb[:, c], nxi[:, c], 2048.0, 64.0, OP.is_lt, OP.mult)
                 elif kind == "ci":
-                    d = ts([], T.ci[:, c], nxi[:, c], 8, 14, OP.arith_shift_right, OP.bitwise_and)
+                    d = ts([d_nx], ci[:, c], nxi[:, c], 8, 14, OP.arith_shift_right, OP.bitwise_and)
                 elif kind == "min":
-                    d = tten([C["hi", h], C["top", h]], T.pb[:, u], T.hi[:, c], T.pb[:, c], OP.min)
+                    d = tten([C["hi", h], C["top", h]], pb[:, u], hi[:, c], pb[:, c], OP.min)
                 else:
-                    d = tten([C["min", h], C["ci", h]], za[:, c], T.ci[:, c], T.pb[:, u], OP.subtract)
+                    d = tten([C["min", h], C["ci", h]], za[:, c], ci[:, c], pb[:, u], OP.subtract)
                 C[kind, h] = d
             return f
 
         def wide():
             C["self"] = do("s", [C["sel", 1]], lambda: act(self_[:], sel[:], AF.Copy))
 
-        def numbers():
-            for h in range(2):
+        def numbers(hs=(0, 1)):
+            for h in hs:
                 do("t", [C["self"], C["em", 1]], lambda: mm(EB[h][:, 0:256], self_[:, 128 * h:128 * h + 128], emf[:], True, False))
 
-        def counts():
-            for h in range(2):
+        def counts(hs=(0, 1)):
+            for h in hs:
                 C["eb", h] = do("t", [C["za", 1]], lambda: mm(EB[h][:, 0:256], sel[:, 128 * h:128 * h + 128], za[:], False, True))
 
-        def out(then=None):
-            for h in range(2):
+        def out(then=None, hs=(0, 1)):
+            for h in hs:
                 c = slice(256 * h, 256 * h + 256)
-                d = do("s", [C["eb", h]], lambda: act(e[:, c], EB[h][:, 0:256], AF.Copy))
+                if x and h:
+                    d = ts([C["eb", h]], e[:, c], EB[h][:, 0:256], CODE, None, OP.mult)
+                else:
+                    d = do("s", [C["eb", h]], lambda: act(e[:, c], EB[h][:, 0:256], AF.Copy, scale=CODE))
                 if then:
                     then(c, d)
             return d
@@ -261,29 +292,24 @@ def rank_program(g, core, T, topo):
     parts, code_sel, code_numbers, code_counts, code_out, CW = code_window("", (T.pew, T.px), l_nx, l_em, None if r else m_s1)
 
     def window(to):
-        wb = (T.pwa, T.pcm, T.pwb, T.pew)
-        for x in range(4):
-            do("t", [c_ramp], lambda: mm(wb[x][:, 0:128], T.evl[:], T.ramp[:, 128 * x:128 * x + 128], True, False))
         for x in range(4):
             h, u = x // 2, x % 2
             d = do("t", [m_s1 if h else m_s0, m_tb if u else m_t0], lambda: mm(
-                wb[x][:, 0:128], T.selo[:, 128 * h:128 * h + 128], T.tq[:, 16 + 128 * u:144 + 128 * u], False, True))
-            d = do("s", [d], lambda: act(T.w[:, 128 * x:128 * x + 128], wb[x][:, 0:128], AF.Copy))
+                WB[x][:, 0:128], T.selo[:, 128 * h:128 * h + 128], T.tq[:, 16 + 128 * u:144 + 128 * u], False, True))
+            d = do("s", [d], lambda: act(T.w[:, 128 * x:128 * x + 128], WB[x][:, 0:128], AF.Copy))
+        symbols()
         if to is not None:
             send([d], [to], T.w1[:], T.w[:], "aw1")
         return d
 
-    def turned():
-        do("v", [m_tb], lambda: vec.transpose(T.tab[:, 0:256], T.tq[:, 16:272]))
-        do("v", [], lambda: vec.transpose(T.tab[:, 256:544], T.tq[:, 0:288]))
-        ts([am, c_k9], T.ot[:, 0:32:2], T.py[:, 64:80], CO[:, 8:9], 16.0, OP.add, OP.mult)
-        K["tab"] = ts([], T.ot[:, 1:32:2], T.py[:, 64:80], CO[:, 9:10], 16.0, OP.add, OP.mult)
 
     def lists(segs):
         def one(j, n):
             def f():
-                K["lt", j] = ts([K["tab"]], T.lt[:, 32 * j:32 * (j + n - 1)],
-                                T.tab[:].indirect(T.ot[:, 2 * j:2 * (j + n - 1)]), 256.0, None, OP.add)
+                d = ts([K["tab"]], T.lt[:, 32 * j:32 * (j + n - 1)],
+                       T.tab[:].indirect(T.ot[:, 2 * j:2 * (j + n - 1)]), 256.0, None, OP.add)
+                for i in range(j, j + n - 1):
+                    K["lt", i] = d
             return f
         return [one(j, n) for j, n, _ in segs]
 
@@ -300,7 +326,7 @@ def rank_program(g, core, T, topo):
                 slot[0] += 1
                 src = box[0].indirect(T.lt[:, 32 * i:32 * i + 32])
                 keep = T.pm[:, j + n - 1:j + n] if masked and i == (j + n - 2 if plus else j) else 1.0
-                deps = [box[1], K["lt", j], K["pm"]]
+                deps = [box[1], K["lt", i], K["pm"]]
                 if plus and i == j:
                     y, e = K["join", plus[0]]
                     d = tten(deps + [e], T.cpm[:] if r == 1 else out, src, T.cp[:, 512 * y:512 * y + 512], OP.add)
@@ -319,7 +345,7 @@ def rank_program(g, core, T, topo):
 
         def three():
             out = CO[:, 10 + len(ends):11 + len(ends)]
-            K["kb"] = ts([K.get("kb")], out, ends[0], ends[1], ends[2], OP.add, OP.add)
+            K["kb"] = ts([K.get("kb"), K["pm"]], out, ends[0], ends[1], ends[2], OP.add, OP.add)
             ends[0:3] = [out]
 
         def last():
@@ -330,7 +356,7 @@ def rank_program(g, core, T, topo):
             K["keep"] = d
 
         def diagonal():
-            K["dba"] = do("s", [K["keep"], c_idn], lambda: act(T.dba[:], T.idn[:], AF.Copy, scale=CO[:, 10:11]))
+            K["dba"] = do("s", [K["keep"], K["idn"]], lambda: act(T.dba[:], T.idn[:], AF.Copy, scale=CO[:, 10:11]))
         return [three] * ((len(ends) - 1) // 2) + [last], diagonal
 
     MB = (T.pcm, T.pc)
@@ -349,7 +375,7 @@ def rank_program(g, core, T, topo):
                 merge_add(T.dba, T.w, 0, [K["dba"], K["w"]], seg == order[0])
             else:
                 n, d = K["join", seg[0]]
-                md = merge_add(T.idn, T.cp, 512 * n, [d, c_idn], seg == order[0], seg == order[-1])
+                md = merge_add(T.idn, T.cp, 512 * n, [d, K["idn"]], seg == order[0], seg == order[-1])
         return md
 
     def merge_out(md):
@@ -381,31 +407,30 @@ def rank_program(g, core, T, topo):
         return out
 
     def string(segs, at, inner, hooks, start=0):
-        reads, late = {0: at}, []
+        reads, late = {segs[start][0]: at}, []
         for m in range(start, len(segs)):
             j, n, win, deps = segs[m]
             at = gather(win, at, deps, (j - 1) % 16)
             for i in range(j, j + n):
                 reads[i + 1] = at
-            play(late)
-            late = []
             steps, single = inner(j, n) if inner else ([], None)
+            row = [] if j in steps else [None]
             for i in steps:
                 def f(i=i, single=single):
                     reads[i + 1] = gather(single, reads[i], [], (i - 1) % 16)
-                late.append(f)
-            if j in steps:
-                late.pop(0)()
+                row.append(f)
+            late = [x for x in late + [row] if x]
+            play([f for f in [x.pop(0) for x in late] if f])
             play(hooks.get(m, []))
-        return reads, at, late
+        return reads, at, [f for f in weave(*late) if f]
 
     def code_at(qn, reads, j, ewin, edep, ee):
         tile, x0, d = reads[j]
         b = 0 if j == 0 else 16 * j + 16
         out, src = ee[:, b:b + 16], ewin[:].indirect(tile[:, x0:x0 + 1])
         if qn == "v":
-            return ts([d, edep, c_mask], out, src, T.mask[:, j:j + 1], None, OP.mult)
-        return do("s", [d, edep, c_mask], lambda: act(out, src, AF.Copy, scale=T.mask[:, j:j + 1]))
+            return ts([d, edep, K["far"]], out, src, T.far[:, j:j + 1], None, OP.add)
+        return do("s", [d, edep, K["far"]], lambda: act(out, src, AF.Identity, bias=T.far[:, j:j + 1]))
 
     def follow(reads, ewin, edep, ee, on_v):
         steps = sorted(range(16), key=lambda j: reads[j][2][1] if j else 0)
@@ -414,61 +439,81 @@ def rank_program(g, core, T, topo):
 
     cd, gd = {}, {}
     ydep = [None, 0]
+    SLOT = (0, 2, 0, 1)
 
-    def buf(name, q, n):
-        x = n * (q == 3)
-        return T[name + "ab"[q // 2]][:, x:x + n]
+    def buf(name, q, n, count=1):
+        return T[name + "abbb"[q]][:, n * SLOT[q]:n * (SLOT[q] + count)]
 
     def code(q):
-        return T["rc" + "ab"[q // 2]][:, 4 * (q == 3):4 * (q == 3) + 1]
+        return T["rc" + "abbb"[q]][:, 4 * SLOT[q]:4 * SLOT[q] + 1]
+
+    def whole(q):
+        K["qi", q] = do("v", [cd[q]], lambda: vec.tensor_copy(buf("qi", q, 1), code(q)))
 
     def total(q, ee, last):
-        cd[q] = do("v", last, lambda: vec.tensor_reduce(code(q), ee[:, 15:271:17], AxisListType.X, OP.add))
+        def one(out):
+            return do("v", last, lambda: vec.tensor_reduce(out, ee if q > 1 else ee[:, 15:271:17], AxisListType.X, OP.max))
+        if r > 1:
+            K["qi", q] = one(buf("qi", q, 1))
+        cd[q] = one(code(q))
+        if r < 2:
+            K["qi", q] = one(buf("qi", q, 1))
 
     def gates(q):
-        gd[q] = ts([cd[q]], buf("cn", q, 1), code(q), 0.0, 263.5, OP.min, OP.add)
+        src, d = (T.q2[:], K["qi", q]) if (r, q) == (1, 2) else (code(q), cd[q])
+        gd[q] = ts([d], buf("cn", q, 1), src, 0.0, 263.5 * CODE, OP.min, OP.add)
 
     def spread(q):
-        K["gg", q] = ts([cd[q], K["late"]], buf("gg", q, 32), T.thg[:], code(q), None, OP.is_le)
+        K["gg", q] = do("s", [cd[q], K["late"]], lambda: act(buf("gg", q, 32), T.thg[:], AF.Relu, bias=code(q), scale=-CODE / 2))
 
     def digits(qs, ep):
-        n, x = len(qs), "ab"[qs[0] // 2]
-        qi, di = T["qi" + x][:, 0:n], T["di" + x]
-
-        def whole():
-            K["qi"] = ts([cd[q] for q in qs], qi, T["rc" + x][:, 0:4 * n:4], CODE, None, OP.mult)
+        n, a = len(qs), 4 * SLOT[qs[0]]
+        qi, di, b = T.q2[:] if (r, qs[0]) == (1, 2) else buf("qi", qs[0], 1, n), T["di" + "abbb"[qs[0]]], a + 4 * n
 
         def low():
-            ts([K["qi"]], di[:, 0:4 * n:4], qi, 63, None, OP.bitwise_and)
-            ts([], di[:, 1:4 * n:4], qi, 6, 63, OP.arith_shift_right, OP.bitwise_and)
+            ts([K["qi", q] for q in qs], di[:, a:b:4], qi, 63, None, OP.bitwise_and)
 
         def high():
-            ts([], di[:, 2:4 * n:4], qi, 12, 63, OP.arith_shift_right, OP.bitwise_and)
-            K["di"] = ts([], di[:, 3:4 * n:4], qi, 18, 63, OP.arith_shift_right, OP.bitwise_and)
+            ts([], di[:, a + 1:b:4], qi, 6, 63, OP.arith_shift_right, OP.bitwise_and)
+            ts([], di[:, a + 2:b:4], qi, 12, 63, OP.arith_shift_right, OP.bitwise_and)
+            K["di"] = ts([], di[:, a + 3:b:4], qi, 18, 63, OP.arith_shift_right, OP.bitwise_and)
 
         def used(i):
             def f():
                 K["ep", qs[i]] = tten([K["di"], K["gg", qs[i]]], ep[:, 32 * i:32 * i + 32],
-                                      di[:, 0:4 * n].indirect(T.l32[:, 2 * i:2 * i + 2]), T["gg" + x][:, 32 * i:32 * i + 32], OP.mult)
+                                      di[:, a:b].indirect(T.l32[:, 2 * i:2 * i + 2]), buf("gg", qs[i], 32), OP.min)
             return f
-        return [whole, low, high] + [used(i) for i in range(n)]
+        return [low, high] + [used(i) for i in range(n)]
 
-    def begin(out, lhss, deps):
-        for lhs in lhss:
-            do("t", [K["late"]] + deps, lambda: mm(out, lhs[:], T.off[:], lhs is lhss[0], False))
+    places = {q: (T.pb, T.pc, T.pwa, T.pb)[q][:, 0:1] for q in range(max(r - 1, 0), min(r + 2, 4))}
+    sums = {q: [T.tri[:]] + [T.bo[:]] * q for q in places}
+    if r == 3:
+        places["Z"], sums["Z"] = T.pew[0:8, 0:1], [T.bo[:, 0:128:16]] * 4
+    missing = {q: len(sums[q]) for q in sums}
 
-    def count(out, lhs, q, stop=True):
-        return do("t", [gd[q]], lambda: mm(out, lhs[:], buf("cn", q, 1), False, stop))
+    def begin(deps):
+        for q in places:
+            for n in range(len(sums[q])):
+                do("t", [K["late"]] + deps, lambda: mm(places[q], sums[q][n], T.off[:], n == 0, False))
 
-    def hot(q, deps, first):
-        oh = T["oh%d" % q][:]
-        if q == 1:
-            K["oh", q] = ts(deps, oh, T.pl[:], T.dec0[:, 33:34], first, OP.subtract, OP.is_equal)
-        else:
-            K["oh", q] = ts(deps + [K["late"]], oh, (T.pl if q < 2 else T.plb)[:], first, None, OP.is_equal)
+    def tally(b):
+        gates(b)
+        for q in places:
+            if q == "Z" or q >= b:
+                missing[q] -= 1
+                K["at", q] = do("t", [gd[b]], lambda: mm(places[q], sums[q][0 if q == b else -1], buf("cn", b, 1), False, not missing[q]))
 
-    def from_two(deps):
-        return ts(deps + [K["late"]], T.plb[:], T.pl[:], T.dec0[:, 33:34], T.dec1[:, 33:34], OP.subtract, OP.subtract)
+    def hot(q):
+        K["oh", q] = ts([K["at", q]], T["oh%d" % q][:], T.pl[:], places[q], None, OP.is_equal)
+
+    def alone(q, out, final):
+        D = digits([q], out)
+        tally(q)
+        spread(q)
+        play(D[:2])
+        hot(q)
+        D[2]()
+        add(q, out, 0, [K["ep", q]], final)
 
     def add(q, src, x, deps, final=False):
         for m in range(4):
@@ -476,74 +521,79 @@ def rank_program(g, core, T, topo):
                 T.py[0:8, 0:32], src[:, x + 8 * m:x + 8 * m + 8], T["oh%d" % q][:, 3 - m:35 - m], ydep[1] == 0, final and m == 3))
             ydep[1] += 1
 
-    def finish(q):
-        dec = T["dec%d" % q]
-        D = digits([q], dec)
-
-        def a():
-            D[0]()
-            gates(q)
-            for x in range(2):
-                begin(T.pb[:, x:x + 1], [(T.tri, T.bo)[x]], [cd[q]])
-                K["sum"] = count(T.pb[:, x:x + 1], (T.tri, T.bo)[x], q)
-            spread(q)
-
-        def b():
-            K["pos"] = do("v", [K["sum"]], lambda: vec.tensor_copy(dec[:, 32:34], T.pb[:, 0:2]))
-        return [a] + D[1:3] + [b] + D[3:]
-
     if r == 0:
-        at = (T.s1, 0, ts([m_0], T.s1[:], T.pc[:, 0:2], 256.0, None, OP.add))
         wdep = [None, None]
-        for u in range(2):
-            for h in range(2):
-                bank, out = (T.pwa, T.pwb, T.pcm, T.py)[2 * u + h][:, 128:256], T.w[:, 256 * h + 128 * u:256 * h + 128 * u + 128]
-                d = do("t", [m_s1 if h else None, m_tb if u else None], lambda: mm(
-                    bank, T.sel[:, 128 * h:128 * h + 128], T.tq[:, 16 + 128 * u:144 + 128 * u], True, True))
-                wdep[h] = do("v", [d], lambda: vec.tensor_copy(out, bank)) if h else do("s", [d], lambda: act(out, bank, AF.Copy))
+        for x in range(4):
+            h, u = x // 2, x % 2
+            bank, out = (T.pwa, T.pwb, T.pcm, T.py)[x][:, 128:256], T.w[:, 128 * x:128 * x + 128]
+            d = do("t", [m_s1 if h else m_s0, m_tb if u else m_t0], lambda: mm(
+                bank, T.sel[:, 128 * h:128 * h + 128], T.tq[:, 16 + 128 * u:144 + 128 * u], True, True))
+            wdep[u] = do("s", [d], lambda: act(out, bank, AF.Copy)) if u else do("v", [d], lambda: vec.tensor_copy(out, bank))
+            if x == 0:
+                at = (T.s1, 0, ts([], T.s1[:], T.pwa[:, 128:130], 256.0, None, OP.add))
+        group_symbols()
+        play(turn[1:3])
         late_constants()
         code_sel()
+        waits("s", wdep)
+        K["w"] = wdep[0]
         parts3, sel3, numbers3, counts3, out3, _ = code_window(
             "x", (T.pwa, T.pwb), arrive(3, "anx"), arrive(3, "aem"), arrive(3, "asel"))
         dl = digit_list()
-        fill = dl[:1] + parts + dl[1:] + parts3
-        hooks = {n + 1: [fill[n]] for n in range(15)}
-        hooks[3].append(code_numbers)
-        hooks[13] += [code_counts, sel3]
-        reads, at1, _ = string(plan(0, (T.w[:], wdep), [None]), at, None, hooks, 1)
+        j = LAST[0]
+        fill = parts[:1] + lists([LAST]) + parts[1:] + parts3[:4] + parts3[4:]
+        hooks = {n + 1: [fill[n]] for n in range(j - 1)}
+        hooks[1].insert(0, turn[3])
+        hooks[2] += joins(LAST, None, False)
+        hooks[3] += [code_numbers] + dl[:1]
+        reads, at1, _ = string(plan(0, (T.w[:], wdep), [None])[:j], at, None, hooks, 1)
+        more, at1, late = string([LAST[:2] + (table(LAST), [K["join", j][1]])], at1, lambda j, n: (range(j, j + n - 1), T.w[:]), {})
+        reads.update({i: more[i] for i in more if i})
         reads[0], reads[1] = (T.zero, 0, c_zero), at
         send([at1[2]], [1], T.s1[:], T.tt[:, at1[1]:at1[1] + 2], "as1")
-        last = follow(reads, T.e, code_out(), T.eea, 0)
-        hooks = {n: [fill[15 + n]] for n in range(single)}
-        hooks[0].append(numbers3)
+        fill = fill[j - 1:]
+        x = 14 - j
+
+        def codes0():
+            reads.update({i: more[i] for i in more if i})
+            code_counts()
+            sel3()
+            K["last"] = follow(reads, T.e, code_out(), T.eea, 0)
+        hooks = {n: [fill[n]] for n in range(single)}
+        hooks[0] += late
+        hooks[x - 1].append(codes0)
+        hooks[x + 1].append(numbers3)
         at = string(plan(1, (T.w1[:], [arrive(1, "aw1")]), [(None, None)])[:single], at1, None, hooks)[1]
         send([at[2]], [2, 3], T.s1[:], T.tt[:, at[1]:at[1] + 2], "as1")
-        play(fill[15 + single:] + [counts3])
+        play(fill[single:] + [counts3])
+        total(0, T.eea, K["last"])
+        send([cd[0]], [2, 3, 1], code(0), code(0), "arc0", "apart")
         out3(lambda c, d: send([d], [2], T.ex[:, c], T.ex[:, c], "aex", "wide"))
-        total(0, T.eea, last)
-        play(finish(0))
-        send([K["ep", 0]], [2, 3, 1], T.dec0[:], T.dec0[:], "arc0", "apart")
-        hot(0, [K["pos"]], T.dec0[:, 32:33])
-        add(0, T.dec0, 0, [])
-        hot(1, [arrive(1, "arc1")], T.dec1[:, 32:33])
-        add(1, T.dec1, 0, [], True)
+        dl[1]()
+        begin([])
+        alone(0, T.epa, False)
+        cd[1] = arrive(1, "arc1")
+        whole(1)
+        alone(1, T.epb, True)
     else:
         mc, diagonal = merge_constants()
         if r == 3:
-            send([l_em], [0], T.emix[:], T.emi[:], "aem")
             send([l_nx], [0], T.nxix[:], T.nxi[:], "anx")
+            send([l_em], [0], T.emix[:], T.emi[:], "aem")
+        else:
+            identity()
         to = {1: 0, 2: 3, 3: 2}[r]
         K["w"] = window(to if r < 3 else None)
         if r == 2:
             late_constants()
         on = {qn: [s for s in long if s[2] == qn] for qn in "sv"}
         S, V = on["s"], on["v"]
-        turned()
+        play(turn)
         js = weave(*[joins(s) for s in S])
         if r == 1:
             jv = joins(V[0], S[0])
             n = 4
-            play(parts[:1] + lists(S + V) + js + weave(jv[:-1], parts[1:n]) + [code_sel, code_numbers] + jv[-1:])
+            play(lists(V + S) + js + jv[:1] + parts[:1] + jv[1:2] + parts[1:2] + jv[2:-1] + parts[2:4] + [code_sel, code_numbers] + jv[-1:])
             cmd = [K["join", V[0][0]][1]]
             send(cmd, [2, 3], T.cp1[:], T.cpm[:], "acp1", "apart")
             js = weave(*[joins(s, None, False) for s in OWN])
@@ -552,18 +602,19 @@ def rank_program(g, core, T, topo):
             play(js[FILL[1]:])
         if r == 2:
             ja, jb = joins(V[0], S[0]), joins(V[1], S[1])
-            play(parts[:1] + lists(S) + js[:1] + parts[1:2] + [code_sel] + weave(parts[2:4] + lists(V), mc) + [code_numbers] + js[1:]
+            play(lists(S) + js[:3] + parts[:2] + weave(lists(V) + parts[2:4], mc) + [code_sel, code_numbers, js[4], js[3]]
                  + [diagonal] + weave(ja[:-1], jb[:-1]) + parts[4:FILL[r]])
-            for i in range(2):
+            for i in (0, 1):
                 (ja, jb)[i][-1]()
                 send([K["join", V[i][0]][1]], [to], (T.cpx, T.cpy)[i][:], table(V[i]), ("acpx", "acpy")[i])
             md = merge(V[:1] + [None] + V[1:])
-            play(parts[FILL[r]:] + [code_counts])
+            play(parts[FILL[r]:FILL[4]])
         if r == 3:
             jv = weave(joins(V[0], S[0]), joins(V[1], S[1]))
             js, je = weave(joins(S[0]), joins(S[1])), joins(S[2])
-            play(parts[:1] + lists(S[:2]) + js[:1] + parts[1:2])
+            play(lists(S[:2]) + js[:1] + parts[:2])
             send([CW["sel", 1]], [0], T.selx[:], T.sel[:], "asel")
+            identity()
             play([code_sel] + weave(parts[2:4] + lists(V), mc) + [code_numbers] + js[1:] + jv[:1]
                  + lists(S[2:]) + je[:1] + [diagonal] + je[1:] + jv[1:])
             md = merge(V[:1] + [None] + V[1:] + S[2:])
@@ -571,15 +622,16 @@ def rank_program(g, core, T, topo):
         if r != 2:
             late_constants()
         dl = digit_list()
-        play(dl[:1])
         if r > 1:
             cmd = merge_out(md)
         if r == 3:
             send(cmd, [to], T.cpx[:], T.cpm[:], "acpx")
-        if r > 1:
+        if r == 3:
             ed = code_out()
-        play(dl[1:])
-        begin(T.pwa[:, 0:1], [T.tri], [])
+        if r == 1:
+            play(dl)
+        if r != 2:
+            begin(cmd + [ed])
     if r == 1:
         segs = plan(1, (T.w[:], []), [(T.cpm[:], cmd)])
         if OWN:
@@ -587,82 +639,116 @@ def rank_program(g, core, T, topo):
         reads, _, late = string(segs, (T.s1, 0, arrive(0, "as1")),
                                 lambda j, n: (range(j, j + n - (1 if j < single else 2)), T.w[:]), {})
         play(late)
-        total(1, T.eea, follow(reads, T.e, ed, T.eea, 4))
-        play(finish(1))
-        send([K["ep", 1]], [2, 3, 0], T.dec1[:], T.dec1[:], "arc1", "apart")
-        for q in range(2):
-            hot(q, [K["pos"], arrive(0, "arc0")], T["dec%d" % q][:, 32:33])
-            add(q, T["dec%d" % q], 0, [])
-        base = from_two([])
-        cd[2] = arrive(2, "arc2")
+        total(1, T.eea, follow(reads, T.e, ed, T.eea, 3))
+        send([cd[1]], [2, 3, 0], code(1), code(1), "arc1", "apart")
+        spread(1)
+        play(digits([1], T.ep1))
+        send([K["ep", 1]], [2], T.ep1[:], T.ep1[:], "aep1")
+        tally(1)
+        cd[0] = arrive(0, "arc0")
+        whole(0)
+        alone(0, T.epa, False)
+        hot(1)
+        add(1, T.ep1, 0, [])
+        K["qi", 2] = arrive(2, "arc2")
+        cd[2] = do("v", [K["qi", 2]], lambda: vec.tensor_copy(code(2), T.q2[:]))
         D = digits([2], T.epb)
-        D[0]()
-        gates(2)
-        c2 = count(T.pwa[:, 0:1], T.tri, 2)
         spread(2)
-        play(D[1:])
-        hot(2, [c2, base], T.pwa[:, 0:1])
+        play(D[:1] + [lambda: tally(2)] + D[1:])
+        hot(2)
         add(2, T.epb, 0, [], True)
     if r > 1:
-        begin(T.pb[:, 0:1], [T.tri, T.bo], [])
         own, other = [(T.cpm[:], cmd)], [(T.cpx[:], [arrive(5 - r, "acpx")])]
         if r == 3:
             other.append((T.cpy[:], [arrive(2, "acpy")]))
         plain = (T.w[:], []) if r == 2 else (T.w1[:], [arrive(2, "aw1")])
         rest = plan(1, (None, None), [(T.cp1[:], [arrive(1, "acp1", "apart")])])[single:]
-        at = string(rest, (T.s1, 0, arrive(0, "as1")), None, {})[1]
-        reads2, at, late = string(plan(2, plain, own if r == 2 else other), at,
-                                  (lambda j, n: (range(j + 1, j + n - 2), T.cpm[:])) if r == 2 else None, {})
+        hooks = {0: dl[:1], 1: dl[1:]}
+        if r == 2:
+            left = parts[FILL[4]:]
+            hooks = {0: left[:len(left) // 2] + dl[:1], 1: left[len(left) // 2:] + [code_counts]}
+            if not left:
+                code_counts()
+                hooks[1] = []
+        at = string(rest, (T.s1, 0, arrive(0, "as1")), None, hooks)[1]
+        if r == 2:
+            ed = code_out()
+            begin(cmd + [ed])
         a0, a1 = arrive(0, "arc0", "apart"), arrive(1, "arc1", "apart")
 
-        def counts2():
-            gates(2)
-            K["c2"] = count(T.pwa[:, 0:1], T.tri, 2)
-            count(T.pb[:, 0:1], T.bo, 2, False)
-            spread(2)
+        def last_two(q):
+            return [range(j + 1, min(j + n + 1, 16)) for j, n, _ in segments(q)[-2:]]
 
-        def t2():
-            total(2, T.eea, K["l2"])
-            send([cd[2]], [3, 1], code(2), code(2), "arc2")
+        def far_two(q):
+            def f():
+                for x in range(2):
+                    js, c = last_two(q)[x], 32 * (q - 2) + 16 * x - 1
+                    do("v", [c_far3], lambda: vec.tensor_copy(T.far3[:, c + js[0]:c + js[-1] + 1], T.far[:, js[0]:js[-1] + 1]))
+            return f
+
+        def codes(q, at, wins, inner, hooks, e, edep, ee):
+            segs, out, n = plan(q, *wins), T["ee%d" % q], last_two(q)[0][0]
+            reads, at, _ = string(segs[:-1], at, inner, hooks)
+            steps = sorted(range(n), key=lambda j: reads[j][2][1] if j else 0)
+            last = [code_at("s", reads, j, e, edep, ee) for j in steps[:-FILL["v", q] or None]][-1]
+
+            def three(x, at):
+                c = 32 * (q - 2) + 16 * x
+                return tten([at[2], edep], out[:, 1 + 16 * x:17 + 16 * x], e[:].indirect(at[0][:, at[1]:at[1] + 1]),
+                            T.far3[:, c:c + 16], OP.add)
+            end = string(segs[-1:], at, None, {})[1]
+            own = [code_at("v", reads, j, e, edep, ee) for j in steps[n - FILL["v", q]:]]
+            three(0, at)
+
+            def early():
+                return do("v", [last] + own, lambda: vec.tensor_reduce(out[:, 0:1], ee[:, 15:17 * n:17], AxisListType.X, OP.max))
+
+            def rest():
+                three(1, end)
+                K["ee2"] = early()
+                send([K["ee2"]], [3], T.ee2[:], T.ee2[:], "arc2")
+            if q == 2:
+                return end, rest
+            tally(0)
+            early()
+            return end, three(1, end)
+
+        cd[0], cd[1] = a0, a1
         if r == 2:
-            K["l2"] = follow(reads2, T.e, ed, T.eea, 2)
-            e3, e3d = T.ex, arrive(0, "aex", "wide", 2)
-            hooks = {0: [t2], 1: [counts2]}
+            at, last = codes(2, at, (plain, own), lambda j, n: (range(j + 1, j + n - 2), T.cpm[:]),
+                             {0: [far_two(2)], 1: [far_two(3)], 2: dl[1:]}, T.e, ed, T.eea)
+            hooks = {0: [last],
+                     1: [lambda: total(2, T.ee2[:], [K["ee2"]]), lambda: send([K["qi", 2]], [1], T.q2[:], buf("qi", 2, 1), "arc2")],
+                     2: [lambda: tally(2)]}
+            last3 = codes(3, at, (None, other), None, hooks, T.ex, arrive(0, "aex", "wide", 2), T.eeb)[1]
+            tally(1)
+            spread(2)
         else:
-            e3, e3d = T.e, ed
-            hooks = {}
-        reads3, _, late = string(plan(3, (other if r == 2 else own)[0], other if r == 2 else own), at,
-                                 lambda j, n: (range(j + 1, j + n - 2), (T.cpx if r == 2 else T.cpm)[:]), hooks)
-        last = follow(reads3, e3, e3d, T.eeb, 3)
+            at = string(plan(2, plain, other), at, None, {0: [far_two(3)]})[1]
+            last3 = codes(3, at, (None, own), None, {}, T.e, ed, T.eeb)[1]
+            tally(1)
+            total(2, T.ee2[:], [arrive(2, "arc2")])
+        total(3, T.ee3[:], [last3])
         if r == 3:
-            cd[2] = arrive(2, "arc2")
-            counts2()
-        total(3, T.eeb, last)
+            tally(2)
         D = digits([2, 3], T.epb)
         D[0]()
-        gates(3)
-        K["c3"] = count(T.pb[:, 0:1], T.tri, 3)
+        tally(3)
         if r == 3:
-            Z, groups = T.pew[0:8, 0:1], T.bo[:, 0:128:16]
-            for q in (2, 3):
-                do("t", [], lambda: mm(Z, groups, T.off[:], q == 2, False))
-                do("t", [], lambda: mm(Z, groups, buf("cn", q, 1), False, False))
-            do("t", [a0], lambda: mm(Z, T.idn[:, 0:128:16], T.dec0[:, 33:34], False, False))
-            zd = do("t", [a1], lambda: mm(Z, T.idn[:, 0:128:16], T.dec1[:, 33:34], False, True))
+            spread(2)
         spread(3)
-        play(D[1:3])
-        base = from_two([a0, a1])
+        D[1]()
         if r == 2:
-            hot(1, [], T.dec1[:, 32:33])
-            add(1, T.dec1, 0, [])
+            hot(1)
+            add(1, T.ep1, 0, [arrive(1, "aep1")])
+        hot(2)
+        D[2]()
+        add(2, T.epb, 0, [K["ep", 2]])
         D[3]()
-        hot(2, [K["c2"], base], T.pwa[:, 0:1])
-        add(2, T.epb, 0, [])
-        D[4]()
-        hot(3, [K["c3"]], T.pb[:, 0:1])
+        hot(3)
         add(3, T.epb, 32, [], True)
     if r == 3:
-        nd = ts([zd], T.neg[:], T.pl[0:8, 3:35], Z, -1.0, OP.is_ge, OP.mult)
+        nd = ts([K["at", "Z"]], T.neg[:], T.pl[0:8, 3:35], places["Z"], -1.0, OP.is_ge, OP.mult)
         yd = tten([ydep[0], nd], T.ysb[:], T.py[0:8, 0:32], T.neg[:], OP.add)
     else:
         yd = do("v", [ydep[0]], lambda: vec.tensor_copy(T.ysb[:], T.py[0:8, 0:32]))

@@ -1,30 +1,33 @@
 import numpy as np
-from concourse.bass import DstId, RemoteDMATransfer
+from concourse.bass import DstId, RemoteDMATransfer, IndirectOffsetOnAxis
 from concourse.mybir import dt, AluOpType, AxisListType, ActivationFunctionType
 
 F, H, I, U = "float32", "bfloat16", "int32", "uint16"
 SCRATCH = {
-    "nxi": ("sbuf", [128, 256], I), "emi": ("sbuf", [128, 256], I), "syr": ("sbuf", [1, 128], I),
-    "syb": ("sbuf", [1, 128], H), "one": ("sbuf", [1, 128], H), "six": ("sbuf", [1, 128], H), "syc": ("sbuf", [128, 1], I),
-    "evl": ("sbuf", [1, 128], H), "ramp": ("sbuf", [1, 512], H),
-    "pci": ("sbuf", [128, 2], I), "pf": ("sbuf", [128, 1], F), "igf": ("sbuf", [128, 128], F),
-    "rowf": ("sbuf", [128, 128], F), "pl": ("sbuf", [128, 36], F), "plb": ("sbuf", [128, 36], F), "mg": ("sbuf", [128, 32], F),
+    "nxi": ("sbuf", [128, 256], I), "emi": ("sbuf", [128, 256], I), "syr": ("sbuf", [1, 128], I), "sy8": ("sbuf", [8, 16], I),
+    "syb": ("sbuf", [1, 128], H), "six": ("sbuf", [1, 128], H), "syc": ("sbuf", [128, 1], I), "sy8b": ("sbuf", [8, 16], H),
+    "evl": ("sbuf", [1, 128], H), "ramp": ("sbuf", [1, 512], H), "ind": ("sbuf", [1, 240], H),
+    "tbd": ("dram", [64, 1024], I), "cw": ("sbuf", [128, 1024], I), "idx": ("sbuf", [128, 1], I),
+    "pci": ("sbuf", [128, 2], I), "igf": ("sbuf", [128, 128], F),
+    "rowf": ("sbuf", [128, 128], F), "pl": ("sbuf", [128, 36], F), "mg": ("sbuf", [128, 32], F),
     "ci5": ("sbuf", [128, 6], I), "cf5": ("sbuf", [128, 6], F), "cols": ("sbuf", [128, 16], F),
     "bo": ("sbuf", [128, 128], H), "tri": ("sbuf", [128, 128], H), "idn": ("sbuf", [128, 128], H), "dba": ("sbuf", [128, 128], H),
-    "mask": ("sbuf", [128, 16], F), "pm": ("sbuf", [128, 16], F), "far": ("sbuf", [128, 16], F),
-    "far3": ("sbuf", [128, 64], F), "ee2": ("sbuf", [128, 33], F), "ee3": ("sbuf", [128, 33], F),
-    "thg": ("sbuf", [128, 32], F), "tho": ("sbuf", [128, 32], F), "l32": ("sbuf", [128, 6], U),
+    "mask": ("sbuf", [128, 17], F), "pm": ("sbuf", [128, 16], F), "vm": ("sbuf", [128, 128], F),
+    "dm": ("sbuf", [128, 32], F), "dn": ("sbuf", [128, 48], F),
+    "thg": ("sbuf", [128, 32], F), "tho": ("sbuf", [128, 32], F), "l32": ("sbuf", [128, 4], U),
     "ti": ("sbuf", [128, 256], I), "sel": ("sbuf", [128, 256], H), "selo": ("sbuf", [128, 256], H),
-    "hi": ("sbuf", [128, 256], I), "ci": ("sbuf", [128, 256], I), "za": ("sbuf", [128, 256], H), "emf": ("sbuf", [128, 256], F),
-    "nxix": ("sbuf", [128, 256], I), "emix": ("sbuf", [128, 256], I), "selx": ("sbuf", [128, 256], H),
-    "hix": ("sbuf", [128, 256], I), "cix": ("sbuf", [128, 256], I), "emfx": ("sbuf", [128, 256], F), "zax": ("sbuf", [128, 256], H), "selfx": ("sbuf", [128, 256], F),
-    "off": ("sbuf", [128, 1], H), "self": ("sbuf", [128, 256], F), "tq": ("sbuf", [128, 288], H), "tab": ("sbuf", [128, 544], H),
-    "d16": ("sbuf", [128, 16], H), "ot": ("sbuf", [128, 32], U), "lt": ("sbuf", [128, 512], U),
-    "w": ("sbuf", [128, 512], H), "w1": ("sbuf", [128, 512], H), "cpy": ("sbuf", [128, 512], H), "cp1": ("sbuf", [128, 512], H),
-    "e": ("sbuf", [128, 512], F), "ex": ("sbuf", [128, 512], F),
-    "cp": ("sbuf", [128, 7168], H), "cpm": ("sbuf", [128, 512], H), "cpx": ("sbuf", [128, 512], H),
-    "s1": ("sbuf", [128, 2], U), "zero": ("sbuf", [128, 2], U), "tt": ("sbuf", [128, 1080], U),
-    "eea": ("sbuf", [128, 272], F), "eeb": ("sbuf", [128, 272], F), "pos": ("sbuf", [128, 4], F), "zed": ("sbuf", [8, 1], F),
+    "nxd": ("dram", [128, 256], I), "emd": ("dram", [128, 256], I), "tbx": ("dram", [64, 1024], I),
+    "cwx": ("sbuf", [128, 1024], I), "idy": ("sbuf", [128, 1], I),
+    "off": ("sbuf", [128, 1], H), "tq": ("sbuf", [128, 288], H), "tab": ("sbuf", [128, 544], H),
+    "ot": ("sbuf", [128, 32], U), "lt": ("sbuf", [128, 512], U),
+    "w": ("sbuf", [128, 512], H), "w1": ("sbuf", [128, 512], H), "ltx": ("sbuf", [128, 512], U), "cp1": ("sbuf", [128, 512], H),
+    "cp": ("sbuf", [128, 7680], H), "cpm": ("sbuf", [128, 512], H), "cpx": ("sbuf", [128, 512], H), "cpe": ("sbuf", [128, 512], H), "wr": ("sbuf", [128, 512], H), "cpy": ("sbuf", [128, 512], H),
+    "s1": ("sbuf", [128, 2], U), "tt": ("sbuf", [128, 1024], U), "tu": ("sbuf", [128, 512], U), "all": ("sbuf", [128, 8], U),
+    "e0": ("sbuf", [128, 32], F), "e1": ("sbuf", [128, 32], F), "e2": ("sbuf", [128, 32], F), "e3": ("sbuf", [128, 64], F),
+    "cn": ("sbuf", [128, 32], H), "gg": ("sbuf", [128, 128], H),
+    "rc0": ("sbuf", [128, 2], I), "rc1": ("sbuf", [128, 2], I), "rcb": ("sbuf", [128, 8], I),
+    "di0": ("sbuf", [128, 4], I), "di1": ("sbuf", [128, 4], I), "dib": ("sbuf", [128, 8], I),
+    "ep0": ("sbuf", [128, 32], H), "ep1": ("sbuf", [128, 32], H), "epb": ("sbuf", [128, 64], H),
     "ysb": ("sbuf", [8, 32], F), "neg": ("sbuf", [8, 32], F),
     "px": ("psum", [128, 512], F), "pwa": ("psum", [128, 512], F), "pwb": ("psum", [128, 512], F),
     "pcm": ("psum", [128, 512], F), "pew": ("psum", [128, 512], F), "pb": ("psum", [128, 512], F),
@@ -32,27 +35,21 @@ SCRATCH = {
 }
 for _q in range(4):
     SCRATCH["oh%d" % _q] = ("sbuf", [128, 36], H)
-for _q in "ab":
-    SCRATCH["rc" + _q] = ("sbuf", [128, 12], F)
-    SCRATCH["qi" + _q] = ("sbuf", [128, 3], I)
-    SCRATCH["di" + _q] = ("sbuf", [128, 12], I)
-    SCRATCH["cn" + _q] = ("sbuf", [128, 3], H)
-    SCRATCH["gg" + _q] = ("sbuf", [128, 96], H)
-    SCRATCH["ep" + _q] = ("sbuf", [128, 96], H)
-SCRATCH["ep1"] = ("sbuf", [128, 32], H)
-SCRATCH["q2"] = ("sbuf", [128, 1], I)
-SEMAPHORES = ["v", "s", "t", "p", "lnx", "lsy", "lsc", "lem", "st", "loc",
-              "as1", "aw1", "acpx", "aex", "arc0", "arc1", "arc2", "anx", "aem", "asel", "acpy", "acp1", "aep1"]
+SEMAPHORES = ["v", "s", "t", "p", "lnx", "lsy", "lsc", "lem", "ltb", "lcw", "ltx", "lcx", "lmg", "st", "loc",
+              "as1", "aw1", "awr", "acpx", "acpy", "acpe", "arc0", "arc1", "arc2", "acn0", "acn1", "anx", "aem", "aidx", "alt", "acp1", "aep1"]
 OP = AluOpType
 AF = ActivationFunctionType
 SEGS = {0: [(1, "")] * 16,
         1: [(1, "")] * 7 + [(5, "v"), (4, "s")],
-        2: [(1, "")] * 2 + [(4, "s"), (4, "v"), (3, "s"), (3, "v")],
-        3: [(3, "s"), (3, "v"), (3, "s"), (3, "v"), (3, "s")]}
-FILL = {1: 2, 2: 8, 4: 14, ("v", 2): 1, ("v", 3): 0}
+        2: [(5, "s"), (5, "v"), (3, "s"), (3, "v")],
+        3: [(3, "s"), (3, "v"), (3, "s"), (3, "1"), (3, "v")]}
 OWN = [(4, 3, "s")]
-LAST = (13, 3, "s")
-CODE = 262144.0
+PIECES = [4, 6, 6, 6, 6, 4]
+ZERO = [(8, 2, "s"), (10, 2, "v"), (12, 2, "s"), (14, 2, "s")]
+ONE = [(5, 2, "s")]
+OPT = {"early": True, "order": [2, 3], "state": "apart", "d2": "s", "d3": 0, "c3": "vvss", "shift": 0, "f2": 1, "f3": 3, "relay": True, "t2": True, "behind": False, "split": False, "patch": False, "by2": True, "p3": 3, "c1": True, "o2": [1, 3], "g2": True}
+UNIT = 512.0
+BASE = 130 * UNIT
 
 
 def segments(q):
@@ -73,7 +70,6 @@ def rank_program(g, core, T, topo):
     vec, act, mm = g.vector, g.scalar.activation, g.tensor.matmul
     long = [s for s in segments(r) if s[1] > 1]
     single = len([s for s in SEGS[1] if s[0] == 1])
-    tb = T.tq[:, 16:272]
 
     def waits(qn, deps):
         need = {}
@@ -134,162 +130,121 @@ def rank_program(g, core, T, topo):
 
     l_nx = dma("y", [], "lnx", T.nxi[:], T.nx[:])
     l_sy = dma("s", [], "lsy", T.syr[:], T.sy[:])
+    if r == 3 or r == 2 and OPT["t2"]:
+        l_em = dma("y", [], "lem", T.emi[:], T.em[:])
     l_sc = dma("s", [], "lsc", T.syc[:], T.sy[:])
-    l_em = dma("y", [], "lem", T.emi[:], T.em[:])
+    dma("y", [], "ltb", T.tbd[:, 0:512], T.nx[:])
+    l_tb = dma("y", [], "ltb", T.tbd[:, 512:1024], T.em[:])
 
     lo = {"allow_small_or_imprecise_dtypes": True}
     c_p = do("p", [], lambda: g.iota(T.pci[:, 0:1], [[0, 1]], 0, 1))
+    if r > 0:
+        c_row = do("p", [], lambda: g.iota(T.rowf[:], [[1, 128]], 0, 0, **lo))
     c_ig = do("p", [], lambda: g.iota(T.igf[:], [[1, 8], [0, 16]], 0, 0, **lo))
+    if r == 0:
+        c_row = do("p", [], lambda: g.iota(T.rowf[:], [[1, 128]], 0, 0, **lo))
     c_17 = do("p", [], lambda: g.iota(T.pci[:, 1:2], [[0, 1]], 0, 17))
-    c_row = do("p", [], lambda: g.iota(T.rowf[:], [[1, 128]], 0, 0, **lo))
     if r > 0:
         c_ramp = [do("s", [c_row], lambda: act(T.ramp[:, 128 * x:128 * x + 128], T.rowf[0:1, :], AF.Identity, bias=128.0 * x - 256))
                   for x in range(4)]
         x = do("v", [], lambda: vec.memset(T.evl[:], 0.0))
-    do("v", [], lambda: vec.memset(T.off[:], -256 * CODE))
-    if r > 1:
-        c_far3 = do("v", [], lambda: vec.memset(T.far3[:], -256 * CODE))
+    do("v", [], lambda: vec.memset(T.ind[:, 0:112], 0.0))
+    do("v", [], lambda: vec.memset(T.ind[:, 112:128], 4.0))
+    c_ind = do("v", [], lambda: vec.memset(T.ind[:, 128:240], 0.0))
     c_six = do("v", [], lambda: vec.memset(T.six[:], 64.0))
     P1, CI, CF, CO = T.pci[:, 0:1], T.ci5, T.cf5, T.cols
+    do("v", [], lambda: vec.memset(T.tq[:, 0:16], 0.0))
     ts([c_p], CI[:, 0:1], P1, 4, None, OP.arith_shift_right)
     y = ts([], CI[:, 1:2], P1, 15, None, OP.bitwise_and)
-    if r == 0:
-        c_zero = do("v", [], lambda: vec.memset(T.zero[:], 0))
-    else:
+    if r > 0:
         for j, n, _ in long:
             c_evl = do("v", [x], lambda: vec.memset(T.evl[:, j + n - 2:128:16], 1.0))
     c_cf = do("v", [y], lambda: vec.tensor_copy(CF[:, 0:2], CI[:, 0:2]))
-    ne = ts([c_17], CI[:, 2:3], T.pci[:, 1:2], 4, 1, OP.arith_shift_right, OP.bitwise_and)
-    do("v", [], lambda: vec.memset(T.tq[:, 0:16], 0.0))
-    c_bo = ts([c_cf, c_ig], T.bo[:], T.igf[:], CF[:, 0:1], None, OP.is_equal)
-    m_sy = ts([l_sy], T.syb[:], T.syr[:], 1.0 / 32, -0.25, OP.mult, OP.add)
-    c_k8 = ts([ne], CO[:, 8:9], CI[:, 2:3], 17.0, CF[:, 1:2], OP.mult, OP.add)
     do("v", [], lambda: vec.memset(T.tq[:, 272:288], 0.0))
-    c_mask = ts([c_row], T.mask[:], T.rowf[:, 0:16], CF[:, 1:2], None, OP.is_equal)
+    do("v", [], lambda: vec.memset(T.off[:], -BASE))
     if r > 0:
-        do("t", [c_bo], lambda: mm(T.pc[:, 0:128], T.bo[:], T.bo[:], True, False))
-        do("t", [c_evl, c_six], lambda: mm(T.pc[:, 0:128], T.six[:], T.evl[:], False, False))
-        m_o = do("t", [m_sy], lambda: mm(T.pc[:, 0:128], T.six[:], T.syb[:], False, True))
-        WB = (T.pwa, T.pwb, T.pcm, T.pew)
-        for x in range(4):
-            do("t", [c_ramp[x]], lambda: mm(WB[x][:, 0:128], T.evl[:], T.ramp[:, 128 * x:128 * x + 128], True, False))
+        c_k1 = ts([c_cf], CO[:, 6:7], CF[:, 1:2], 1.0, None, OP.add)
+        c_g8 = ts([], CO[:, 3:4], CF[:, 0:1], 8.0, None, OP.mult)
+    c_bo = ts([c_cf, c_ig], T.bo[:], T.igf[:], CF[:, 0:1], None, OP.is_equal)
+    if r == 0:
+        c_k1 = ts([], CO[:, 6:7], CF[:, 1:2], 1.0, None, OP.add)
+        c_g8 = ts([], CO[:, 3:4], CF[:, 0:1], 8.0, None, OP.mult)
+    m_sy = ts([l_sy], T.syb[:], T.syr[:], 1.0 / 32, -0.25, OP.mult, OP.add)
+    ne = ts([c_17], CI[:, 2:3], T.pci[:, 1:2], 4, 1, OP.arith_shift_right, OP.bitwise_and)
+    c_mask = ts([c_row], T.mask[:, 0:16], T.rowf[:, 0:16], CF[:, 1:2], None, OP.is_equal)
+    c_k8 = ts([ne, c_k1], CO[:, 8:9], CI[:, 2:3], 17.0, CO[:, 6:7], OP.mult, OP.add)
     K = {"pm": None}
+    am = T.py[:, 64:80] if r else T.pew[:, 304:320]
 
     def symbols():
         do("t", [c_bo], lambda: mm(T.px[:, 0:128], T.bo[:], T.bo[:], True, False))
         K["x"] = do("t", [m_sy, c_six], lambda: mm(T.px[:, 0:128], T.six[:], T.syb[:], False, True))
-
-    def columns():
-        K["sf"] = do("v", [l_sc], lambda: vec.tensor_copy(CO[:, 3:4], T.syc[:]))
-        K["k9"] = ts([c_k8], CO[:, 9:10], CO[:, 8:9], 1.0 / 16, None, OP.add)
-    if r == 0:
-        symbols()
-    m_ta = ts([l_nx], T.ti[:, 0:128], T.nxi[:, 0:128], 511, None, OP.bitwise_and)
-    m_ti = ts([], T.ti[:, 128:256], T.nxi[:, 128:256], 511, None, OP.bitwise_and)
     if r > 0:
-        columns()
-    am = T.py[:, 64:80] if r else T.pew[:, 304:320]
+        do("t", [c_evl, c_six], lambda: mm(T.pc[:, 0:128], T.six[:], T.evl[:], True, False))
+        WB = (T.pwa, T.pwb, T.pcm, T.pew)
+        for x in range(4):
+            do("t", [c_ramp[x]], lambda: mm(WB[x][:, 0:128], T.evl[:], T.ramp[:, 128 * x:128 * x + 128], True, False))
+        do("t", [c_bo], lambda: mm(T.pc[:, 0:128], T.bo[:], T.bo[:], False, False))
+        m_o = do("t", [m_sy], lambda: mm(T.pc[:, 0:128], T.six[:], T.syb[:], False, True))
+    else:
+        symbols()
+    for x in range(8):
+        m_am = do("t", [c_ind], lambda: mm(am, T.ind[:, 112 - 16 * x:240 - 16 * x], T.syb[:, 16 * x:16 * x + 16], x == 0, x == 7))
 
     def select(out, X, h, deps):
         return ts(deps, out[:, 128 * h:128 * h + 128], X[:, 0:128], float(h), CF[:, 1:2], OP.add, OP.is_equal)
-
-    def own_symbol():
-        K["d16"] = ts([K["sf"], c_mask], T.d16[:], T.mask[:], CO[:, 3:4], 0.125, OP.mult, OP.mult)
-
-    def group_symbols():
-        K["am"] = do("t", [K["d16"]], lambda: mm(am, T.bo[:], T.d16[:], True, True))
     so, po, mo = (T.selo, T.pc, m_o) if r > 0 else (T.sel, T.px, K["x"])
-    m_s0 = select(so, po, 0, [mo])
+    m_ta = ts([l_nx], T.ti[:, 0:128], T.nxi[:, 0:128], 511, None, OP.bitwise_and)
+    m_ti = ts([], T.ti[:, 128:256], T.nxi[:, 128:256], 511, None, OP.bitwise_and)
     if r > 0:
-        own_symbol()
-        group_symbols()
+        c_k9 = ts([c_k8], CO[:, 9:10], CO[:, 8:9], 1.0 / 16, None, OP.add)
+    m_s0 = select(so, po, 0, [mo])
     m_t0 = ts([m_ta], T.tq[:, 16:144], T.ti[:, 0:128], -256.0, None, OP.add)
     m_tb = ts([m_ti], T.tq[:, 144:272], T.ti[:, 128:256], -256.0, None, OP.add)
     m_s1 = select(so, po, 1, [])
-    turn = [lambda: do("v", [m_tb], lambda: vec.transpose(T.tab[:, 0:256], T.tq[:, 16:272])),
-            lambda: do("v", [], lambda: vec.transpose(T.tab[:, 256:544], T.tq[:, 0:288])),
-            lambda: ts([K["am"], K["k9"]], T.ot[:, 0:32:2], am, CO[:, 8:9], 16.0, OP.add, OP.mult),
-            lambda: K.update(tab=ts([], T.ot[:, 1:32:2], am, CO[:, 9:10], 16.0, OP.add, OP.mult))]
+    if r == 0:
+        c_k9 = ts([c_k8], CO[:, 9:10], CO[:, 8:9], 1.0 / 16, None, OP.add)
+    turn = [lambda: ts([m_am, c_k9], T.ot[:, 0:32:2], am, CO[:, 8:9], 16.0, OP.add, OP.mult),
+            lambda: ts([], T.ot[:, 1:32:2], am, CO[:, 9:10], 16.0, OP.add, OP.mult),
+            lambda: do("v", [m_tb], lambda: vec.transpose(T.tab[:, 0:256], T.tq[:, 16:272])),
+            lambda: K.update(tab=do("v", [], lambda: vec.transpose(T.tab[:, 256:544], T.tq[:, 0:288])))]
     if r > 0:
         turn.append(lambda: K.update(pm=tten([c_mask], T.pm[:, 1:16], T.mask[:, 1:16], T.mask[:, 0:15], OP.add)))
-    else:
-        columns()
-        turn[0]()
-        own_symbol()
 
     def identity():
         K["idn"] = do("p", [c_bo], lambda: g.affine_select(T.idn[:], T.bo[:], [[1, 128]], OP.is_equal, 0.0, 0, -1))
 
-    def late_constants():
-        x = do("p", [], lambda: g.iota(T.mg[:], [[4, 4], [0, 8]], -13, 0, **lo))
-        K["tri"] = do("p", [c_bo], lambda: g.affine_select(T.tri[:], T.bo[:], [[1, 128]], OP.is_gt, 0.0, 0, -1))
-        x = do("p", [x], lambda: g.affine_select(T.tho[:], T.mg[:], [[0, 4], [-16, 8]], OP.is_ge, 256.0, 0, 1))
-        K["pl"] = do("p", [], lambda: g.iota(T.plb[:], [[2, 36]], 64 * r - 6, 0, **lo))
-        K["late"] = do("p", [x], lambda: g.affine_select(T.thg[:], T.tho[:], [[0, 4], [16, 8]], OP.is_ge, 256.0, 15, -1))
+    def late_constants(part):
+        if part == 0:
+            K["mg"] = do("p", [], lambda: g.iota(T.mg[:], [[2, 4], [0, 8]], 261, 0, **lo))
+            do("p", [], lambda: g.iota(T.pl[:], [[int(UNIT), 36]], int(UNIT) * (32 * r - 3), 0, **lo))
+        if part == 1:
+            K["mg"] = do("p", [K["mg"]], lambda: g.affine_select(T.tho[:], T.mg[:], [[0, 4], [-16, 8]], OP.is_ge, 1024.0, 0, 1))
+            do("p", [c_bo], lambda: g.affine_select(T.tri[:], T.bo[:], [[1, 128]], OP.is_gt, 0.0, 0, -1))
+        if part == 2:
+            K["late"] = do("p", [K["mg"]], lambda: g.affine_select(T.thg[:], T.tho[:], [[0, 4], [16, 8]], OP.is_ge, 1024.0, 15, -1))
 
-    def digit_list():
+    def small_constants():
         def a():
             K["up"] = ts([], CO[:, 5:6], CF[:, 1:2], 8.0, None, OP.is_ge)
-            K["far"] = ts([c_mask], T.far[:], T.mask[:], -1.0, 256 * CODE, OP.add, OP.mult)
+            K["m16"] = do("v", [c_mask], lambda: vec.tensor_copy(T.mask[:, 16:17], T.mask[:, 0:1]))
+            if r != 2:
+                x = 8 * min(r, 2) + 1
+                do("v", [], lambda: vec.memset(T.cn[:, x:x + 1], 0.0))
 
         def b():
-            ts([K["up"]], T.l32[:], T.rowf[:, 0:12:2], CO[:, 5:6], None, OP.add)
-            ts([K["pl"]], T.pl[:], T.plb[:], CODE, None, OP.mult)
+            ts([K["up"]], T.l32[:], T.rowf[:, 0:8:2], CO[:, 5:6], None, OP.add)
+            K["dn"] = ts([K["m16"]], T.dn[:, 0:16], T.mask[:, 1:17], BASE - 255.75, None, OP.mult)
         return [a, b]
 
+    def row_numbers():
+        K["idx"] = ts([l_sc, c_g8], T.idx[:], T.syc[:], CO[:, 3:4], None, OP.add)
 
-    def code_window(x, EB, d_nx, d_em, d_sel):
-        nxi, emi, sel, emf, za, self_, e, hi, ci = [T[n + x] for n in ("nxi", "emi", "sel", "emf", "za", "self", "e", "hi", "ci")]
-        pb = T.pc if x else T.pb
-        C = {("sel", 1): d_sel}
-
-        def part(kind, h):
-            c = slice(128 * h, 128 * h + 128)
-            u = slice(256 + 128 * h, 384 + 128 * h)
-
-            def f():
-                if kind == "sel":
-                    d = select(sel, T.px, h, [K["x"]])
-                elif kind == "em":
-                    d = ts([d_em], emf[:, c], emi[:, c], 1.0 / CODE, -8.0, OP.mult, OP.add)
-                elif kind == "hi":
-                    d = ts([d_em], hi[:, c], emi[:, c], 18, None, OP.arith_shift_right)
-                elif kind == "top":
-                    d = ts([d_nx], pb[:, c], nxi[:, c], 2048.0, 64.0, OP.is_lt, OP.mult)
-                elif kind == "ci":
-                    d = ts([d_nx], ci[:, c], nxi[:, c], 8, 14, OP.arith_shift_right, OP.bitwise_and)
-                elif kind == "min":
-                    d = tten([C["hi", h], C["top", h]], pb[:, u], hi[:, c], pb[:, c], OP.min)
-                else:
-                    d = tten([C["min", h], C["ci", h]], za[:, c], ci[:, c], pb[:, u], OP.subtract)
-                C[kind, h] = d
-            return f
-
-        def wide():
-            C["self"] = do("s", [C["sel", 1]], lambda: act(self_[:], sel[:], AF.Copy))
-
-        def numbers(hs=(0, 1)):
-            for h in hs:
-                do("t", [C["self"], C["em", 1]], lambda: mm(EB[h][:, 0:256], self_[:, 128 * h:128 * h + 128], emf[:], True, False))
-
-        def counts(hs=(0, 1)):
-            for h in hs:
-                C["eb", h] = do("t", [C["za", 1]], lambda: mm(EB[h][:, 0:256], sel[:, 128 * h:128 * h + 128], za[:], False, True))
-
-        def out(then=None, hs=(0, 1)):
-            for h in hs:
-                c = slice(256 * h, 256 * h + 256)
-                if x and h:
-                    d = ts([C["eb", h]], e[:, c], EB[h][:, 0:256], CODE, None, OP.mult)
-                else:
-                    d = do("s", [C["eb", h]], lambda: act(e[:, c], EB[h][:, 0:256], AF.Copy, scale=CODE))
-                if then:
-                    then(c, d)
-            return d
-        kinds = ([] if d_sel else ["sel"]) + ["em", "hi", "top", "ci", "min", "za"]
-        return [part(kind, h) for kind in kinds for h in range(2)], wide, numbers, counts, out, C
-
-    parts, code_sel, code_numbers, code_counts, code_out, CW = code_window("", (T.pew, T.px), l_nx, l_em, None if r else m_s1)
+    def fetch(out=T.cw, rows=T.tbd, idx=T.idx, deps=None, sn="lcw"):
+        waits("p", deps or [K["idx"], l_tb])
+        g.indirect_dma_start(out[:], None, rows[:], IndirectOffsetOnAxis(ap=idx[:], axis=0), bounds_check=63).then_inc(T.sem[sn], 16)
+        cnt[sn] = 16
+    own_codes = (T.cw[:, 0:512], T.cw[:, 512:1024], [("lcw", 16)])
 
     def window(to):
         for x in range(4):
@@ -297,11 +252,9 @@ def rank_program(g, core, T, topo):
             d = do("t", [m_s1 if h else m_s0, m_tb if u else m_t0], lambda: mm(
                 WB[x][:, 0:128], T.selo[:, 128 * h:128 * h + 128], T.tq[:, 16 + 128 * u:144 + 128 * u], False, True))
             d = do("s", [d], lambda: act(T.w[:, 128 * x:128 * x + 128], WB[x][:, 0:128], AF.Copy))
-        symbols()
         if to is not None:
             send([d], [to], T.w1[:], T.w[:], "aw1")
         return d
-
 
     def lists(segs):
         def one(j, n):
@@ -315,33 +268,43 @@ def rank_program(g, core, T, topo):
 
     slot = [0]
 
-    def joins(seg, plus=None, masked=True):
+    def joins(seg, plus=None, masked=True, foreign=False, last=None):
         j, n, qn = seg
-        box = [T.w[:], K["w"]]
+        owner = {0: 1, 1: 3, 3: 2}.get(r)
+        box = [T.w1[:], arrive(owner, "aw1", "apart")] if foreign else [T.w[:], K["w"]]
 
         def one(i):
             def f():
                 x = slot[0]
                 out = T.cp[:, 512 * x:512 * x + 512]
                 slot[0] += 1
-                src = box[0].indirect(T.lt[:, 32 * i:32 * i + 32])
+                src = box[0].indirect((T.ltx if foreign else T.lt)[:, 32 * i:32 * i + 32])
                 keep = T.pm[:, j + n - 1:j + n] if masked and i == (j + n - 2 if plus else j) else 1.0
-                deps = [box[1], K["lt", i], K["pm"]]
+                deps = [box[1], arrive(owner, "alt", "apart") if foreign else K["lt", i], K["pm"]]
                 if plus and i == j:
                     y, e = K["join", plus[0]]
                     d = tten(deps + [e], T.cpm[:] if r == 1 else out, src, T.cp[:, 512 * y:512 * y + 512], OP.add)
-                elif qn == "v":
+                elif (last if last and i == j else qn) == "v":
                     d = ts(deps, out, src, keep, None, OP.mult)
                 else:
                     d = do("s", deps, lambda: act(out, src, AF.Copy, scale=keep))
                 box[0], box[1] = out, d
                 if i == j:
-                    K["join", j] = (x, d)
+                    K["join", j + 16 * foreign] = (x, d)
             return f
         return [one(i) for i in range(j + n - 2, j - 1, -1)]
 
+    def in_pieces(j, deps):
+        x = slot[0]
+        slot[0] += 1
+
+        def one(a, n):
+            return lambda: K.update({("join", j): (x, ts(deps + [K["lt", j]], T.cp[:, 512 * x + 16 * a:512 * x + 16 * (a + n)],
+                                                         T.w[:].indirect(T.lt[:, 32 * j + a:32 * j + a + n]), 1.0, None, OP.mult))})
+        return [one(sum(PIECES[:i]), PIECES[i]) for i in range(len(PIECES))]
+
     def merge_constants():
-        ends = [T.pm[:, j + n - 1:j + n] for j, n, _ in long]
+        ends = [T.pm[:, j + n - 1:j + n] for j, n, qn in long if qn != "1"]
 
         def three():
             out = CO[:, 10 + len(ends):11 + len(ends)]
@@ -361,9 +324,13 @@ def rank_program(g, core, T, topo):
 
     MB = (T.pcm, T.pc)
 
-    def table(seg):
+    def table(seg, rows=slice(None)):
         x = K["join", seg[0]][0]
-        return T.cp[:, 512 * x:512 * x + 512]
+        return T.cp[rows, 512 * x:512 * x + 512]
+
+    def own_table(seg, foreign=False):
+        x, d = K["join", seg[0] + 16 * foreign]
+        return seg[:2] + (T.cp[:, 512 * x:512 * x + 512], [d])
 
     def merge_add(lhs, src, x, deps, first=False, last=False):
         return [do("t", deps, lambda: mm(MB[h][:, 0:256], lhs[:], src[:, x + 256 * h:x + 256 * h + 256], first, last))
@@ -390,14 +357,42 @@ def rank_program(g, core, T, topo):
                     out.append(x.pop(0))
         return out
 
-    free_col = [16]
+    free = {"tt": 16, "tu": 16}
 
-    def gather(win, at, deps, k):
-        col = free_col[0]
-        free_col[0] += 32
-        b = col - k
-        tile, x0, d = at
-        return (T.tt, col, ts([d] + deps, T.tt[:, b:b + 16], win.indirect(tile[:, x0:x0 + 1]), 256.0, None, OP.add))
+    def column(tile):
+        free[tile] += 32
+        return free[tile] - 32
+
+    def gather(win, at, deps, k, keep=None, col=None):
+        tile = T.tt if keep else T.tu
+        col = col or column(tile.name)
+        out, src = tile[:, col - k:col - k + 16], win.indirect(at[0][:, at[1]:at[1] + 1])
+        if keep:
+            K["col", col] = ts([at[2], keep[1]] + deps, out, src, 256.0, keep[0], OP.add, OP.mult)
+            return (tile, col, K["col", col])
+        return (tile, col, ts([at[2]] + deps, out, src, 256.0, None, OP.add))
+
+    def only(i):
+        return (T.mask[:, i:i + 1], c_mask)
+
+    def merged_constants(qs):
+        def one(n):
+            return lambda: K.update({("vm", n): tten([K["pm"]], T.vm[:, 16 * n + n - 1:16 * n + 16], T.pm[:, n - 1:16],
+                                                     T.mask[:, 0:17 - n], OP.add)})
+        return [one(n) for n in sorted({n for q in qs for n, _ in SEGS[q] if n > 2})]
+
+    def merged(j, n):
+        e = j + n - 1
+        if n == 1:
+            return only(j), []
+        keep = (T.pm[:, e:e + 1], K["pm"]) if n == 2 else (T.vm[:, 16 * n + e:16 * n + e + 1], K["vm", n])
+        return keep, range(j + 1, e - 1)
+
+    def last_two(j, n):
+        e = j + n - 1
+        if n == 1:
+            return only(j), []
+        return (only(14) if e == 15 else (T.pm[:, e:e + 1], K["pm"])), range(j, e - 1)
 
     def plan(q, plain, joined):
         out, segs = [], segments(q)
@@ -406,84 +401,121 @@ def rank_program(g, core, T, topo):
             out.append(segs[m][:2] + (plain if segs[m][1] == 1 else joined[x]))
         return out
 
-    def string(segs, at, inner, hooks, start=0):
-        reads, late = {segs[start][0]: at}, []
-        for m in range(start, len(segs)):
+    def string(segs, at, gives, single_window, hooks, onward=None):
+        reads, late = {segs[0][0]: at}, []
+        for m in range(len(segs)):
             j, n, win, deps = segs[m]
-            at = gather(win, at, deps, (j - 1) % 16)
-            for i in range(j, j + n):
-                reads[i + 1] = at
-            steps, single = inner(j, n) if inner else ([], None)
+            keep, steps = gives(j, n) if gives else (None, [])
+            before, k = at, (j - 1) % 16
+            behind = onward is not None and m == len(segs) - 1 and keep and r == 2 and OPT["behind"]
+            if onward is not None and m == len(segs) - 1:
+                if not behind:
+                    at = made = gather(win, before, deps, k, only(15), onward)
+                if keep:
+                    made = gather(win, before, deps, k, keep)
+            else:
+                at = made = gather(win, before, deps, k, keep)
+            if gives:
+                for i in range(j, j + n):
+                    reads[i + 1] = made
             row = [] if j in steps else [None]
             for i in steps:
-                def f(i=i, single=single):
-                    reads[i + 1] = gather(single, reads[i], [], (i - 1) % 16)
+                def f(i=i):
+                    reads[i + 1] = gather(single_window, reads[i], [], (i - 1) % 16, only(i))
                 row.append(f)
-            late = [x for x in late + [row] if x]
+            late = [x for x in [row] + late if x]
             play([f for f in [x.pop(0) for x in late] if f])
+            if behind:
+                at = gather(win, before, deps, k, only(15), onward)
             play(hooks.get(m, []))
-        return reads, at, [f for f in weave(*late) if f]
-
-    def code_at(qn, reads, j, ewin, edep, ee):
-        tile, x0, d = reads[j]
-        b = 0 if j == 0 else 16 * j + 16
-        out, src = ee[:, b:b + 16], ewin[:].indirect(tile[:, x0:x0 + 1])
-        if qn == "v":
-            return ts([d, edep, K["far"]], out, src, T.far[:, j:j + 1], None, OP.add)
-        return do("s", [d, edep, K["far"]], lambda: act(out, src, AF.Identity, bias=T.far[:, j:j + 1]))
-
-    def follow(reads, ewin, edep, ee, on_v):
-        steps = sorted(range(16), key=lambda j: reads[j][2][1] if j else 0)
-        return [[code_at(qn, reads, j, ewin, edep, ee) for j in part][-1]
-                for qn, part in (("s", steps[:16 - on_v]), ("v", steps[16 - on_v:])) if part]
+        return at, [f for f in weave(*late) if f]
 
     cd, gd = {}, {}
     ydep = [None, 0]
-    SLOT = (0, 2, 0, 1)
 
-    def buf(name, q, n, count=1):
-        return T[name + "abbb"[q]][:, n * SLOT[q]:n * (SLOT[q] + count)]
+    def pair(q):
+        return (T.rc0[:], T.rc1[:], T.rcb[:, 0:2], T.rcb[:, 4:6])[q]
 
-    def code(q):
-        return T["rc" + "abbb"[q]][:, 4 * SLOT[q]:4 * SLOT[q] + 1]
+    def numbers(q):
+        return (T.rc0[:, 1:2], T.rc1[:, 1:2], T.rcb[:, 1:2], T.rcb[:, 5:6])[q]
 
-    def whole(q):
-        K["qi", q] = do("v", [cd[q]], lambda: vec.tensor_copy(buf("qi", q, 1), code(q)))
+    def codes(q, first, count, wins, sent):
+        nxw, emw, deps = wins
+        at = T.all[:, 2 * q:2 * q + 1]
+        en, ee = [T["e%d" % q][:, x:x + (32 if q == 3 else 16)] for x in (0, 32 if q == 3 else 16)]
 
-    def total(q, ee, last):
-        def one(out):
-            return do("v", last, lambda: vec.tensor_reduce(out, ee if q > 1 else ee[:, 15:271:17], AxisListType.X, OP.max))
-        if r > 1:
-            K["qi", q] = one(buf("qi", q, 1))
-        cd[q] = one(code(q))
-        if r < 2:
-            K["qi", q] = one(buf("qi", q, 1))
+        def top(d, out, src):
+            return do("v", [d], lambda: vec.tensor_reduce(out, src, AxisListType.X, OP.max))
+
+        def bring():
+            waits("v", [K.get(("col", first + 32 * n)) for n in range(count)])
+            K["all", q] = top(None, at, T.tt[:, first:first + 32 * count:32])
+
+        def pick(end=None):
+            ones, base = (T.mask[:, 1:17], T.dn[:, 0:16]) if q < 3 else (T.dm[:, 16:32], T.dn[:, 32:48])
+            if end:
+                src = end[0][:, end[1]:end[1] + 1]
+                tten([end[2], K["dn"]] + deps, ee[:, 16:32], emw.indirect(src), T.dm[:, 0:16], OP.mult)
+                tten([], en[:, 16:32], nxw.indirect(src), T.dn[:, 16:32], OP.add)
+            for x in ("en", "ee") if sent else ("ee", "en"):
+                if x == "ee":
+                    K[x, q] = tten([K["all", q], K["dn"]] + deps, ee[:, 0:16], emw.indirect(at), ones, OP.mult)
+                else:
+                    K[x, q] = tten([K["all", q], K["dn"]] + deps, en[:, 0:16], nxw.indirect(at), base, OP.add)
+
+        def keep():
+            if sent:
+                gd[q] = top(K["en", q], count_of(q), en)
+            cd[q] = top(K["ee", q], numbers(q), ee)
+            if sent:
+                K["sent", q] = top(K["en", q], pair(q)[:, 0:1], en)
+            else:
+                gd[q] = top(K["en", q], count_of(q), en)
+        return [bring, pick, keep]
+
+    def last_masks():
+        j, n = segments(3)[-1][:2]
+
+        def a():
+            K["dm"] = do("v", [], lambda: vec.memset(T.dm[:, 0:16], 0.0))
+
+        def b():
+            K["dm"] = do("v", [K["dm"]], lambda: vec.tensor_copy(T.dm[:, j:j + n], T.mask[:, j + 1:j + n + 1]))
+
+        def c():
+            K["dm"] = tten([K["dm"], K["m16"]], T.dm[:, 16:32], T.mask[:, 1:17], T.dm[:, 0:16], OP.subtract)
+
+        def d():
+            K["dn"] = ts([K["dm"]], T.dn[:, 16:48], T.dm[:], BASE - 255.75, None, OP.mult)
+        return [a, b, c, d]
+
+    def count_of(q, n=1):
+        return T.cn[:, 8 * q:8 * q + n]
 
     def gates(q):
-        src, d = (T.q2[:], K["qi", q]) if (r, q) == (1, 2) else (code(q), cd[q])
-        gd[q] = ts([d], buf("cn", q, 1), src, 0.0, 263.5 * CODE, OP.min, OP.add)
+        gd[q] = ts([cd[q]], count_of(q), pair(q)[:, 0:1], 0.25, None, OP.add)
 
     def spread(q):
-        K["gg", q] = do("s", [cd[q], K["late"]], lambda: act(buf("gg", q, 32), T.thg[:], AF.Relu, bias=code(q), scale=-CODE / 2))
+        K["gg", q] = do("s", [gd[q], K["late"]], lambda: act(T.gg[:, 32 * q:32 * q + 32], T.thg[:], AF.Relu,
+                                                             bias=count_of(q), scale=-UNIT / 2))
 
-    def digits(qs, ep):
-        n, a = len(qs), 4 * SLOT[qs[0]]
-        qi, di, b = T.q2[:] if (r, qs[0]) == (1, 2) else buf("qi", qs[0], 1, n), T["di" + "abbb"[qs[0]]], a + 4 * n
+    def digits(qs):
+        n = len(qs)
+        qi = numbers(qs[0])
+        di, ep = (T.di0, T.di1, T.dib, T.di0)[qs[0]], (T.ep0, T.ep1, T.epb, T.ep0)[qs[0]]
 
         def low():
-            ts([K["qi", q] for q in qs], di[:, a:b:4], qi, 63, None, OP.bitwise_and)
+            ts([cd[q] for q in qs], di[:, 0:4 * n:4], qi, 63, None, OP.bitwise_and)
 
         def high():
-            ts([], di[:, a + 1:b:4], qi, 6, 63, OP.arith_shift_right, OP.bitwise_and)
-            ts([], di[:, a + 2:b:4], qi, 12, 63, OP.arith_shift_right, OP.bitwise_and)
-            K["di"] = ts([], di[:, a + 3:b:4], qi, 18, 63, OP.arith_shift_right, OP.bitwise_and)
+            for m in (1, 2, 3):
+                K["di"] = ts([], di[:, m:4 * n:4], qi, 6 * m, 63, OP.arith_shift_right, OP.bitwise_and)
 
-        def used(i):
-            def f():
-                K["ep", qs[i]] = tten([K["di"], K["gg", qs[i]]], ep[:, 32 * i:32 * i + 32],
-                                      di[:, a:b].indirect(T.l32[:, 2 * i:2 * i + 2]), buf("gg", qs[i], 32), OP.min)
-            return f
-        return [low, high] + [used(i) for i in range(n)]
+        def used():
+            d = tten([K["di"]] + [K["gg", q] for q in qs], ep[:, 0:32 * n], di[:, 0:4 * n].indirect(T.l32[:, 0:2 * n]),
+                     T.gg[:, 32 * qs[0]:32 * (qs[0] + n)], OP.min)
+            K.update({("ep", q): d for q in qs})
+        return [low, high, used]
 
     places = {q: (T.pb, T.pc, T.pwa, T.pb)[q][:, 0:1] for q in range(max(r - 1, 0), min(r + 2, 4))}
     sums = {q: [T.tri[:]] + [T.bo[:]] * q for q in places}
@@ -497,256 +529,275 @@ def rank_program(g, core, T, topo):
                 do("t", [K["late"]] + deps, lambda: mm(places[q], sums[q][n], T.off[:], n == 0, False))
 
     def tally(b):
-        gates(b)
         for q in places:
             if q == "Z" or q >= b:
                 missing[q] -= 1
-                K["at", q] = do("t", [gd[b]], lambda: mm(places[q], sums[q][0 if q == b else -1], buf("cn", b, 1), False, not missing[q]))
+                K["at", q] = do("t", [gd[b]], lambda: mm(places[q], sums[q][0 if q == b else -1], count_of(b), False, not missing[q]))
 
     def hot(q):
         K["oh", q] = ts([K["at", q]], T["oh%d" % q][:], T.pl[:], places[q], None, OP.is_equal)
 
-    def alone(q, out, final):
-        D = digits([q], out)
+    def add(q, final=False, deps=None):
+        src, x = (T.ep0, T.ep1, T.epb, T.ep0)[q], 0
+        for m in range(4):
+            ydep[0] = do("t", [K["oh", q]] + (deps or [K["ep", q]]), lambda: mm(
+                T.py[0:8, 0:32], src[:, x + 8 * m:x + 8 * m + 8], T["oh%d" % q][:, 3 - m:35 - m], ydep[1] == 0, final and m == 3))
+            ydep[1] += 1
+
+    def alone(q, final):
+        D = digits([q])
         tally(q)
         spread(q)
         play(D[:2])
         hot(q)
         D[2]()
-        add(q, out, 0, [K["ep", q]], final)
+        add(q, final)
 
-    def add(q, src, x, deps, final=False):
-        for m in range(4):
-            ydep[0] = do("t", [K["oh", q]] + deps, lambda: mm(
-                T.py[0:8, 0:32], src[:, x + 8 * m:x + 8 * m + 8], T["oh%d" % q][:, 3 - m:35 - m], ydep[1] == 0, final and m == 3))
-            ydep[1] += 1
+    def with_joined(steps, plain, segs, foreign=False):
+        out, at = [], {s[0]: s for s in segs}
+        for j in steps:
+            if j in at:
+                out.append(own_table(at[j], foreign))
+            elif not out or j >= out[-1][0] + out[-1][1]:
+                out.append((j, 1) + plain)
+        return out
 
+    def other_tables(x):
+        K["tbx"] = dma("y", [arrive(5 - r, ("anx", "aem")[x])], "ltx", T.tbx[:, 512 * x:512 * x + 512], (T.nxd, T.emd)[x][:])
+
+    def fetch_other():
+        fetch(T.cwx, T.tbx, T.idy, [arrive(5 - r, "aidx"), K["tbx"]], "lcx")
+
+    sc = small_constants()
     if r == 0:
-        wdep = [None, None]
+        for x in range(3):
+            late_constants(x)
+        row_numbers()
+        fetch()
+        if OPT["relay"]:
+            send([arrive(2, "awr", "apart")], [3], T.w1[:], T.wr[:], "aw1")
+        play(turn[2:] + turn[:2])
+        K["tab"] = ("v", cnt["v"])
+        wdep = {}
         for x in range(4):
             h, u = x // 2, x % 2
             bank, out = (T.pwa, T.pwb, T.pcm, T.py)[x][:, 128:256], T.w[:, 128 * x:128 * x + 128]
             d = do("t", [m_s1 if h else m_s0, m_tb if u else m_t0], lambda: mm(
                 bank, T.sel[:, 128 * h:128 * h + 128], T.tq[:, 16 + 128 * u:144 + 128 * u], True, True))
-            wdep[u] = do("s", [d], lambda: act(out, bank, AF.Copy)) if u else do("v", [d], lambda: vec.tensor_copy(out, bank))
-            if x == 0:
-                at = (T.s1, 0, ts([], T.s1[:], T.pwa[:, 128:130], 256.0, None, OP.add))
-        group_symbols()
-        play(turn[1:3])
-        late_constants()
-        code_sel()
+            wdep[x] = do("v", [d], lambda: vec.tensor_copy(out, bank)) if x == 2 else do("s", [d], lambda: act(out, bank, AF.Copy))
+        c = column("tt")
+        at = (T.tt, c, ts([c_mask, wdep[0]], T.tt[:, c:c + 1], T.w[:, 0:1], 256.0, T.mask[:, 0:1], OP.add, OP.mult))
+        wdep = [wdep[2], wdep[3]]
         waits("s", wdep)
         K["w"] = wdep[0]
-        parts3, sel3, numbers3, counts3, out3, _ = code_window(
-            "x", (T.pwa, T.pwb), arrive(3, "anx"), arrive(3, "aem"), arrive(3, "asel"))
-        dl = digit_list()
-        j = LAST[0]
-        fill = parts[:1] + lists([LAST]) + parts[1:] + parts3[:4] + parts3[4:]
-        hooks = {n + 1: [fill[n]] for n in range(j - 1)}
-        hooks[1].insert(0, turn[3])
-        hooks[2] += joins(LAST, None, False)
-        hooks[3] += [code_numbers] + dl[:1]
-        reads, at1, _ = string(plan(0, (T.w[:], wdep), [None])[:j], at, None, hooks, 1)
-        more, at1, late = string([LAST[:2] + (table(LAST), [K["join", j][1]])], at1, lambda j, n: (range(j, j + n - 1), T.w[:]), {})
-        reads.update({i: more[i] for i in more if i})
-        reads[0], reads[1] = (T.zero, 0, c_zero), at
-        send([at1[2]], [1], T.s1[:], T.tt[:, at1[1]:at1[1] + 2], "as1")
-        fill = fill[j - 1:]
-        x = 14 - j
-
-        def codes0():
-            reads.update({i: more[i] for i in more if i})
-            code_counts()
-            sel3()
-            K["last"] = follow(reads, T.e, code_out(), T.eea, 0)
-        hooks = {n: [fill[n]] for n in range(single)}
-        hooks[0] += late
-        hooks[x - 1].append(codes0)
-        hooks[x + 1].append(numbers3)
-        at = string(plan(1, (T.w1[:], [arrive(1, "aw1")]), [(None, None)])[:single], at1, None, hooks)[1]
-        send([at[2]], [2, 3], T.s1[:], T.tt[:, at[1]:at[1] + 2], "as1")
-        play(fill[single:] + [counts3])
-        total(0, T.eea, K["last"])
-        send([cd[0]], [2, 3, 1], code(0), code(0), "arc0", "apart")
-        out3(lambda c, d: send([d], [2], T.ex[:, c], T.ex[:, c], "aex", "wide"))
-        dl[1]()
+        first, S = ZERO[0], [s for s in ZERO if s[2] == "s"]
+        play(lists(S[:1]) + joins(S[0], None, False))
+        hooks = {n: [] for n in range(first[0])}
+        for n, s in enumerate(S[1:]):
+            hooks[n] += lists([s]) + joins(s, None, False)
+        hooks[n] += [f for s in ONE for f in joins(s, None, False, True)]
+        for s in ZERO:
+            if s[2] == "v":
+                hooks[0] = lists([s]) + hooks[0]
+                for n, f in enumerate(in_pieces(s[0], wdep)):
+                    hooks[first[0] - 1 - len(PIECES) + n].append(f)
+        at = string(with_joined(range(1, first[0]), (T.w[:], wdep), []), at, lambda j, n: (only(j), []), None, hooks)[0]
+        at1, late = string(with_joined(range(first[0], 16), (T.w[:], []), ZERO), at,
+                           lambda j, n: (only(j + n - 1) if j + n < 16 else None, range(j, j + n - 1)), T.w[:],
+                           {0: sc[:1], 1: sc[1:]}, 16 + 32 * 15)
+        send([at1[2]], [1], T.tt[:, 16:18], T.tt[:, at1[1]:at1[1] + 2], "as1")
+        c0 = codes(0, 16, 15, own_codes, True)
+        segs = with_joined(range(single), (T.w1[:], [arrive(1, "aw1")]), ONE, True)
+        fill = [[f] for f in late] + [c0[:1]]
+        if OPT["early"]:
+            fill += [c0[1:2], c0[2:] + [lambda: send([gd[0]], [2], count_of(0, 2), count_of(0, 2), "acn0", "apart")]]
+        at = string(segs, at1, None, None, dict(enumerate(fill[:len(segs)])))[0]
+        send([at[2]], OPT["order"], T.s1[:], T.tu[:, at[1]:at[1] + 2], "as1", OPT["state"])
+        for x in fill[len(segs):]:
+            play(x)
+        if not OPT["early"]:
+            play(c0[1:])
+        send([gd[0]], [3] if OPT["early"] else [2, 3], count_of(0, 2), count_of(0, 2), "acn0", "apart")
+        send([K["sent", 0]], [1], pair(0), pair(0), "arc0")
         begin([])
-        alone(0, T.epa, False)
+        alone(0, False)
         cd[1] = arrive(1, "arc1")
-        whole(1)
-        alone(1, T.epb, True)
+        gates(1)
+        alone(1, True)
     else:
-        mc, diagonal = merge_constants()
-        if r == 3:
-            send([l_nx], [0], T.nxix[:], T.nxi[:], "anx")
-            send([l_em], [0], T.emix[:], T.emi[:], "aem")
-        else:
+        late_constants(0)
+        if r == 3 or r == 2 and OPT["t2"]:
+            send([l_nx], [5 - r], T.nxd[:], T.nxi[:], "anx")
+        late_constants(1)
+        if r == 3 or r == 2 and OPT["t2"]:
+            send([l_em], [5 - r], T.emd[:], T.emi[:], "aem")
+        late_constants(2)
+        if r == 3 and not OPT["patch"]:
             identity()
-        to = {1: 0, 2: 3, 3: 2}[r]
-        K["w"] = window(to if r < 3 else None)
-        if r == 2:
-            late_constants()
+        if r == 2 or r == 3 and not OPT["patch"]:
+            other_tables(0)
+            other_tables(1)
+        both = segments(2)[-2:]
+        end = [s for s in segments(3) if s[2] == "1"][0][:2] + ("s",)
         on = {qn: [s for s in long if s[2] == qn] for qn in "sv"}
         S, V = on["s"], on["v"]
-        play(turn)
-        js = weave(*[joins(s) for s in S])
+        K["w"] = window(None)
+        play(turn + [row_numbers])
+        if r == 3 or r == 2 and OPT["t2"]:
+            send([K["idx"]], [5 - r], T.idy[:], T.idx[:], "aidx")
+        if r == 2 and OPT["relay"]:
+            send([K["w"]], [0], T.wr[:], T.w[:], "awr", "apart")
+        else:
+            send([K["w"]], [{1: 0, 2: 3, 3: 1}[r]], T.w1[:], T.w[:], "aw1", "apart")
+
+        def ahead(segs):
+            cut = [(j, j + n - 2 - (qn == "v"), j + n) for j, n, qn in segs]
+            return lists([(b, c - b, "") for _, b, c in cut]), lists([(a, b + 1 - a, "") for a, b, _ in cut])
         if r == 1:
-            jv = joins(V[0], S[0])
-            n = 4
-            play(lists(V + S) + js + jv[:1] + parts[:1] + jv[1:2] + parts[1:2] + jv[2:-1] + parts[2:4] + [code_sel, code_numbers] + jv[-1:])
+            js, jv, (la, lb) = joins(S[0]), joins(V[0], S[0]), ahead(S + V)
+            a, b = min(s[0] for s in OWN + ONE), max(s[0] + s[1] for s in OWN + ONE)
+            play(la + lb[:1] + js + jv[:1] + lb[1:] + lists([(a, b - a, "")]))
+            if ONE:
+                send([K["lt", a]], [0], T.ltx[:, 32 * a:32 * b - 32], T.lt[:, 32 * a:32 * b - 32], "alt")
+            play([fetch] + jv[1:3] + sc[:1] + jv[3:] + sc[1:])
             cmd = [K["join", V[0][0]][1]]
-            send(cmd, [2, 3], T.cp1[:], T.cpm[:], "acp1", "apart")
-            js = weave(*[joins(s, None, False) for s in OWN])
-            play(lists(OWN) + js[:FILL[1]] + parts[n:] + [code_counts])
-            ed = code_out()
-            play(js[FILL[1]:])
+            for x in ([2], [3]) if OPT["c1"] else ([2, 3],):
+                send(cmd, x, T.cp1[:], T.cpm[:], "acp1", "apart")
+            play(weave([f for s in OWN for f in joins(s, None, False)], joins(end, None, False, True)))
+            x, d = own_table(end, True)[2:]
+            send(d, [2, 3], T.cpe[:], x, "acpe", "apart")
         if r == 2:
-            ja, jb = joins(V[0], S[0]), joins(V[1], S[1])
-            play(lists(S) + js[:3] + parts[:2] + weave(lists(V) + parts[2:4], mc) + [code_sel, code_numbers, js[4], js[3]]
-                 + [diagonal] + weave(ja[:-1], jb[:-1]) + parts[4:FILL[r]])
-            for i in (0, 1):
-                (ja, jb)[i][-1]()
-                send([K["join", V[i][0]][1]], [to], (T.cpx, T.cpy)[i][:], table(V[i]), ("acpx", "acpy")[i])
-            md = merge(V[:1] + [None] + V[1:])
-            play(parts[FILL[r]:FILL[4]])
+            ja, jb, j = joins(V[0], None if OPT["split"] else S[0]), joins(V[1], None, False, last=OPT["d2"]), both[0][0]
+            la, lb = ahead([S[0], V[0]])
+            play(la + lb[:1] + joins(S[0]) + ja[:1] + lb[1:] + lists([(j, 16 - j, "")]))
+            send([K["lt", j]], [3], T.ltx[:, 32 * j:480], T.lt[:, 32 * j:480], "alt")
+            f2 = [fetch, fetch_other]
+            play(f2[:OPT["f2"]])
+            if OPT["split"]:
+                play(joins(S[1], None, False) + ja[1:] + jb[:1])
+                send(own_table(S[0])[3], [3], T.cpy[:], table(S[0]), "acpy")
+            else:
+                play(joins(S[1], None, False) + ja[1:-1] + jb[:1] + ja[-1:])
+            cmd = [K["join", V[0][0]][1]]
+            send(cmd, [3], T.cpx[:], table(V[0]), "acpx")
+            play(f2[OPT["f2"]:] + jb[1:])
         if r == 3:
-            jv = weave(joins(V[0], S[0]), joins(V[1], S[1]))
-            js, je = weave(joins(S[0]), joins(S[1])), joins(S[2])
-            play(lists(S[:2]) + js[:1] + parts[:2])
-            send([CW["sel", 1]], [0], T.selx[:], T.sel[:], "asel")
-            identity()
-            play([code_sel] + weave(parts[2:4] + lists(V), mc) + [code_numbers] + js[1:] + jv[:1]
-                 + lists(S[2:]) + je[:1] + [diagonal] + je[1:] + jv[1:])
-            md = merge(V[:1] + [None] + V[1:] + S[2:])
-            play(parts[4:] + [code_counts])
-        if r != 2:
-            late_constants()
-        dl = digit_list()
-        if r > 1:
-            cmd = merge_out(md)
-        if r == 3:
-            send(cmd, [to], T.cpx[:], T.cpm[:], "acpx")
-        if r == 3:
-            ed = code_out()
-        if r == 1:
-            play(dl)
-        if r != 2:
-            begin(cmd + [ed])
+            mc, diagonal = merge_constants()
+            jv, js = weave(joins(V[0]), joins(V[1], S[0])), weave(joins(S[0]), joins(S[1]))
+            j, n = end[:2]
+            play(lists(S[:2]) + js[:2] + lists([end]))
+            send([K["lt", j]], [1], T.ltx[:, 32 * j:32 * (j + n - 1)], T.lt[:, 32 * j:32 * (j + n - 1)], "alt", "apart")
+            jc = joins(both[0][:2] + (OPT["c3"][0],), None, False, True, OPT["c3"][1])
+            jd = joins(both[1][:2] + (OPT["c3"][2],), None, False, True, OPT["c3"][3])
+            f3 = [[fetch, fetch_other], [fetch_other, fetch]][OPT["f3"] < 2] if OPT["t2"] else [fetch]
+            if OPT["f3"] == 3:
+                f3 = [fetch, fetch_other]
+            if OPT["patch"]:
+                mc, diagonal = [], lambda: None
+            play(lists(V[:1]) + mc[:1] + lists(V[1:]) + jv[:1] + mc[1:] + [diagonal] + js[2:] + jv[1:]
+                 + f3[:OPT["f3"] % 2 if OPT["f3"] == 3 else OPT["f3"]] + jc[:OPT["d3"]])
+            if OPT["patch"]:
+                whole = dma("y", [K["w"]], "lmg", T.cpm[:], T.w[:])
+                other_tables(0)
+                for s in (S[0], V[0], None, S[1], V[1]):
+                    if s is None:
+                        other_tables(1)
+                        continue
+                    for e in (s[0] + s[1] - 2, s[0] + s[1] - 1):
+                        cmd = [dma("y", own_table(s)[3] + [whole], "lmg", T.cpm[e:128:16, :], table(s, slice(e, 128, 16)))]
+            else:
+                cmd = merge_out(merge([None, V[0], S[1], V[1]]))
+            send(cmd, [2], T.cpx[:], T.cpm[:], "acpx")
+            play(f3[OPT["f3"] % 2 if OPT["f3"] == 3 else OPT["f3"]:] + jc[OPT["d3"]:] + jd)
+        begin(cmd)
     if r == 1:
-        segs = plan(1, (T.w[:], []), [(T.cpm[:], cmd)])
-        if OWN:
-            segs[OWN[0][0]:single] = [(s[0], s[1], table(s), [K["join", s[0]][1]]) for s in OWN]
-        reads, _, late = string(segs, (T.s1, 0, arrive(0, "as1")),
-                                lambda j, n: (range(j, j + n - (1 if j < single else 2)), T.w[:]), {})
+        segs = with_joined(range(single), (T.w[:], []), OWN) + plan(1, (None, None), [(T.cpm[:], cmd)])[single:]
+        late = string(segs, (T.tt, column("tt"), arrive(0, "as1")),
+                      lambda j, n: (only(j + n - 1), range(j, j + n - 1)) if j < single else last_two(j, n), T.w[:], {})[1]
         play(late)
-        total(1, T.eea, follow(reads, T.e, ed, T.eea, 3))
-        send([cd[1]], [2, 3, 0], code(1), code(1), "arc1", "apart")
+        play(codes(1, 16, (free["tt"] - 16) // 32, own_codes, True))
+        send([gd[1]], [2, 3], count_of(1, 2), count_of(1, 2), "acn1", "apart")
+        send([K["sent", 1]], [0], pair(1), pair(1), "arc1")
         spread(1)
-        play(digits([1], T.ep1))
+        play(digits([1]))
         send([K["ep", 1]], [2], T.ep1[:], T.ep1[:], "aep1")
         tally(1)
         cd[0] = arrive(0, "arc0")
-        whole(0)
-        alone(0, T.epa, False)
+        gates(0)
+        alone(0, False)
         hot(1)
-        add(1, T.ep1, 0, [])
-        K["qi", 2] = arrive(2, "arc2")
-        cd[2] = do("v", [K["qi", 2]], lambda: vec.tensor_copy(code(2), T.q2[:]))
-        D = digits([2], T.epb)
-        spread(2)
-        play(D[:1] + [lambda: tally(2)] + D[1:])
-        hot(2)
-        add(2, T.epb, 0, [], True)
+        add(1)
+        K["en", 2] = K["ee", 2] = arrive(2, "arc2")
+        codes(2, None, None, own_codes, False)[2]()
+        alone(2, True)
     if r > 1:
         own, other = [(T.cpm[:], cmd)], [(T.cpx[:], [arrive(5 - r, "acpx")])]
-        if r == 3:
-            other.append((T.cpy[:], [arrive(2, "acpy")]))
-        plain = (T.w[:], []) if r == 2 else (T.w1[:], [arrive(2, "aw1")])
         rest = plan(1, (None, None), [(T.cp1[:], [arrive(1, "acp1", "apart")])])[single:]
-        hooks = {0: dl[:1], 1: dl[1:]}
-        if r == 2:
-            left = parts[FILL[4]:]
-            hooks = {0: left[:len(left) // 2] + dl[:1], 1: left[len(left) // 2:] + [code_counts]}
-            if not left:
-                code_counts()
-                hooks[1] = []
-        at = string(rest, (T.s1, 0, arrive(0, "as1")), None, hooks)[1]
-        if r == 2:
-            ed = code_out()
-            begin(cmd + [ed])
-        a0, a1 = arrive(0, "arc0", "apart"), arrive(1, "arc1", "apart")
+        second = plan(2, (T.w[:], []), [(table(V[0]), cmd)]) if r == 2 else plan(2, (T.w1[:], []), other)
+        second[-2:] = [own_table(s, r == 3) for s in both]
+        if OPT["split"]:
+            second[0] = own_table(S[0]) if r == 2 else second[0][:2] + (T.cpy[:], [arrive(2, "acpy")])
+        third = [end[:2] + (T.cpe[:], [arrive(1, "acpe", "apart")]) if s[0] == end[0] else s
+                 for s in plan(3, None, other if r == 2 else own)]
 
-        def last_two(q):
-            return [range(j + 1, min(j + n + 1, 16)) for j, n, _ in segments(q)[-2:]]
+        def gives(j, n):
+            return last_two(j, n) if j == end[0] else merged(j, n)
+        first = column("tt")
+        lm = last_masks()
+        at = string(rest, (T.s1, 0, arrive(0, "as1", OPT["state"])), None, None,
+                    {0: sc[:1] + lm[:1], 1: merged_constants([3]) + sc[1:]}, first)[0]
+        gd[0], gd[1] = arrive(0, "acn0", "apart"), arrive(1, "acn1", "apart")
+        other_codes = (T.cwx[:, 0:512], T.cwx[:, 512:1024], [("lcx", 16)])
+        count = 1 + sum(max(1, n - 1) for n, _ in SEGS[2])
+        c2 = codes(2, first, count, own_codes if r == 2 else other_codes, False)
+        first += 32 * count
+        at, late = string(second, at, last_two, T.w[:] if r == 2 else T.w1[:], {0: lm[1:2], 1: lm[2:3]}, first)
+        play(late)
+        column("tt")
 
-        def far_two(q):
-            def f():
-                for x in range(2):
-                    js, c = last_two(q)[x], 32 * (q - 2) + 16 * x - 1
-                    do("v", [c_far3], lambda: vec.tensor_copy(T.far3[:, c + js[0]:c + js[-1] + 1], T.far[:, js[0]:js[-1] + 1]))
-            return f
-
-        def codes(q, at, wins, inner, hooks, e, edep, ee):
-            segs, out, n = plan(q, *wins), T["ee%d" % q], last_two(q)[0][0]
-            reads, at, _ = string(segs[:-1], at, inner, hooks)
-            steps = sorted(range(n), key=lambda j: reads[j][2][1] if j else 0)
-            last = [code_at("s", reads, j, e, edep, ee) for j in steps[:-FILL["v", q] or None]][-1]
-
-            def three(x, at):
-                c = 32 * (q - 2) + 16 * x
-                return tten([at[2], edep], out[:, 1 + 16 * x:17 + 16 * x], e[:].indirect(at[0][:, at[1]:at[1] + 1]),
-                            T.far3[:, c:c + 16], OP.add)
-            end = string(segs[-1:], at, None, {})[1]
-            own = [code_at("v", reads, j, e, edep, ee) for j in steps[n - FILL["v", q]:]]
-            three(0, at)
-
-            def early():
-                return do("v", [last] + own, lambda: vec.tensor_reduce(out[:, 0:1], ee[:, 15:17 * n:17], AxisListType.X, OP.max))
-
-            def rest():
-                three(1, end)
-                K["ee2"] = early()
-                send([K["ee2"]], [3], T.ee2[:], T.ee2[:], "arc2")
-            if q == 2:
-                return end, rest
+        def second_done():
             tally(0)
-            early()
-            return end, three(1, end)
-
-        cd[0], cd[1] = a0, a1
-        if r == 2:
-            at, last = codes(2, at, (plain, own), lambda j, n: (range(j + 1, j + n - 2), T.cpm[:]),
-                             {0: [far_two(2)], 1: [far_two(3)], 2: dl[1:]}, T.e, ed, T.eea)
-            hooks = {0: [last],
-                     1: [lambda: total(2, T.ee2[:], [K["ee2"]]), lambda: send([K["qi", 2]], [1], T.q2[:], buf("qi", 2, 1), "arc2")],
-                     2: [lambda: tally(2)]}
-            last3 = codes(3, at, (None, other), None, hooks, T.ex, arrive(0, "aex", "wide", 2), T.eeb)[1]
-            tally(1)
-            spread(2)
-        else:
-            at = string(plan(2, plain, other), at, None, {0: [far_two(3)]})[1]
-            last3 = codes(3, at, (None, own), None, {}, T.e, ed, T.eeb)[1]
-            tally(1)
-            total(2, T.ee2[:], [arrive(2, "arc2")])
-        total(3, T.ee3[:], [last3])
-        if r == 3:
             tally(2)
-        D = digits([2, 3], T.epb)
-        D[0]()
-        tally(3)
-        if r == 3:
             spread(2)
-        spread(3)
-        D[1]()
+        D2, D3 = digits([2]), digits([3])
         if r == 2:
-            hot(1)
-            add(1, T.ep1, 0, [arrive(1, "aep1")])
-        hot(2)
-        D[2]()
-        add(2, T.epb, 0, [K["ep", 2]])
-        D[3]()
-        hot(3)
-        add(3, T.epb, 32, [], True)
+            hooks = {0: c2[:1], 1: [c2[1], lambda: send([K["en", 2]], [1], T.e2[:], T.e2[:], "arc2")], 2: lm[3:], 3: [c2[2], second_done]}
+        else:
+            hooks = {1: c2[:1], 2: lm[3:], OPT["p3"]: c2[1:2]}
+        at = string(third, at, gives, T.cpx[:] if r == 2 else T.cpm[:], hooks)[0]
+        c3 = codes(3, first, (free["tt"] - first) // 32 - 1, other_codes if r == 2 else own_codes, False)
+        if r == 3 and OPT["p3"] > 4:
+            play(c3[:1])
+            tally(1)
+            c3[1](at)
+            play(c2[1:2] + c3[2:])
+            tally(3)
+            spread(3)
+            play([c2[2], second_done] + D3[:2] + D2[:2])
+            hot(2)
+            hot(3)
+            D3[2]()
+            add(3)
+            D3 = D2
+        else:
+            play(c3[:1] + (D2[:2] if r == 2 else [c2[2], second_done]))
+            tally(1)
+            c3[1](at)
+            play((D2[2:] if r == 2 else D2[:2]) + c3[2:])
+            tally(3)
+            spread(3)
+            hot(2)
+            if r == 2:
+                add(2)
+                hot(1)
+                add(1, False, [arrive(1, "aep1")])
+            play(D3[:2])
+            if r == 3:
+                D2[2]()
+                add(2)
+            hot(3)
+        D3[2]()
+        add(2 if r == 3 and OPT["p3"] > 4 else 3, True)
     if r == 3:
         nd = ts([K["at", "Z"]], T.neg[:], T.pl[0:8, 3:35], places["Z"], -1.0, OP.is_ge, OP.mult)
         yd = tten([ydep[0], nd], T.ysb[:], T.py[0:8, 0:32], T.neg[:], OP.add)

import numpy as np
from concourse.bass import DstId, RemoteDMATransfer, IndirectOffsetOnAxis
from concourse.mybir import dt, AluOpType, AxisListType, ActivationFunctionType

F, H, I, U = "float32", "bfloat16", "int32", "uint16"
SCRATCH = {
    "nxi": ("sbuf", [128, 256], I), "emi": ("sbuf", [128, 256], I), "syr": ("sbuf", [1, 128], I), "sy8": ("sbuf", [8, 16], I),
    "syb": ("sbuf", [1, 128], H), "six": ("sbuf", [1, 128], H), "syc": ("sbuf", [128, 1], I), "sy8b": ("sbuf", [8, 16], H),
    "evl": ("sbuf", [1, 128], H), "ramp": ("sbuf", [1, 512], H), "ind": ("sbuf", [1, 240], H),
    "tbd": ("dram", [64, 1024], I), "cw": ("sbuf", [128, 1024], I), "idx": ("sbuf", [128, 1], I),
    "pci": ("sbuf", [128, 2], I), "igf": ("sbuf", [128, 128], F),
    "rowf": ("sbuf", [128, 128], F), "pl": ("sbuf", [128, 36], F), "mg": ("sbuf", [128, 32], F),
    "ci5": ("sbuf", [128, 6], I), "cf5": ("sbuf", [128, 6], F), "cols": ("sbuf", [128, 16], F),
    "bo": ("sbuf", [128, 128], H), "tri": ("sbuf", [128, 128], H), "idn": ("sbuf", [128, 128], H), "dba": ("sbuf", [128, 128], H),
    "mask": ("sbuf", [128, 17], F), "pm": ("sbuf", [128, 16], F), "vm": ("sbuf", [128, 128], F),
    "dm": ("sbuf", [128, 32], F), "dn": ("sbuf", [128, 48], F),
    "thg": ("sbuf", [128, 32], F), "tho": ("sbuf", [128, 32], F), "l32": ("sbuf", [128, 4], U),
    "ti": ("sbuf", [128, 256], I), "sel": ("sbuf", [128, 256], H), "selo": ("sbuf", [128, 256], H),
    "nxd": ("dram", [128, 256], I), "emd": ("dram", [128, 256], I), "tbx": ("dram", [64, 1024], I),
    "cwx": ("sbuf", [128, 1024], I), "idy": ("sbuf", [128, 1], I),
    "off": ("sbuf", [128, 1], H), "tq": ("sbuf", [128, 288], H), "tab": ("sbuf", [128, 544], H),
    "ot": ("sbuf", [128, 32], U), "lt": ("sbuf", [128, 512], U),
    "w": ("sbuf", [128, 512], H), "w1": ("sbuf", [128, 512], H), "ltx": ("sbuf", [128, 512], U), "cp1": ("sbuf", [128, 512], H),
    "cp": ("sbuf", [128, 7680], H), "cpm": ("sbuf", [128, 512], H), "cpx": ("sbuf", [128, 512], H), "cpe": ("sbuf", [128, 512], H), "wr": ("sbuf", [128, 512], H), "cpy": ("sbuf", [128, 512], H),
    "s1": ("sbuf", [128, 2], U), "tt": ("sbuf", [128, 1024], U), "tu": ("sbuf", [128, 512], U), "all": ("sbuf", [128, 8], U),
    "e0": ("sbuf", [128, 32], F), "e1": ("sbuf", [128, 32], F), "e2": ("sbuf", [128, 32], F), "e3": ("sbuf", [128, 64], F),
    "cn": ("sbuf", [128, 32], H), "gg": ("sbuf", [128, 128], H),
    "rc0": ("sbuf", [128, 2], I), "rc1": ("sbuf", [128, 2], I), "rcb": ("sbuf", [128, 8], I),
    "di0": ("sbuf", [128, 4], I), "di1": ("sbuf", [128, 4], I), "dib": ("sbuf", [128, 8], I),
    "ep0": ("sbuf", [128, 32], H), "ep1": ("sbuf", [128, 32], H), "epb": ("sbuf", [128, 64], H),
    "ysb": ("sbuf", [8, 32], F), "neg": ("sbuf", [8, 32], F),
    "px": ("psum", [128, 512], F), "pwa": ("psum", [128, 512], F), "pwb": ("psum", [128, 512], F),
    "pcm": ("psum", [128, 512], F), "pew": ("psum", [128, 512], F), "pb": ("psum", [128, 512], F),
    "pc": ("psum", [128, 512], F), "py": ("psum", [128, 512], F),
}
for _q in range(4):
    SCRATCH["oh%d" % _q] = ("sbuf", [128, 36], H)
SEMAPHORES = ["v", "s", "t", "p", "lnx", "lsy", "lsc", "lem", "ltb", "lcw", "ltx", "lcx", "lmg", "st", "loc",
              "as1", "aw1", "awr", "acpx", "acpy", "acpe", "arc0", "arc1", "arc2", "acn0", "acn1", "anx", "aem", "aidx", "alt", "acp1", "aep1"]
OP = AluOpType
AF = ActivationFunctionType
SEGS = {0: [(1, "")] * 16,
        1: [(1, "")] * 7 + [(5, "v"), (4, "s")],
        2: [(5, "s"), (5, "v"), (3, "s"), (3, "v")],
        3: [(3, "s"), (3, "v"), (3, "s"), (3, "1"), (3, "v")]}
OWN = [(4, 3, "s")]
PIECES = [4, 6, 6, 6, 6, 4]
ZERO = [(8, 2, "s"), (10, 2, "v"), (12, 2, "s"), (14, 2, "s")]
ONE = [(5, 2, "s")]
OPT = {"early": True, "order": [2, 3], "state": "apart", "d2": "s", "d3": 0, "c3": "vvss", "shift": 0, "f2": 1, "f3": 3, "relay": True, "t2": True, "behind": False, "split": False, "patch": False, "by2": True, "p3": 3, "c1": True, "o2": [1, 3], "g2": True}
UNIT = 512.0
BASE = 130 * UNIT


def segments(q):
    out, j = [], 0
    for n, qn in SEGS[q]:
        out.append((j, n, qn))
        j += n
    return out


def rank_program(g, core, T, topo):
    r = T.rank_of(core)
    if r is None:
        return
    Q = {"v": g.vector, "s": g.scalar, "t": g.tensor, "p": g, "y": g.sync}
    cnt = {}
    seen = {}
    vec, act, mm = g.vector, g.scalar.activation, g.tensor.matmul
    long = [s for s in segments(r) if s[1] > 1]
    single = len([s for s in SEGS[1] if s[0] == 1])

    def waits(qn, deps):
        need = {}
        for d in deps:
            if d is not None:
                need[d[0]] = max(need.get(d[0], 0), d[1])
        for sn in need:
            if seen.get((qn, sn), 0) < need[sn]:
                Q[qn].wait_ge(T.sem[sn], need[sn])
                seen[(qn, sn)] = need[sn]

    def do(qn, deps, fn):
        waits(qn, deps)
        fn().then_inc(T.sem[qn], 1)
        cnt[qn] = cnt.get(qn, 0) + 1
        return (qn, cnt[qn])

    def ts(deps, *a):
        return do("v", deps, lambda: vec.tensor_scalar(*a))

    def tten(deps, *a):
        return do("v", deps, lambda: vec.tensor_tensor(*a))

    def dma(qn, deps, sn, out, in_):
        waits(qn, deps)
        Q[qn].dma_start(out, in_).then_inc(T.sem[sn], 16)
        cnt[sn] = cnt.get(sn, 0) + 16
        return (sn, cnt[sn])

    def fan(src):
        m = -1
        for c in T.cores:
            if c != T.cores[src]:
                m &= topo.mask(T.cores[src], c)
        return m

    def lane(src, dst, how):
        m = topo.mask(T.cores[src], T.cores[dst])
        return m if how == "wide" else (m & ~fan(src) if how == "apart" else 0) or fan(src)

    def send(deps, dsts, out, src, sn, how=None):
        waits("p", deps)
        lanes = {}
        for d in dsts:
            rid, pid, _ = topo.addr(T.cores[d])
            lanes[lane(r, d, how)] = lanes.get(lane(r, d, how), []) + [DstId(rid=rid, pnc=pid)]
        g.remote_dma_fused([RemoteDMATransfer(dst_ids=lanes[m], dma_engine_mask=m, remote_sem=T.sem[sn], srcs=[src],
                                              dsts=[out for _ in lanes[m]], alu_op=0) for m in lanes], local_sem=T.sem.loc)
        cnt["loc"] = cnt.get("loc", 0) + sum(bin(m).count("1") for m in lanes)

    def arrive(src, sn, how=None, calls=1):
        cnt[sn] = calls * bin(lane(src, r, how)).count("1")
        return (sn, cnt[sn])

    def play(fs):
        for f in fs:
            f()

    l_nx = dma("y", [], "lnx", T.nxi[:], T.nx[:])
    l_sy = dma("s", [], "lsy", T.syr[:], T.sy[:])
    if r == 3 or r == 2 and OPT["t2"]:
        l_em = dma("y", [], "lem", T.emi[:], T.em[:])
    l_sc = dma("s", [], "lsc", T.syc[:], T.sy[:])
    dma("y", [], "ltb", T.tbd[:, 0:512], T.nx[:])
    l_tb = dma("y", [], "ltb", T.tbd[:, 512:1024], T.em[:])

    lo = {"allow_small_or_imprecise_dtypes": True}
    c_p = do("p", [], lambda: g.iota(T.pci[:, 0:1], [[0, 1]], 0, 1))
    if r > 0:
        c_row = do("p", [], lambda: g.iota(T.rowf[:], [[1, 128]], 0, 0, **lo))
    c_ig = do("p", [], lambda: g.iota(T.igf[:], [[1, 8], [0, 16]], 0, 0, **lo))
    if r == 0:
        c_row = do("p", [], lambda: g.iota(T.rowf[:], [[1, 128]], 0, 0, **lo))
    c_17 = do("p", [], lambda: g.iota(T.pci[:, 1:2], [[0, 1]], 0, 17))
    if r > 0:
        c_ramp = [do("s", [c_row], lambda: act(T.ramp[:, 128 * x:128 * x + 128], T.rowf[0:1, :], AF.Identity, bias=128.0 * x - 256))
                  for x in range(4)]
        x = do("v", [], lambda: vec.memset(T.evl[:], 0.0))
    do("v", [], lambda: vec.memset(T.ind[:, 0:112], 0.0))
    do("v", [], lambda: vec.memset(T.ind[:, 112:128], 4.0))
    c_ind = do("v", [], lambda: vec.memset(T.ind[:, 128:240], 0.0))
    c_six = do("v", [], lambda: vec.memset(T.six[:], 64.0))
    P1, CI, CF, CO = T.pci[:, 0:1], T.ci5, T.cf5, T.cols
    do("v", [], lambda: vec.memset(T.tq[:, 0:16], 0.0))
    ts([c_p], CI[:, 0:1], P1, 4, None, OP.arith_shift_right)
    y = ts([], CI[:, 1:2], P1, 15, None, OP.bitwise_and)
    if r > 0:
        for j, n, _ in long:
            c_evl = do("v", [x], lambda: vec.memset(T.evl[:, j + n - 2:128:16], 1.0))
    c_cf = do("v", [y], lambda: vec.tensor_copy(CF[:, 0:2], CI[:, 0:2]))
    do("v", [], lambda: vec.memset(T.tq[:, 272:288], 0.0))
    do("v", [], lambda: vec.memset(T.off[:], -BASE))
    if r > 0:
        c_k1 = ts([c_cf], CO[:, 6:7], CF[:, 1:2], 1.0, None, OP.add)
        c_g8 = ts([], CO[:, 3:4], CF[:, 0:1], 8.0, None, OP.mult)
    c_bo = ts([c_cf, c_ig], T.bo[:], T.igf[:], CF[:, 0:1], None, OP.is_equal)
    if r == 0:
        c_k1 = ts([], CO[:, 6:7], CF[:, 1:2], 1.0, None, OP.add)
        c_g8 = ts([], CO[:, 3:4], CF[:, 0:1], 8.0, None, OP.mult)
    m_sy = ts([l_sy], T.syb[:], T.syr[:], 1.0 / 32, -0.25, OP.mult, OP.add)
    ne = ts([c_17], CI[:, 2:3], T.pci[:, 1:2], 4, 1, OP.arith_shift_right, OP.bitwise_and)
    c_mask = ts([c_row], T.mask[:, 0:16], T.rowf[:, 0:16], CF[:, 1:2], None, OP.is_equal)
    c_k8 = ts([ne, c_k1], CO[:, 8:9], CI[:, 2:3], 17.0, CO[:, 6:7], OP.mult, OP.add)
    K = {"pm": None}
    am = T.py[:, 64:80] if r else T.pew[:, 304:320]

    def symbols():
        do("t", [c_bo], lambda: mm(T.px[:, 0:128], T.bo[:], T.bo[:], True, False))
        K["x"] = do("t", [m_sy, c_six], lambda: mm(T.px[:, 0:128], T.six[:], T.syb[:], False, True))
    if r > 0:
        do("t", [c_evl, c_six], lambda: mm(T.pc[:, 0:128], T.six[:], T.evl[:], True, False))
        WB = (T.pwa, T.pwb, T.pcm, T.pew)
        for x in range(4):
            do("t", [c_ramp[x]], lambda: mm(WB[x][:, 0:128], T.evl[:], T.ramp[:, 128 * x:128 * x + 128], True, False))
        do("t", [c_bo], lambda: mm(T.pc[:, 0:128], T.bo[:], T.bo[:], False, False))
        m_o = do("t", [m_sy], lambda: mm(T.pc[:, 0:128], T.six[:], T.syb[:], False, True))
    else:
        symbols()
    for x in range(8):
        m_am = do("t", [c_ind], lambda: mm(am, T.ind[:, 112 - 16 * x:240 - 16 * x], T.syb[:, 16 * x:16 * x + 16], x == 0, x == 7))

    def select(out, X, h, deps):
        return ts(deps, out[:, 128 * h:128 * h + 128], X[:, 0:128], float(h), CF[:, 1:2], OP.add, OP.is_equal)
    so, po, mo = (T.selo, T.pc, m_o) if r > 0 else (T.sel, T.px, K["x"])
    m_ta = ts([l_nx], T.ti[:, 0:128], T.nxi[:, 0:128], 511, None, OP.bitwise_and)
    m_ti = ts([], T.ti[:, 128:256], T.nxi[:, 128:256], 511, None, OP.bitwise_and)
    if r > 0:
        c_k9 = ts([c_k8], CO[:, 9:10], CO[:, 8:9], 1.0 / 16, None, OP.add)
    m_s0 = select(so, po, 0, [mo])
    m_t0 = ts([m_ta], T.tq[:, 16:144], T.ti[:, 0:128], -256.0, None, OP.add)
    m_tb = ts([m_ti], T.tq[:, 144:272], T.ti[:, 128:256], -256.0, None, OP.add)
    m_s1 = select(so, po, 1, [])
    if r == 0:
        c_k9 = ts([c_k8], CO[:, 9:10], CO[:, 8:9], 1.0 / 16, None, OP.add)
    turn = [lambda: ts([m_am, c_k9], T.ot[:, 0:32:2], am, CO[:, 8:9], 16.0, OP.add, OP.mult),
            lambda: ts([], T.ot[:, 1:32:2], am, CO[:, 9:10], 16.0, OP.add, OP.mult),
            lambda: do("v", [m_tb], lambda: vec.transpose(T.tab[:, 0:256], T.tq[:, 16:272])),
            lambda: K.update(tab=do("v", [], lambda: vec.transpose(T.tab[:, 256:544], T.tq[:, 0:288])))]
    if r > 0:
        turn.append(lambda: K.update(pm=tten([c_mask], T.pm[:, 1:16], T.mask[:, 1:16], T.mask[:, 0:15], OP.add)))

    def identity():
        K["idn"] = do("p", [c_bo], lambda: g.affine_select(T.idn[:], T.bo[:], [[1, 128]], OP.is_equal, 0.0, 0, -1))

    def late_constants(part):
        if part == 0:
            K["mg"] = do("p", [], lambda: g.iota(T.mg[:], [[2, 4], [0, 8]], 261, 0, **lo))
            do("p", [], lambda: g.iota(T.pl[:], [[int(UNIT), 36]], int(UNIT) * (32 * r - 3), 0, **lo))
        if part == 1:
            K["mg"] = do("p", [K["mg"]], lambda: g.affine_select(T.tho[:], T.mg[:], [[0, 4], [-16, 8]], OP.is_ge, 1024.0, 0, 1))
            do("p", [c_bo], lambda: g.affine_select(T.tri[:], T.bo[:], [[1, 128]], OP.is_gt, 0.0, 0, -1))
        if part == 2:
            K["late"] = do("p", [K["mg"]], lambda: g.affine_select(T.thg[:], T.tho[:], [[0, 4], [16, 8]], OP.is_ge, 1024.0, 15, -1))

    def small_constants():
        def a():
            K["up"] = ts([], CO[:, 5:6], CF[:, 1:2], 8.0, None, OP.is_ge)
            K["m16"] = do("v", [c_mask], lambda: vec.tensor_copy(T.mask[:, 16:17], T.mask[:, 0:1]))
            if r != 2:
                x = 8 * min(r, 2) + 1
                do("v", [], lambda: vec.memset(T.cn[:, x:x + 1], 0.0))

        def b():
            ts([K["up"]], T.l32[:], T.rowf[:, 0:8:2], CO[:, 5:6], None, OP.add)
            K["dn"] = ts([K["m16"]], T.dn[:, 0:16], T.mask[:, 1:17], BASE - 255.75, None, OP.mult)
        return [a, b]

    def row_numbers():
        K["idx"] = ts([l_sc, c_g8], T.idx[:], T.syc[:], CO[:, 3:4], None, OP.add)

    def fetch(out=T.cw, rows=T.tbd, idx=T.idx, deps=None, sn="lcw"):
        waits("p", deps or [K["idx"], l_tb])
        g.indirect_dma_start(out[:], None, rows[:], IndirectOffsetOnAxis(ap=idx[:], axis=0), bounds_check=63).then_inc(T.sem[sn], 16)
        cnt[sn] = 16
    own_codes = (T.cw[:, 0:512], T.cw[:, 512:1024], [("lcw", 16)])

    def window(to):
        for x in range(4):
            h, u = x // 2, x % 2
            d = do("t", [m_s1 if h else m_s0, m_tb if u else m_t0], lambda: mm(
                WB[x][:, 0:128], T.selo[:, 128 * h:128 * h + 128], T.tq[:, 16 + 128 * u:144 + 128 * u], False, True))
            d = do("s", [d], lambda: act(T.w[:, 128 * x:128 * x + 128], WB[x][:, 0:128], AF.Copy))
        if to is not None:
            send([d], [to], T.w1[:], T.w[:], "aw1")
        return d

    def lists(segs):
        def one(j, n):
            def f():
                d = ts([K["tab"]], T.lt[:, 32 * j:32 * (j + n - 1)],
                       T.tab[:].indirect(T.ot[:, 2 * j:2 * (j + n - 1)]), 256.0, None, OP.add)
                for i in range(j, j + n - 1):
                    K["lt", i] = d
            return f
        return [one(j, n) for j, n, _ in segs]

    slot = [0]

    def joins(seg, plus=None, masked=True, foreign=False, last=None):
        j, n, qn = seg
        owner = {0: 1, 1: 3, 3: 2}.get(r)
        box = [T.w1[:], arrive(owner, "aw1", "apart")] if foreign else [T.w[:], K["w"]]

        def one(i):
            def f():
                x = slot[0]
                out = T.cp[:, 512 * x:512 * x + 512]
                slot[0] += 1
                src = box[0].indirect((T.ltx if foreign else T.lt)[:, 32 * i:32 * i + 32])
                keep = T.pm[:, j + n - 1:j + n] if masked and i == (j + n - 2 if plus else j) else 1.0
                deps = [box[1], arrive(owner, "alt", "apart") if foreign else K["lt", i], K["pm"]]
                if plus and i == j:
                    y, e = K["join", plus[0]]
                    d = tten(deps + [e], T.cpm[:] if r == 1 else out, src, T.cp[:, 512 * y:512 * y + 512], OP.add)
                elif (last if last and i == j else qn) == "v":
                    d = ts(deps, out, src, keep, None, OP.mult)
                else:
                    d = do("s", deps, lambda: act(out, src, AF.Copy, scale=keep))
                box[0], box[1] = out, d
                if i == j:
                    K["join", j + 16 * foreign] = (x, d)
            return f
        return [one(i) for i in range(j + n - 2, j - 1, -1)]

    def in_pieces(j, deps):
        x = slot[0]
        slot[0] += 1

        def one(a, n):
            return lambda: K.update({("join", j): (x, ts(deps + [K["lt", j]], T.cp[:, 512 * x + 16 * a:512 * x + 16 * (a + n)],
                                                         T.w[:].indirect(T.lt[:, 32 * j + a:32 * j + a + n]), 1.0, None, OP.mult))})
        return [one(sum(PIECES[:i]), PIECES[i]) for i in range(len(PIECES))]

    def merge_constants():
        ends = [T.pm[:, j + n - 1:j + n] for j, n, qn in long if qn != "1"]

        def three():
            out = CO[:, 10 + len(ends):11 + len(ends)]
            K["kb"] = ts([K.get("kb"), K["pm"]], out, ends[0], ends[1], ends[2], OP.add, OP.add)
            ends[0:3] = [out]

        def last():
            if len(ends) > 1:
                d = ts([K.get("kb")], CO[:, 10:11], ends[0], ends[1], 0.0, OP.add, OP.is_equal)
            else:
                d = ts([K.get("kb")], CO[:, 10:11], ends[0], 0.0, None, OP.is_equal)
            K["keep"] = d

        def diagonal():
            K["dba"] = do("s", [K["keep"], K["idn"]], lambda: act(T.dba[:], T.idn[:], AF.Copy, scale=CO[:, 10:11]))
        return [three] * ((len(ends) - 1) // 2) + [last], diagonal

    MB = (T.pcm, T.pc)

    def table(seg, rows=slice(None)):
        x = K["join", seg[0]][0]
        return T.cp[rows, 512 * x:512 * x + 512]

    def own_table(seg, foreign=False):
        x, d = K["join", seg[0] + 16 * foreign]
        return seg[:2] + (T.cp[:, 512 * x:512 * x + 512], [d])

    def merge_add(lhs, src, x, deps, first=False, last=False):
        return [do("t", deps, lambda: mm(MB[h][:, 0:256], lhs[:], src[:, x + 256 * h:x + 256 * h + 256], first, last))
                for h in range(2)]

    def merge(order):
        for seg in order:
            if seg is None:
                merge_add(T.dba, T.w, 0, [K["dba"], K["w"]], seg == order[0])
            else:
                n, d = K["join", seg[0]]
                md = merge_add(T.idn, T.cp, 512 * n, [d, K["idn"]], seg == order[0], seg == order[-1])
        return md

    def merge_out(md):
        return [[do("s", [md[h]], lambda: act(T.cpm[:, 256 * h:256 * h + 256], MB[h][:, 0:256], AF.Copy)) for h in range(2)][1]]

    def weave(*rows):
        rows = [list(x) for x in rows]
        out = []
        while any(rows):
            for x in rows:
                if x:
                    out.append(x.pop(0))
        return out

    free = {"tt": 16, "tu": 16}

    def column(tile):
        free[tile] += 32
        return free[tile] - 32

    def gather(win, at, deps, k, keep=None, col=None):
        tile = T.tt if keep else T.tu
        col = col or column(tile.name)
        out, src = tile[:, col - k:col - k + 16], win.indirect(at[0][:, at[1]:at[1] + 1])
        if keep:
            K["col", col] = ts([at[2], keep[1]] + deps, out, src, 256.0, keep[0], OP.add, OP.mult)
            return (tile, col, K["col", col])
        return (tile, col, ts([at[2]] + deps, out, src, 256.0, None, OP.add))

    def only(i):
        return (T.mask[:, i:i + 1], c_mask)

    def merged_constants(qs):
        def one(n):
            return lambda: K.update({("vm", n): tten([K["pm"]], T.vm[:, 16 * n + n - 1:16 * n + 16], T.pm[:, n - 1:16],
                                                     T.mask[:, 0:17 - n], OP.add)})
        return [one(n) for n in sorted({n for q in qs for n, _ in SEGS[q] if n > 2})]

    def merged(j, n):
        e = j + n - 1
        if n == 1:
            return only(j), []
        keep = (T.pm[:, e:e + 1], K["pm"]) if n == 2 else (T.vm[:, 16 * n + e:16 * n + e + 1], K["vm", n])
        return keep, range(j + 1, e - 1)

    def last_two(j, n):
        e = j + n - 1
        if n == 1:
            return only(j), []
        return (only(14) if e == 15 else (T.pm[:, e:e + 1], K["pm"])), range(j, e - 1)

    def plan(q, plain, joined):
        out, segs = [], segments(q)
        for m in range(len(segs)):
            x = min(len(joined) - 1, len([s for s in segs[:m] if s[1] > 1]) // 2)
            out.append(segs[m][:2] + (plain if segs[m][1] == 1 else joined[x]))
        return out

    def string(segs, at, gives, single_window, hooks, onward=None):
        reads, late = {segs[0][0]: at}, []
        for m in range(len(segs)):
            j, n, win, deps = segs[m]
            keep, steps = gives(j, n) if gives else (None, [])
            before, k = at, (j - 1) % 16
            behind = onward is not None and m == len(segs) - 1 and keep and r == 2 and OPT["behind"]
            if onward is not None and m == len(segs) - 1:
                if not behind:
                    at = made = gather(win, before, deps, k, only(15), onward)
                if keep:
                    made = gather(win, before, deps, k, keep)
            else:
                at = made = gather(win, before, deps, k, keep)
            if gives:
                for i in range(j, j + n):
                    reads[i + 1] = made
            row = [] if j in steps else [None]
            for i in steps:
                def f(i=i):
                    reads[i + 1] = gather(single_window, reads[i], [], (i - 1) % 16, only(i))
                row.append(f)
            late = [x for x in [row] + late if x]
            play([f for f in [x.pop(0) for x in late] if f])
            if behind:
                at = gather(win, before, deps, k, only(15), onward)
            play(hooks.get(m, []))
        return at, [f for f in weave(*late) if f]

    cd, gd = {}, {}
    ydep = [None, 0]

    def pair(q):
        return (T.rc0[:], T.rc1[:], T.rcb[:, 0:2], T.rcb[:, 4:6])[q]

    def numbers(q):
        return (T.rc0[:, 1:2], T.rc1[:, 1:2], T.rcb[:, 1:2], T.rcb[:, 5:6])[q]

    def codes(q, first, count, wins, sent):
        nxw, emw, deps = wins
        at = T.all[:, 2 * q:2 * q + 1]
        en, ee = [T["e%d" % q][:, x:x + (32 if q == 3 else 16)] for x in (0, 32 if q == 3 else 16)]

        def top(d, out, src):
            return do("v", [d], lambda: vec.tensor_reduce(out, src, AxisListType.X, OP.max))

        def bring():
            waits("v", [K.get(("col", first + 32 * n)) for n in range(count)])
            K["all", q] = top(None, at, T.tt[:, first:first + 32 * count:32])

        def pick(end=None):
            ones, base = (T.mask[:, 1:17], T.dn[:, 0:16]) if q < 3 else (T.dm[:, 16:32], T.dn[:, 32:48])
            if end:
                src = end[0][:, end[1]:end[1] + 1]
                tten([end[2], K["dn"]] + deps, ee[:, 16:32], emw.indirect(src), T.dm[:, 0:16], OP.mult)
                tten([], en[:, 16:32], nxw.indirect(src), T.dn[:, 16:32], OP.add)
            for x in ("en", "ee") if sent else ("ee", "en"):
                if x == "ee":
                    K[x, q] = tten([K["all", q], K["dn"]] + deps, ee[:, 0:16], emw.indirect(at), ones, OP.mult)
                else:
                    K[x, q] = tten([K["all", q], K["dn"]] + deps, en[:, 0:16], nxw.indirect(at), base, OP.add)

        def keep():
            if sent:
                gd[q] = top(K["en", q], count_of(q), en)
            cd[q] = top(K["ee", q], numbers(q), ee)
            if sent:
                K["sent", q] = top(K["en", q], pair(q)[:, 0:1], en)
            else:
                gd[q] = top(K["en", q], count_of(q), en)
        return [bring, pick, keep]

    def last_masks():
        j, n = segments(3)[-1][:2]

        def a():
            K["dm"] = do("v", [], lambda: vec.memset(T.dm[:, 0:16], 0.0))

        def b():
            K["dm"] = do("v", [K["dm"]], lambda: vec.tensor_copy(T.dm[:, j:j + n], T.mask[:, j + 1:j + n + 1]))

        def c():
            K["dm"] = tten([K["dm"], K["m16"]], T.dm[:, 16:32], T.mask[:, 1:17], T.dm[:, 0:16], OP.subtract)

        def d():
            K["dn"] = ts([K["dm"]], T.dn[:, 16:48], T.dm[:], BASE - 255.75, None, OP.mult)
        return [a, b, c, d]

    def count_of(q, n=1):
        return T.cn[:, 8 * q:8 * q + n]

    def gates(q):
        gd[q] = ts([cd[q]], count_of(q), pair(q)[:, 0:1], 0.25, None, OP.add)

    def spread(q):
        K["gg", q] = do("s", [gd[q], K["late"]], lambda: act(T.gg[:, 32 * q:32 * q + 32], T.thg[:], AF.Relu,
                                                             bias=count_of(q), scale=-UNIT / 2))

    def digits(qs):
        n = len(qs)
        qi = numbers(qs[0])
        di, ep = (T.di0, T.di1, T.dib, T.di0)[qs[0]], (T.ep0, T.ep1, T.epb, T.ep0)[qs[0]]

        def low():
            ts([cd[q] for q in qs], di[:, 0:4 * n:4], qi, 63, None, OP.bitwise_and)

        def high():
            for m in (1, 2, 3):
                K["di"] = ts([], di[:, m:4 * n:4], qi, 6 * m, 63, OP.arith_shift_right, OP.bitwise_and)

        def used():
            d = tten([K["di"]] + [K["gg", q] for q in qs], ep[:, 0:32 * n], di[:, 0:4 * n].indirect(T.l32[:, 0:2 * n]),
                     T.gg[:, 32 * qs[0]:32 * (qs[0] + n)], OP.min)
            K.update({("ep", q): d for q in qs})
        return [low, high, used]

    places = {q: (T.pb, T.pc, T.pwa, T.pb)[q][:, 0:1] for q in range(max(r - 1, 0), min(r + 2, 4))}
    sums = {q: [T.tri[:]] + [T.bo[:]] * q for q in places}
    if r == 3:
        places["Z"], sums["Z"] = T.pew[0:8, 0:1], [T.bo[:, 0:128:16]] * 4
    missing = {q: len(sums[q]) for q in sums}

    def begin(deps):
        for q in places:
            for n in range(len(sums[q])):
                do("t", [K["late"]] + deps, lambda: mm(places[q], sums[q][n], T.off[:], n == 0, False))

    def tally(b):
        for q in places:
            if q == "Z" or q >= b:
                missing[q] -= 1
                K["at", q] = do("t", [gd[b]], lambda: mm(places[q], sums[q][0 if q == b else -1], count_of(b), False, not missing[q]))

    def hot(q):
        K["oh", q] = ts([K["at", q]], T["oh%d" % q][:], T.pl[:], places[q], None, OP.is_equal)

    def add(q, final=False, deps=None):
        src, x = (T.ep0, T.ep1, T.epb, T.ep0)[q], 0
        for m in range(4):
            ydep[0] = do("t", [K["oh", q]] + (deps or [K["ep", q]]), lambda: mm(
                T.py[0:8, 0:32], src[:, x + 8 * m:x + 8 * m + 8], T["oh%d" % q][:, 3 - m:35 - m], ydep[1] == 0, final and m == 3))
            ydep[1] += 1

    def alone(q, final):
        D = digits([q])
        tally(q)
        spread(q)
        play(D[:2])
        hot(q)
        D[2]()
        add(q, final)

    def with_joined(steps, plain, segs, foreign=False):
        out, at = [], {s[0]: s for s in segs}
        for j in steps:
            if j in at:
                out.append(own_table(at[j], foreign))
            elif not out or j >= out[-1][0] + out[-1][1]:
                out.append((j, 1) + plain)
        return out

    def other_tables(x):
        K["tbx"] = dma("y", [arrive(5 - r, ("anx", "aem")[x])], "ltx", T.tbx[:, 512 * x:512 * x + 512], (T.nxd, T.emd)[x][:])

    def fetch_other():
        fetch(T.cwx, T.tbx, T.idy, [arrive(5 - r, "aidx"), K["tbx"]], "lcx")

    sc = small_constants()
    if r == 0:
        for x in range(3):
            late_constants(x)
        row_numbers()
        fetch()
        if OPT["relay"]:
            send([arrive(2, "awr", "apart")], [3], T.w1[:], T.wr[:], "aw1")
        play(turn[2:] + turn[:2])
        K["tab"] = ("v", cnt["v"])
        wdep = {}
        for x in range(4):
            h, u = x // 2, x % 2
            bank, out = (T.pwa, T.pwb, T.pcm, T.py)[x][:, 128:256], T.w[:, 128 * x:128 * x + 128]
            d = do("t", [m_s1 if h else m_s0, m_tb if u else m_t0], lambda: mm(
                bank, T.sel[:, 128 * h:128 * h + 128], T.tq[:, 16 + 128 * u:144 + 128 * u], True, True))
            wdep[x] = do("v", [d], lambda: vec.tensor_copy(out, bank)) if x == 2 else do("s", [d], lambda: act(out, bank, AF.Copy))
        c = column("tt")
        at = (T.tt, c, ts([c_mask, wdep[0]], T.tt[:, c:c + 1], T.w[:, 0:1], 256.0, T.mask[:, 0:1], OP.add, OP.mult))
        wdep = [wdep[2], wdep[3]]
        waits("s", wdep)
        K["w"] = wdep[0]
        first, S = ZERO[0], [s for s in ZERO if s[2] == "s"]
        play(lists(S[:1]) + joins(S[0], None, False))
        hooks = {n: [] for n in range(first[0])}
        for n, s in enumerate(S[1:]):
            hooks[n] += lists([s]) + joins(s, None, False)
        hooks[n] += [f for s in ONE for f in joins(s, None, False, True)]
        for s in ZERO:
            if s[2] == "v":
                hooks[0] = lists([s]) + hooks[0]
                for n, f in enumerate(in_pieces(s[0], wdep)):
                    hooks[first[0] - 1 - len(PIECES) + n].append(f)
        at = string(with_joined(range(1, first[0]), (T.w[:], wdep), []), at, lambda j, n: (only(j), []), None, hooks)[0]
        at1, late = string(with_joined(range(first[0], 16), (T.w[:], []), ZERO), at,
                           lambda j, n: (only(j + n - 1) if j + n < 16 else None, range(j, j + n - 1)), T.w[:],
                           {0: sc[:1], 1: sc[1:]}, 16 + 32 * 15)
        send([at1[2]], [1], T.tt[:, 16:18], T.tt[:, at1[1]:at1[1] + 2], "as1")
        c0 = codes(0, 16, 15, own_codes, True)
        segs = with_joined(range(single), (T.w1[:], [arrive(1, "aw1")]), ONE, True)
        fill = [[f] for f in late] + [c0[:1]]
        if OPT["early"]:
            fill += [c0[1:2], c0[2:] + [lambda: send([gd[0]], [2], count_of(0, 2), count_of(0, 2), "acn0", "apart")]]
        at = string(segs, at1, None, None, dict(enumerate(fill[:len(segs)])))[0]
        send([at[2]], OPT["order"], T.s1[:], T.tu[:, at[1]:at[1] + 2], "as1", OPT["state"])
        for x in fill[len(segs):]:
            play(x)
        if not OPT["early"]:
            play(c0[1:])
        send([gd[0]], [3] if OPT["early"] else [2, 3], count_of(0, 2), count_of(0, 2), "acn0", "apart")
        send([K["sent", 0]], [1], pair(0), pair(0), "arc0")
        begin([])
        alone(0, False)
        cd[1] = arrive(1, "arc1")
        gates(1)
        alone(1, True)
    else:
        late_constants(0)
        if r == 3 or r == 2 and OPT["t2"]:
            send([l_nx], [5 - r], T.nxd[:], T.nxi[:], "anx")
        late_constants(1)
        if r == 3 or r == 2 and OPT["t2"]:
            send([l_em], [5 - r], T.emd[:], T.emi[:], "aem")
        late_constants(2)
        if r == 3 and not OPT["patch"]:
            identity()
        if r == 2 or r == 3 and not OPT["patch"]:
            other_tables(0)
            other_tables(1)
        both = segments(2)[-2:]
        end = [s for s in segments(3) if s[2] == "1"][0][:2] + ("s",)
        on = {qn: [s for s in long if s[2] == qn] for qn in "sv"}
        S, V = on["s"], on["v"]
        K["w"] = window(None)
        play(turn + [row_numbers])
        if r == 3 or r == 2 and OPT["t2"]:
            send([K["idx"]], [5 - r], T.idy[:], T.idx[:], "aidx")
        if r == 2 and OPT["relay"]:
            send([K["w"]], [0], T.wr[:], T.w[:], "awr", "apart")
        else:
            send([K["w"]], [{1: 0, 2: 3, 3: 1}[r]], T.w1[:], T.w[:], "aw1", "apart")

        def ahead(segs):
            cut = [(j, j + n - 2 - (qn == "v"), j + n) for j, n, qn in segs]
            return lists([(b, c - b, "") for _, b, c in cut]), lists([(a, b + 1 - a, "") for a, b, _ in cut])
        if r == 1:
            js, jv, (la, lb) = joins(S[0]), joins(V[0], S[0]), ahead(S + V)
            a, b = min(s[0] for s in OWN + ONE), max(s[0] + s[1] for s in OWN + ONE)
            play(la + lb[:1] + js + jv[:1] + lb[1:] + lists([(a, b - a, "")]))
            if ONE:
                send([K["lt", a]], [0], T.ltx[:, 32 * a:32 * b - 32], T.lt[:, 32 * a:32 * b - 32], "alt")
            play([fetch] + jv[1:3] + sc[:1] + jv[3:] + sc[1:])
            cmd = [K["join", V[0][0]][1]]
            for x in ([2], [3]) if OPT["c1"] else ([2, 3],):
                send(cmd, x, T.cp1[:], T.cpm[:], "acp1", "apart")
            play(weave([f for s in OWN for f in joins(s, None, False)], joins(end, None, False, True)))
            x, d = own_table(end, True)[2:]
            send(d, [2, 3], T.cpe[:], x, "acpe", "apart")
        if r == 2:
            ja, jb, j = joins(V[0], None if OPT["split"] else S[0]), joins(V[1], None, False, last=OPT["d2"]), both[0][0]
            la, lb = ahead([S[0], V[0]])
            play(la + lb[:1] + joins(S[0]) + ja[:1] + lb[1:] + lists([(j, 16 - j, "")]))
            send([K["lt", j]], [3], T.ltx[:, 32 * j:480], T.lt[:, 32 * j:480], "alt")
            f2 = [fetch, fetch_other]
            play(f2[:OPT["f2"]])
            if OPT["split"]:
                play(joins(S[1], None, False) + ja[1:] + jb[:1])
                send(own_table(S[0])[3], [3], T.cpy[:], table(S[0]), "acpy")
            else:
                play(joins(S[1], None, False) + ja[1:-1] + jb[:1] + ja[-1:])
            cmd = [K["join", V[0][0]][1]]
            send(cmd, [3], T.cpx[:], table(V[0]), "acpx")
            play(f2[OPT["f2"]:] + jb[1:])
        if r == 3:
            mc, diagonal = merge_constants()
            jv, js = weave(joins(V[0]), joins(V[1], S[0])), weave(joins(S[0]), joins(S[1]))
            j, n = end[:2]
            play(lists(S[:2]) + js[:2] + lists([end]))
            send([K["lt", j]], [1], T.ltx[:, 32 * j:32 * (j + n - 1)], T.lt[:, 32 * j:32 * (j + n - 1)], "alt", "apart")
            jc = joins(both[0][:2] + (OPT["c3"][0],), None, False, True, OPT["c3"][1])
            jd = joins(both[1][:2] + (OPT["c3"][2],), None, False, True, OPT["c3"][3])
            f3 = [[fetch, fetch_other], [fetch_other, fetch]][OPT["f3"] < 2] if OPT["t2"] else [fetch]
            if OPT["f3"] == 3:
                f3 = [fetch, fetch_other]
            if OPT["patch"]:
                mc, diagonal = [], lambda: None
            play(lists(V[:1]) + mc[:1] + lists(V[1:]) + jv[:1] + mc[1:] + [diagonal] + js[2:] + jv[1:]
                 + f3[:OPT["f3"] % 2 if OPT["f3"] == 3 else OPT["f3"]] + jc[:OPT["d3"]])
            if OPT["patch"]:
                whole = dma("y", [K["w"]], "lmg", T.cpm[:], T.w[:])
                other_tables(0)
                for s in (S[0], V[0], None, S[1], V[1]):
                    if s is None:
                        other_tables(1)
                        continue
                    for e in (s[0] + s[1] - 2, s[0] + s[1] - 1):
                        cmd = [dma("y", own_table(s)[3] + [whole], "lmg", T.cpm[e:128:16, :], table(s, slice(e, 128, 16)))]
            else:
                cmd = merge_out(merge([None, V[0], S[1], V[1]]))
            send(cmd, [2], T.cpx[:], T.cpm[:], "acpx")
            play(f3[OPT["f3"] % 2 if OPT["f3"] == 3 else OPT["f3"]:] + jc[OPT["d3"]:] + jd)
        begin(cmd)
    if r == 1:
        segs = with_joined(range(single), (T.w[:], []), OWN) + plan(1, (None, None), [(T.cpm[:], cmd)])[single:]
        late = string(segs, (T.tt, column("tt"), arrive(0, "as1")),
                      lambda j, n: (only(j + n - 1), range(j, j + n - 1)) if j < single else last_two(j, n), T.w[:], {})[1]
        play(late)
        play(codes(1, 16, (free["tt"] - 16) // 32, own_codes, True))
        send([gd[1]], [2, 3], count_of(1, 2), count_of(1, 2), "acn1", "apart")
        send([K["sent", 1]], [0], pair(1), pair(1), "arc1")
        spread(1)
        play(digits([1]))
        send([K["ep", 1]], [2], T.ep1[:], T.ep1[:], "aep1")
        tally(1)
        cd[0] = arrive(0, "arc0")
        gates(0)
        alone(0, False)
        hot(1)
        add(1)
        K["en", 2] = K["ee", 2] = arrive(2, "arc2")
        codes(2, None, None, own_codes, False)[2]()
        alone(2, True)
    if r > 1:
        own, other = [(T.cpm[:], cmd)], [(T.cpx[:], [arrive(5 - r, "acpx")])]
        rest = plan(1, (None, None), [(T.cp1[:], [arrive(1, "acp1", "apart")])])[single:]
        second = plan(2, (T.w[:], []), [(table(V[0]), cmd)]) if r == 2 else plan(2, (T.w1[:], []), other)
        second[-2:] = [own_table(s, r == 3) for s in both]
        if OPT["split"]:
            second[0] = own_table(S[0]) if r == 2 else second[0][:2] + (T.cpy[:], [arrive(2, "acpy")])
        third = [end[:2] + (T.cpe[:], [arrive(1, "acpe", "apart")]) if s[0] == end[0] else s
                 for s in plan(3, None, other if r == 2 else own)]

        def gives(j, n):
            return last_two(j, n) if j == end[0] else merged(j, n)
        first = column("tt")
        lm = last_masks()
        at = string(rest, (T.s1, 0, arrive(0, "as1", OPT["state"])), None, None,
                    {0: sc[:1] + lm[:1], 1: merged_constants([3]) + sc[1:]}, first)[0]
        gd[0], gd[1] = arrive(0, "acn0", "apart"), arrive(1, "acn1", "apart")
        other_codes = (T.cwx[:, 0:512], T.cwx[:, 512:1024], [("lcx", 16)])
        count = 1 + sum(max(1, n - 1) for n, _ in SEGS[2])
        c2 = codes(2, first, count, own_codes if r == 2 else other_codes, False)
        first += 32 * count
        at, late = string(second, at, last_two, T.w[:] if r == 2 else T.w1[:], {0: lm[1:2], 1: lm[2:3]}, first)
        play(late)
        column("tt")

        def second_done():
            tally(0)
            tally(2)
            spread(2)
        D2, D3 = digits([2]), digits([3])
        if r == 2:
            hooks = {0: c2[:1], 1: [c2[1], lambda: send([K["en", 2]], [1], T.e2[:], T.e2[:], "arc2")], 2: lm[3:], 3: [c2[2], second_done]}
        else:
            hooks = {1: c2[:1], 2: lm[3:], OPT["p3"]: c2[1:2]}
        at = string(third, at, gives, T.cpx[:] if r == 2 else T.cpm[:], hooks)[0]
        c3 = codes(3, first, (free["tt"] - first) // 32 - 1, other_codes if r == 2 else own_codes, False)
        if r == 3 and OPT["p3"] > 4:
            play(c3[:1])
            tally(1)
            c3[1](at)
            play(c2[1:2] + c3[2:])
            tally(3)
            spread(3)
            play([c2[2], second_done] + D3[:2] + D2[:2])
            hot(2)
            hot(3)
            D3[2]()
            add(3)
            D3 = D2
        else:
            play(c3[:1] + (D2[:2] if r == 2 else [c2[2], second_done]))
            tally(1)
            c3[1](at)
            play((D2[2:] if r == 2 else D2[:2]) + c3[2:])
            tally(3)
            spread(3)
            hot(2)
            if r == 2:
                add(2)
                hot(1)
                add(1, False, [arrive(1, "aep1")])
            play(D3[:2])
            if r == 3:
                D2[2]()
                add(2)
            hot(3)
        D3[2]()
        add(2 if r == 3 and OPT["p3"] > 4 else 3, True)
    if r == 3:
        nd = ts([K["at", "Z"]], T.neg[:], T.pl[0:8, 3:35], places["Z"], -1.0, OP.is_ge, OP.mult)
        yd = tten([ydep[0], nd], T.ysb[:], T.py[0:8, 0:32], T.neg[:], OP.add)
    else:
        yd = do("v", [ydep[0]], lambda: vec.tensor_copy(T.ysb[:], T.py[0:8, 0:32]))
    dma("y", [yd], "st", T.y[:], T.ysb[:])
    for sn in list(cnt):
        if sn != "st":
            waits("p", [(sn, cnt[sn])])
    waits("p", [("st", 16)])
